import numpy as np, ml_dtypes
CORES = [3,11,19,27,35,43,51,59]
N = 8
import mx_ref
BF = ml_dtypes.bfloat16
def entries(a):
    return np.ascontiguousarray(a.T).reshape(-1)
def table(e):
    return np.ascontiguousarray(np.reshape(e, (-1, 16)).T).astype(np.int32)
def pick(q, e):
    c = np.concatenate([q[0].reshape(128, -1, 4), np.zeros((128, 1, 4), np.uint8)], axis=1); s = np.concatenate([q[1], np.ones((16, 1), np.uint8)], axis=1)
    return (np.ascontiguousarray(c[:, e].reshape(128, -1)), np.ascontiguousarray(s[:, e]))
def join(*qs):
    return (np.concatenate([q[0] for q in qs], axis=1), np.concatenate([q[1] for q in qs], axis=1))
def put(q, e, v):
    c, s = q[0].reshape(128, -1, 4).copy(), q[1].copy(); c[:, e] = v[0].reshape(128, -1, 4); s[:, e] = v[1]
    return (c.reshape(128, -1), s)
def pk(c, s):
    return (np.ascontiguousarray(c), mx_ref.live(s))
def emit(q):
    return q[0], q[1]
def decode(q):
    o = []
    for b in range(4):
        e = np.zeros((128, 128, 4), np.float32); e[np.arange(128), np.arange(128), b] = 1
        o.append(mx_ref.matmul(mx_ref.quantize(e.reshape(128, 512).astype(BF)), q))
    return np.stack(o, axis=2).reshape(128, -1)
def cut(t, i, w=512):
    return t[:, w * i:w * i + w]
def f(rng, *shape):
    return mx_ref.flush((rng.standard_normal(shape, dtype=np.float32) * np.exp2(rng.integers(-2, 3, shape[:-1] + (1,)))).astype(BF))
def wide(rng, *shape, cols=0):
    v = rng.standard_normal(shape, dtype=np.float32) * np.exp2(rng.integers(-12, 13, shape)).astype(np.float32)
    if cols: v *= np.repeat(np.exp2(rng.integers(-cols, cols + 1, shape[:-2] + (1, shape[-1] // 4))) * (rng.random(shape[:-2] + (1, shape[-1] // 4)) > 0.0625), 4, axis=-1).astype(np.float32)
    return mx_ref.flush(v.astype(BF))
P, M, A, CAPP, R = 512, 128, 32, 16, 3
def big(v):
    v = v.astype(np.float32)
    v[np.abs(v) < np.float32(2.0 ** -16)] = 0
    return v.astype(BF)
def listed(e):
    return np.stack([table(v) for v in e])
def setup_inputs(rng):
    return {"ky": big(f(rng, N, 128, 4 * P)), "nx": listed(rng.integers(0, N * M, (N, P))), "x": big(f(rng, N, 128, 4 * A)), "st": listed(rng.integers(0, N * M, (N, A))), "w": f(rng, N, 128, 512)}
def setup_inputs_spread(rng):
    d = setup_inputs(rng)
    d["ky"] = big(wide(rng, N, 128, 4 * P, cols=6))
    d["x"] = big(wide(rng, N, 128, 4 * A, cols=4))
    return d
def setup_inputs_ties(rng):
    d = setup_inputs(rng)
    o = np.argsort(rng.random((N, M, 4)), axis=2) % 2
    v = d["ky"].reshape(N, 128, M, 4, 4)
    v = np.ascontiguousarray(np.stack([np.take_along_axis(v[r], np.broadcast_to(o[r][None, :, :, None], (128, M, 4, 4)), axis=2) for r in range(N)]))
    for r in range(N): v[r][:, rng.permutation(M)[:M // 8]] = 0
    d["ky"] = v.reshape(N, 128, 4 * P)
    to = np.argsort(rng.random((N, M, N)), axis=2)[:, :, :4]
    d["nx"] = listed((to * M + rng.integers(0, M, (N, M, 4))).reshape(N, P))
    return d
def setup_inputs_crowd(rng):
    d = setup_inputs(rng)
    o, st = rng.permutation(N), np.zeros((N, A), int)
    for i in range(N):
        s, to = o[i], o[(i + 1) % N]
        here = rng.permutation(A) < (CAPP if i % 2 == 0 else A - CAPP // 4)
        near = to * M + (rng.integers(0, M, A) if i % 2 == 0 else np.full(A, int(rng.integers(0, M))))
        far = (to + rng.integers(1, N, A)) % N * M + rng.integers(0, M, A)
        st[s] = np.where(here, near, far)
    d["st"] = listed(st)
    return d
def kept(rng, *shape):
    return 4 * rng.integers(0, M // 4, shape) + rng.integers(0, 3, shape)
def setup_inputs_stay(rng):
    d = setup_inputs(rng)
    o = rng.permutation(N)
    z, z2 = int(o[0]), int(o[1])
    v = np.arange(M)[None, :, None]
    to = np.arange(N)[:, None, None] * M + np.where(v % 2 == 0, v, kept(rng, N, M, 4))
    to[z, 3::4] = o[rng.integers(2, N, (M // 4, 4))] * M + rng.integers(0, M, (M // 4, 4))
    to[z2] = z * M + kept(rng, M, 4)
    d["nx"] = listed(to.reshape(N, P))
    leave = np.zeros((N, A), bool)
    leave[:, :CAPP] = np.argsort(rng.random((N, CAPP)), axis=1) < CAPP // 4
    st = z * M + np.where(leave, 4 * rng.integers(0, M // 4, (N, A)) + 3, kept(rng, N, A))
    n = CAPP + CAPP // 2
    st[:, n:] = z2 * M + rng.integers(0, M, (N, A - n))
    low = rng.permutation(N) < N // 2
    st[low] = np.roll(st[low], A - n, axis=1)
    d["st"] = listed(st)
    return d
def setup_inputs_turn(rng):
    d = setup_inputs(rng)
    sign = rng.choice([-1.0, 1.0], (128, 4))
    top = np.arange(128) < 64
    o = np.argsort(rng.random((N, M, 4)), axis=2).reshape(N, P)
    g = np.where(top[None, :, None], np.exp2(-2.0 * o)[:, None, :], np.exp2(2.0 * o + 2)[:, None, :])
    d["ky"] = big(((1 + rng.random((N, 128, P, 4))) * g[..., None] * sign[None, :, None, :]).reshape(N, 128, 4 * P))
    d["x"] = big(((1 + rng.random((N, 128, A, 4))) * top[None, :, None, None] * sign[None, :, None, :]).reshape(N, 128, 4 * A))
    return d
def check_inputs(d):
    b = []
    for k, lo, hi in (("ky", -16, 24), ("x", -16, 24), ("w", -30, 30)):
        v = np.abs(d[k].astype(np.float32))
        if not (np.isfinite(v).all() and ((v == 0) | (v >= 2.0 ** lo) & (v <= 2.0 ** hi)).all()): b.append("a value of " + k)
    for k in ("nx", "st"):
        if d[k].min() < 0 or d[k].max() >= N * M: b.append("an entry of " + k)
    return b
def served(node):
    ok = np.zeros(N * A, bool)
    for s in range(N):
        at = node[A * s:A * s + A] // M
        for d in range(N): ok[A * s + np.flatnonzero(at == d)[:CAPP]] = True
    return np.flatnonzero(ok)
def reference(ky, nx, x, st, w):
    pieces = [mx_ref.quantize(np.ascontiguousarray(cut(ky[d], i))) for d in range(N) for i in range(P // 128)]
    dk = decode(join(*pieces)).reshape(128, N * P, 4)
    leads = np.concatenate([entries(nx[d]) for d in range(N)])
    q = join(*[mx_ref.quantize(np.ascontiguousarray(x[s])) for s in range(N)])
    node = np.concatenate([entries(st[s]) for s in range(N)])
    e = np.arange(N * A)
    way = [node]
    for t in range(R):
        go = served(node)
        z = np.concatenate([mx_ref.matmul(p, q) for p in pieces])
        four = 4 * node[:, None] + np.arange(4)
        k = 4 * node + np.argmax(z[four, e[:, None]] + np.float32(0), axis=1)
        v = decode(q).reshape(128, N * A, 4) * np.float32(0.5) + dk[:, k] * np.float32(0.5)
        new = mx_ref.quantize(np.ascontiguousarray(v.reshape(128, -1).astype(BF)))
        q = put(q, go, pick(new, go))
        node = node.copy()
        node[go] = leads[k[go]]
        way.append(node)
    oc, osc = np.zeros((N, 128, 4 * A), np.uint8), np.zeros((N, 16, A), np.uint8)
    nd, y = np.zeros((N, R + 1, A), np.float32), np.zeros((N, 128, A), np.float32)
    for s in range(N):
        own = pick(q, np.arange(A * s, A * s + A))
        oc[s], osc[s] = emit(own)
        nd[s] = np.stack(way)[:, A * s:A * s + A]
        y[s] = mx_ref.matmul(mx_ref.quantize(np.ascontiguousarray(w[s])), own)
    return {"oc": oc, "osc": osc, "nd": nd, "y": y}

@@ -1,0 +1,463 @@
+from concourse.bass import DstId, RemoteDMATransfer
+from concourse.mybir import dt, AluOpType, AxisListType, ActivationFunctionType
+
+R, A, P, CAP, N = 3, 32, 512, 16, 8
+HOME = A + N * CAP
+
+SCRATCH = {}
+
+
+def _sb(name, cols, ty):
+    SCRATCH[name] = ("sbuf", [128, cols], ty)
+
+
+_F, _I, _U, _B, _Q, _S = "float32", "int32", "uint16", "bfloat16", "float8_e4m3fn_x4", "uint8"
+for _n, _c, _t in [
+    ("iF", 516, _F), ("eF", 516, _B), ("iw", 128, _B), ("ia", 64, _I), ("ia2", 64, _I), ("ib", 64, _I), ("ib2", 64, _I), ("iab", 64, _I),
+    ("mask64", 64, _F), ("mask32", 32, _F), ("ip", 1, _I), ("ip15", 1, _I), ("ip5", 1, _I), ("ip31", 1, _I), ("r1", 1, _F),
+    ("tb", 1, _F), ("a128", 1, _F), ("il", 1, _I), ("il2", 1, _I), ("cl1", 1, _F), ("cl2", 1, _F), ("cloc", 1, _F), ("i8", 8, _I),
+    ("i82", 8, _I), ("mask8", 8, _F), ("ja", 64, _F), ("rowb", 64, _F), ("ct", 64, _F), ("rst32", 64, _F), ("rst16", 64, _F),
+    ("c128", 4, _F), ("ik", 32, _I), ("ik2", 32, _I), ("ikb", 32, _I), ("ik3", 32, _I), ("ku", 32, _U), ("i2", 2, _I), ("i22", 2, _I),
+    ("mask2", 2, _F), ("stt", 2, _I), ("stm", 2, _F), ("nxa", 32, _I), ("nxf", 32, _F), ("nrow", 512, _F), ("tab", 512, _F),
+    ("xb", 512, _B), ("kb", 2048, _B), ("wb", 512, _B), ("yb", 32, _F),
+]:
+    _sb(_n, _c, _t)
+for _n, _c in [("kn", 512), ("kj", 512), ("wq", 128), ("e0", 128), ("e1", 128), ("e2", 128), ("e3", 128), ("hq0", 128), ("fin", 128)]:
+    _sb(_n + "c", _c, _Q)
+    _sb(_n + "s", _c, _S)
+for _t in range(R):
+    for _n, _c in [("sd", 128), ("ld", 128), ("kp", 128), ("qn", 128)]:
+        _sb("%s%dc" % (_n, _t), _c, _Q)
+        _sb("%s%ds" % (_n, _t), _c, _S)
+    _sb("hq%dc" % (_t + 1), HOME, _Q)
+    _sb("hq%ds" % (_t + 1), HOME, _S)
+    _sb("pk%d" % _t, 8, _I)
+    _sb("vl%d" % _t, 12, _I)
+    _sb("sn%d" % _t, 32, _F)
+    _sb("nl%d" % (_t + 1), 12, _F)
+SMALL, WF, WI, WU = {}, [0], [0], [0]
+
+
+def _small(ty, name, cols):
+    c = {"f": WF, "i": WI, "u": WU}[ty]
+    SMALL[name] = ({"f": "smf", "i": "smi", "u": "smu"}[ty], c[0], c[0] + cols)
+    c[0] += cols + cols % 2
+
+
+for _t in range(R + 1):
+    for _n, _c in [("u", 1), ("bc", 64), ("bt", 64), ("ind", 64), ("cum", 64), ("hit", 64), ("pkr", 64), ("ipk", 64), ("hpk", 64), ("sp", 64),
+                   ("q0", 8), ("n", 1), ("f1", 1), ("f2", 1), ("f3", 1), ("lm", 32), ("lsc", 32), ("vp", 8), ("pkf", 1), ("wf", 1), ("a1", 1),
+                   ("c1", 1), ("i0", 64), ("oh", 64), ("oht", 64), ("q1", 1), ("dp", 1), ("p0", 128), ("p1", 128), ("p2", 128), ("p3", 128),
+                   ("s4", 4), ("mx", 1), ("ne", 4), ("js", 4), ("d0", 64), ("dt", 64), ("ds", 64), ("lf", 8), ("l2", 2), ("gt", 32),
+                   ("n1", 32), ("n2", 32), ("j0", 128), ("j1", 128), ("j2", 128), ("j3", 128)]:
+        _small("f", "%s_%d" % (_n, _t), _c)
+    for _n, _c in [("ri", 64), ("be", 64), ("lo", 64), ("sr", 8), ("ui", 1), ("e1", 1), ("e2", 1), ("e3", 1), ("e4", 1), ("lr", 32),
+                   ("pki", 1), ("wi", 1), ("ai", 1)]:
+        _small("i", "%s_%d" % (_n, _t), _c)
+    for _n, _c in [("su", 8), ("lu", 2), ("ko", 8), ("l2u", 2)]:
+        _small("u", "%s_%d" % (_n, _t), _c)
+for _n, _c in [("x1", 32), ("x2", 32), ("x3", 32)]:
+    _small("i", _n, _c)
+for _n, _c in [("y1", 32), ("y2", 32), ("y3", 32)]:
+    _small("f", _n, _c)
+_sb("smf", WF[0], _F)
+_sb("smi", WI[0], _I)
+_sb("smu", WU[0], _U)
+for _t in range(R):
+    _sb("hb%d" % _t, 512, _B)
+for _b in range(4):
+    SCRATCH["z%d" % _b] = ("psum", [128, 512], "float32")
+    SCRATCH["d%d" % _b] = ("psum", [128, 512], "float32")
+
+SEMAPHORES = ["qv", "qs", "qt", "qg", "ls"] + ["m%d" % _k for _k in range(40)]
+for _t in range(R):
+    SEMAPHORES += ["apk%d" % _t, "aco%d" % _t, "adl%d" % _t, "are%d" % _t]
+
+
+def rank_program(g, core, T, topo):
+    me = T.rank_of(core)
+    if me is None:
+        return
+    OP, X, CP = AluOpType, AxisListType.X, ActivationFunctionType.Copy
+    V, S, TE, Y = g.vector, g.scalar, g.tensor, g.sync
+    eng = {"v": V, "s": S, "t": TE, "g": g, "y": Y}
+    known = {q: {} for q in eng}
+    total, waited = {}, {}
+    wr, rd = {}, {}
+    nm = [0]
+
+    def need(q, evs):
+        for sem, n, clk in sorted(evs, key=lambda e: -sum(e[2].values())):
+            k = known[q]
+            if k.get(sem, 0) < n:
+                eng[q].wait_ge(T.sem[sem], n)
+                k[sem] = n
+                waited[sem] = max(waited.get(sem, 0), n)
+                for x in clk:
+                    k[x] = max(k.get(x, 0), clk[x])
+
+    def before(q, r, w):
+        evs = []
+        for k in r:
+            evs += wr.get(k, [])
+        for k in w:
+            evs += wr.get(k, []) + rd.get(k, [])
+        need(q, evs)
+
+    def done(q, sem, n, r, w, a=()):
+        ev = (sem, n, dict(known[q]))
+        for k in r:
+            rd.setdefault(k, []).append(ev)
+        for k in w:
+            wr[k] = [ev]
+            rd[k] = []
+        for k in a:
+            wr.setdefault(k, []).append(ev)
+
+    def run(q, fn, r=(), w=(), a=()):
+        before(q, r, w)
+        sem = "q" + q
+        fn().then_inc(T.sem[sem], 1)
+        total[sem] = total.get(sem, 0) + 1
+        done(q, sem, total[sem], r, w, a)
+
+    def dma(q, pairs, r=(), w=(), a=()):
+        before(q, r, w)
+        sem = "m%d" % nm[0]
+        nm[0] += 1
+        for o, i in pairs:
+            eng[q].dma_start(o, i).then_inc(T.sem[sem], 16)
+        total[sem] = 16 * len(pairs)
+        done(q, sem, total[sem], r, w, a)
+
+    others = [(me + i) % N for i in range(1, N)]
+
+    def send(sem, part, r, rot):
+        before("g", r, ())
+        tr = []
+        for i, d in enumerate(others):
+            dst = T.cores[d]
+            rid, pid, _ = topo.addr(dst)
+            es = topo.engines(core, dst)
+            o, s = part(d)
+            tr.append(RemoteDMATransfer(dst_ids=[DstId(rid=rid, pnc=pid)], dma_engine_mask=1 << es[(i + rot) % len(es)], remote_sem=T.sem[sem], src=s, dst=o))
+        g.remote_dma_fused(tr, local_sem=T.sem["ls"])
+        total["ls"] = total.get("ls", 0) + len(tr)
+
+    def arrive(sem, n, keys):
+        total[sem] = n
+        for k in keys:
+            wr.setdefault(k, []).append((sem, n, {}))
+
+    def ap(name, p=None, c=None):
+        if name in SMALL:
+            buf, lo, hi = SMALL[name]
+            c0, c1, st = (0, hi - lo, 1) if c is None else (c if len(c) == 3 else c + (1,))
+            cols = slice(lo + c0, lo + c1, st)
+        else:
+            buf = name
+            cols = slice(None) if c is None else (slice(*c))
+        rows = slice(None) if p is None else slice(*p)
+        return T[buf][rows, cols]
+
+    def codes(name, lo, hi):
+        return T[name + "c"][:, lo:hi].bitcast(dt.uint8)
+
+    def words(name, lo, hi):
+        return T[name + "c"][:, lo:hi].bitcast(dt.uint32)
+
+    def plane(name, lo, hi):
+        return T[name + "s"][:, lo:hi]
+
+    def ts(o, i, s1, op0, s2=None, op1=None, r=(), w=(), po=None, pi=None, co=None, ci=None, a=()):
+        def fn():
+            out, in0 = ap(o, po, co), ap(i, pi if pi else po, ci)
+            if op1 is None:
+                return V.tensor_scalar(out, in0, s1, None, op0)
+            return V.tensor_scalar(out, in0, s1, s2, op0, op1)
+        run("v", fn, r=tuple(r) + (i,), w=w if (w or a) else (o,), a=a)
+
+    def tt(o, x, y, op, po=None, co=None, cx=None, cy=None, w=(), a=()):
+        run("v", lambda: V.tensor_tensor(ap(o, po, co), ap(x, po, cx), ap(y, po, cy), op), r=(x, y), w=w if (w or a) else (o,), a=a)
+
+    def cp(o, i, po=None, pi=None, co=None, ci=None, w=(), a=(), q="v"):
+        def fn():
+            if q == "v":
+                return V.tensor_copy(ap(o, po, co), ap(i, pi if pi else po, ci))
+            return S.activation(ap(o, po, co), ap(i, pi if pi else po, ci), CP)
+        run(q, fn, r=(i,), w=w if (w or a) else (o,), a=a)
+
+    def scan(o, d0, d1, c0=None, po=None):
+        run("v", lambda: V.tensor_tensor_scan(ap(o, po), ap(d0, po, c0), ap(d1, po), 0.0, OP.mult, OP.add), r=(d0, d1), w=(o,))
+
+    def total_of(o, i, po=None, ci=None):
+        run("v", lambda: V.tensor_reduce(ap(o, po), ap(i, po, ci), X, OP.add), r=(i,), w=(o,))
+
+    def trans(o, i, po=None):
+        run("v", lambda: V.transpose(ap(o, po), ap(i, po)), r=(i,), w=(o,))
+
+    def pick(o, olo, ohi, i, ilo, ihi, lst, r, wkeys, c=None):
+        buf, lo, hi = SMALL.get(lst, (lst, 0, SCRATCH[lst][1][1] if lst not in SMALL else 0))
+        off = T[buf][:, lo:hi]
+        run("v", lambda: V.tensor_copy(words(o, olo, ohi), words(i, ilo, ihi).indirect(off)), r=tuple(k + "c" for k in r) + (lst,), a=tuple(k + "c" for k in wkeys))
+        run("s", lambda: S.activation(plane(o, olo, ohi), plane(i, ilo, ihi).indirect(off), CP), r=tuple(k + "s" for k in r) + (lst,), a=tuple(k + "s" for k in wkeys))
+
+    def quant(o, lo, hi, src, slo, shi, r, w):
+        run("v", lambda: V.quantize_mx(T[o + "c"][:, lo:hi], T[o + "s"][:, lo:hi], T[src][:, slo:shi]), r=r, a=(w + "c", w + "s"))
+
+    def iota(name, pattern, base, cm):
+        if SCRATCH[name][2] == "int32":
+            run("g", lambda: g.iota(T[name][:], pattern, base, cm), w=(name,))
+        else:
+            run("g", lambda: g.iota(T[name][:], pattern, base, cm, allow_small_or_imprecise_dtypes=True), w=(name,))
+
+    quad = [(32 * b, 32 * b + 32) for b in range(4)]
+    mine = quad[me // 2]
+    half = me % 2
+
+    dma("y", [(T.stt[0:16, 0:2], T.st[:, :]), (T.stt[16:32, 0:2], T.st[:, :])], w=("stt",))
+    dma("s", [(T.xb[:, 0:4 * A], T.x[:, :])], a=("xb",))
+    dma("y", [(T.nxa[0:16, :], T.nx[:, :])], w=("nxa",))
+    dma("s", [(T.kb[:], T.ky[:, :])], w=("kb",))
+    dma("y", [(T.wb[:], T.w[:, :])], w=("wb",))
+
+    run("v", lambda: V.memset(T.xb[:, 4 * A:512], 0.0), a=("xb",))
+    iota("ip", [[1, 1]], 0, 1)
+    iota("i2", [[16, 2]], 0, 1)
+    iota("ja", [[0, 2], [1, A]], 1, 0)
+    iota("ia", [[0, 2], [1, 32]], 256, -1)
+    iota("ib", [[32, 2], [0, 32]], 0, 1)
+    iota("i8", [[-16, 8]], 256 - 16 * me, 1)
+    iota("il", [[1, 1]], 16 * (me + 7) + 15, -1)
+    iota("ik", [[1, 4], [4, 4], [0, 2]], 0, 16)
+    iota("ikb", [[0, 16], [256, 2]], 0, 0)
+    iota("iw", [[1, 128]], 0, 0)
+    iota("iF", [[1, 516]], -3, -4)
+    run("v", lambda: V.memset(ap("ct", None, (0, 32)), float((15 - me) * 65536)), a=("ct",))
+    run("v", lambda: V.memset(ap("ct", None, (32, 64)), float((14 - me) * 65536)), a=("ct",))
+    run("v", lambda: V.memset(T.rst32[:], 1.0), w=("rst32",))
+    run("v", lambda: V.memset(T.rst32[:, 0:64:32], 0.0), w=("rst32",))
+    run("v", lambda: V.memset(T.rst16[:], 1.0), w=("rst16",))
+    run("v", lambda: V.memset(T.rst16[:, 0:64:16], 0.0), w=("rst16",))
+    run("v", lambda: V.memset(T.c128[:], 128.0), w=("c128",))
+    ts("ip15", "ip", 15, OP.bitwise_and)
+    ts("r1", "ip15", 1.0, OP.add)
+    ts("ip5", "ip", 5, OP.logical_shift_right)
+    ts("tb", "ip5", 2.0, OP.mult)
+    ts("ip31", "ip", 31, OP.bitwise_and)
+    ts("a128", "ip31", 128.0, OP.mult)
+    ts("i22", "i2", 16, OP.bitwise_and)
+    ts("mask2", "i22", 0.0, OP.is_equal)
+    ts("rowb", "ja", 65536.0, OP.mult)
+
+    def constants():
+        ts("ia2", "ia", 15, OP.bitwise_and)
+        ts("mask32", "ia2", 0.0, OP.is_equal, ci=(0, 32))
+        ts("ib2", "ib", 32, OP.bitwise_and)
+        tt("iab", "ia2", "ib2", OP.add)
+        ts("mask64", "iab", 0.0, OP.is_equal)
+        ts("i82", "i8", 112, OP.bitwise_and)
+        ts("mask8", "i82", 0.0, OP.is_equal)
+        ts("il2", "il", 112, OP.bitwise_and)
+        ts("cl1", "il2", 128.0, OP.mult, float(128 * 32 - 65536 * me), OP.add)
+        ts("cl2", "r1", 128.0, OP.mult)
+        tt("cloc", "cl1", "cl2", OP.add)
+        q = (0, 16)
+        ts("x1", "nxa", 3, OP.bitwise_and, po=q)
+        ts("x2", "nxa", 127, OP.bitwise_and, 2, OP.logical_shift_right, po=q)
+        ts("x3", "nxa", 7, OP.logical_shift_right, po=q)
+        ts("y1", "x1", 32.0, OP.mult, po=q)
+        tt("y2", "y1", "x2", OP.add, po=q)
+        ts("y3", "x3", 65536.0, OP.mult, po=q)
+        tt("nxf", "y2", "y3", OP.add, po=q)
+        dma("y", [(T.nrow[0:1, 128 * j:128 * j + 128], T.nxf[j:16:4, :]) for j in range(4)], r=("nxf",), w=("nrow",))
+        run("g", lambda: g.partition_broadcast(T.tab[:], T.nrow[0:1, :], 128), r=("nrow",), w=("tab",))
+        ts("eF", "iF", 0.0, OP.is_equal, 0.5, OP.mult)
+        for b in range(4):
+            quant("e%d" % b, 0, 128, "eF", 3 - b, 3 - b + 512, ("eF",), "e%d" % b)
+        ts("ik2", "ik", 255, OP.bitwise_and)
+        tt("ik3", "ik2", "ikb", OP.add)
+        cp("ku", "ik3")
+        quant("kn", 0, 512, "kb", 0, 2048, ("kb",), "kn")
+        pick("kj", 0, 512, "kn", 0, 512, "ku", ("kn",), ("kj",))
+        quant("wq", 0, 128, "wb", 0, 512, ("wb",), "wq")
+        dma("y", [(codes("fin", A, 128), codes("hq0", A, 128)), (plane("fin", A, 128), plane("hq0", A, 128))], r=("hq0c", "hq0s"), a=("finc", "fins"))
+        dma("y", [(codes("hq1", 0, A), codes("hq0", 0, A)), (plane("hq1", 0, A), plane("hq0", 0, A))], r=("hq0c", "hq0s"), a=("hq1c", "hq1s"))
+
+    def rows(t, q):
+        n = "_%d" % t
+        ts("bc" + n, "ct", ap("u" + n, q), OP.add, r=("u" + n,), po=q)
+        trans("bt" + n, "bc" + n, q)
+        for b in quad:
+            cp("ri" + n, "bt" + n, po=b, pi=q, a=("ri" + n,))
+
+    def route(t, q):
+        n = "_%d" % t
+        rows(t, q)
+        ts("be" + n, "ri" + n, 16, OP.logical_shift_right, 7, OP.bitwise_and)
+        ts("ind" + n, "be" + n, T.tb[:, 0:1], OP.is_equal, r=("tb",))
+        scan("cum" + n, "rst32", "ind" + n)
+        ts("lo" + n, "ri" + n, 65535, OP.bitwise_and)
+        tt("pkr" + n, "lo" + n, "rowb", OP.add)
+        tt("ipk" + n, "ind" + n, "pkr" + n, OP.mult)
+        ts("hit" + n, "cum" + n, T.r1[:, 0:1], OP.is_equal, r=("r1",))
+        tt("hpk" + n, "hit" + n, "ipk" + n, OP.mult)
+        scan("sp" + n, "rst32", "hpk" + n)
+        for b in range(4):
+            cp("q0" + n, "sp" + n, po=(0, 32), pi=quad[b], co=(2 * b, 2 * b + 2), ci=(31, 64, 32), a=("q0" + n,), q="v" if b < 2 else "s")
+        for b in quad:
+            cp("pk%d" % t, "q0" + n, po=b, pi=(0, 32), a=("pk%d" % t,))
+        send("apk%d" % t, lambda d: (T["vl%d" % t][:, 3 + (me - d) % N:4 + (me - d) % N], T["pk%d" % t][:, (d - me - 1) % N:(d - me - 1) % N + 1]), ("pk%d" % t,), 2)
+        ts("sr" + n, "pk%d" % t, 7, OP.logical_shift_right, 511, OP.bitwise_and)
+        cp("su" + n, "sr" + n)
+
+    def depart(t):
+        hi = 128 if t == 0 else HOME
+        pick("sd%d" % t, 0, 128, "hq%d" % t, 0, hi, "su_%d" % t, ("hq%d" % t,), ("sd%d" % t,))
+        at = lambda d: CAP * ((d - me - 1) % N)
+        send("aco%d" % t, lambda d: (codes("ld%d" % t, CAP * me, CAP * me + CAP), codes("sd%d" % t, at(d), at(d) + CAP)), ("sd%dc" % t,), 0)
+        send("aco%d" % t, lambda d: (plane("ld%d" % t, CAP * me, CAP * me + CAP), plane("sd%d" % t, at(d), at(d) + CAP)), ("sd%ds" % t,), 1)
+        dma("y", [(codes("ld%d" % t, CAP * me, CAP * me + CAP), codes("sd%d" % t, 112, 128)), (plane("ld%d" % t, CAP * me, CAP * me + CAP), plane("sd%d" % t, 112, 128))],
+            r=("sd%dc" % t, "sd%ds" % t), a=("ld%dc" % t, "ld%ds" % t))
+        cp("vl%d" % t, "pk%d" % t, co=(3, 4), ci=(7, 8), a=("vl%d" % t,))
+        arrive("apk%d" % t, 7, ("vl%d" % t,))
+        arrive("aco%d" % t, 14, ("ld%dc" % t, "ld%ds" % t))
+
+    def stand(t):
+        n, q = "_%d" % t, mine
+        cp("ui" + n, "u" + n, po=q)
+        ts("e1" + n, "ui" + n, 31, OP.bitwise_and, po=q)
+        ts("e2" + n, "ui" + n, 127, OP.bitwise_and, 5, OP.logical_shift_right, po=q)
+        ts("e3" + n, "ui" + n, 16, OP.logical_shift_right, po=q)
+        ts("f1" + n, "e1" + n, 4.0, OP.mult, po=q)
+        tt("f2" + n, "f1" + n, "e2" + n, OP.add, po=q)
+        ts("f3" + n, "e3" + n, 128.0, OP.mult, po=q)
+        tt("n" + n, "f2" + n, "f3" + n, OP.add, po=q)
+        dma("y", [(T.nd[t:t + 1, 0:A], ap("n" + n, q))], r=("n" + n,))
+        if t < R:
+            ts("e4" + n, "ui" + n, 127, OP.bitwise_and, po=q)
+            ts("f3" + n, "e3" + n, 65536.0, OP.mult, T.a128[q[0]:q[1], 0:1], OP.add, r=("a128",), po=q)
+            run("v", lambda: V.tensor_tensor(ap("nl%d" % (t + 1), q, (2, 3)), ap("f3" + n, q), ap("e4" + n, q), OP.add), r=("f3" + n, "e4" + n), a=("nl%d" % (t + 1),))
+
+    def places(t):
+        n = "_%d" % t
+        ts("lr" + n, "ri" + n, 7, OP.logical_shift_right, 511, OP.bitwise_and, ci=(0, 32))
+        tt("lm" + n, "lr" + n, "mask32", OP.mult)
+        scan("lsc" + n, "rst16", "lm" + n, c0=(0, 32))
+        cp("lu" + n, "lsc" + n, ci=(15, 32, 16))
+
+    def slots(t):
+        n = "_%d" % t
+        run("v", lambda: V.tensor_tensor(ap("vp" + n), ap("vl%d" % t, None, (3, 11)), T.mask8[:], OP.mult), r=("vl%d" % t, "mask8"), w=("vp" + n,))
+        total_of("pkf" + n, "vp" + n)
+        cp("pki" + n, "pkf" + n)
+        ts("wi" + n, "pki" + n, 127, OP.bitwise_and)
+        ts("ai" + n, "pki" + n, 16, OP.logical_shift_right)
+        cp("wf" + n, "wi" + n)
+        run("v", lambda: V.tensor_scalar(T.mm[:] if t % 2 == 0 else T.mn[:], T.iw[:], ap("wf" + n), None, OP.is_equal), r=("iw", "wf" + n), w=("mm%d" % (t % 2),))
+        cp("a1" + n, "ai" + n)
+        ts("c1" + n, "wf" + n, 1024.0, OP.add)
+        ts("i0" + n, "mask64", ap("c1" + n), OP.mult, -1024.0, OP.add, r=("c1" + n,))
+        ts("oh" + n, "ja", ap("a1" + n), OP.is_equal, r=("a1" + n,), co=(0, 32), ci=(0, 32), a=("oh" + n,))
+        ts("q1" + n, "a1" + n, -128.0, OP.mult, T.cloc[:, 0:1], OP.add, r=("cloc",))
+        tt("dp" + n, "q1" + n, "wf" + n, OP.subtract)
+        run("v", lambda: V.tensor_scalar(ap("oh" + n, None, (32, 64)), ap("oh" + n, None, (0, 32)), ap("dp" + n), None, OP.mult), r=("oh" + n, "dp" + n), a=("oh" + n,))
+        trans("oht" + n, "oh" + n)
+
+    def hop(t):
+        n, ld, kp, qn = "_%d" % t, "ld%d" % t, "kp%d" % t, "qn%d" % t
+        for j in range(4):
+            run("t", lambda: TE.matmul_mx(T["z%d" % j][:, 0:128], T[ld + "c"][:, 0:128], T[ld + "s"][:, 0:128], T.kjc[:, 128 * j:128 * j + 128], T.kjs[:, 128 * j:128 * j + 128], True, True),
+                r=(ld + "c", ld + "s", "kjc", "kjs"), w=("z%d" % j,))
+        for b in range(4):
+            run("t", lambda: TE.matmul_mx(T["d%d" % b][:, 0:128], T["e%dc" % b][:], T["e%ds" % b][:], T[ld + "c"][:, 0:128], T[ld + "s"][:, 0:128], True, False),
+                r=(ld + "c", ld + "s", "e%dc" % b, "e%ds" % b), w=("d%d" % b,))
+        m = T.mm if t % 2 == 0 else T.mn
+        for j in range(4):
+            run("v", lambda: V.tensor_tensor(ap("p%d" % j + n), T["z%d" % j][:, 0:128], m[:], OP.mult), r=("z%d" % j, "mm%d" % (t % 2)), w=("p%d" % j + n,))
+            run("s", lambda: S.activation(ap("j%d" % j + n), ap("p%d" % j + n), CP, accum_out=ap("s4" + n, None, (3 - j, 4 - j))), r=("p%d" % j + n,), w=("j%d" % j + n,), a=("s4" + n,))
+        run("v", lambda: V.tensor_reduce(ap("mx" + n), ap("s4" + n), X, OP.max), r=("s4" + n,), w=("mx" + n,))
+        ts("ne" + n, "s4" + n, ap("mx" + n), OP.not_equal, 1000000.0, OP.mult, r=("mx" + n,))
+        run("v", lambda: V.tensor_tensor_scan(ap("js" + n), T.c128[:], ap("ne" + n), 0.0, OP.add, OP.min), r=("c128", "ne" + n), w=("js" + n,))
+        ts("d0" + n, "i0" + n, ap("js" + n, None, (3, 4)), OP.add, 0.0, OP.max, r=("js" + n,))
+        trans("dt" + n, "d0" + n)
+        scan("ds" + n, "rst16", "dt" + n)
+        for k in range(2):
+            run("v", lambda: V.tensor_tensor(ap("lf" + n, (0, 32), (4 * k, 4 * k + 4)), ap("ds" + n, quad[2 * k], (15, 64, 16)), ap("ds" + n, quad[2 * k + 1], (15, 64, 16)), OP.add),
+                r=("ds" + n,), a=("lf" + n,))
+        for b in quad:
+            cp("ko" + n, "lf" + n, po=b, pi=(0, 32), a=("ko" + n,))
+        pick(kp, 0, 128, "kj", 0, 512, "ko" + n, ("kj",), (kp,))
+        for b in range(4):
+            run("t", lambda: TE.matmul_mx(T["d%d" % b][:, 0:128], T["e%dc" % b][:], T["e%ds" % b][:], T[kp + "c"][:], T[kp + "s"][:], False, True),
+                r=(kp + "c", kp + "s", "e%dc" % b, "e%ds" % b), a=("d%d" % b,))
+        run("v", lambda: V.tensor_tensor(ap("l2" + n), ap("ds" + n, None, (15, 32, 16)), ap("ds" + n, None, (47, 64, 16)), OP.add), r=("ds" + n,), w=("l2" + n,))
+        cp("l2u" + n, "l2" + n)
+        run("v", lambda: V.tensor_copy(ap("gt" + n), T.tab[:, 0:512].indirect(ap("l2u" + n))), r=("tab", "l2u" + n), w=("gt" + n,))
+        tt("n1" + n, "gt" + n, "oht" + n, OP.mult, cy=(0, 32))
+        tt("n2" + n, "n1" + n, "oht" + n, OP.add, cy=(32, 64))
+        run("v", lambda: V.tensor_tensor_scan(T["sn%d" % t][:], T.rst16[:, 0:32], ap("n2" + n), 0.0, OP.mult, OP.add), r=("rst16", "n2" + n), w=("sn%d" % t,))
+        beta = lambda s: (me - s - 1) % N
+        send("adl%d" % t, lambda s: (T["nl%d" % (t + 1)][:, 4 + beta(s):5 + beta(s)], T["sn%d" % t][:, 15 + 16 * (s % 2):16 + 16 * (s % 2)]), ("sn%d" % t,), 2)
+        arrive("adl%d" % t, 7, ("nl%d" % (t + 1),))
+        for b in range(4):
+            o = T["hb%d" % t][:, b:512:4]
+            if b % 2 == 0:
+                run("s", lambda: S.activation(o, T["d%d" % b][:, 0:128], CP), r=("d%d" % b,), a=("hb%d" % t,))
+            else:
+                run("v", lambda: V.tensor_copy(o, T["d%d" % b][:, 0:128]), r=("d%d" % b,), a=("hb%d" % t,))
+        quant(qn, 0, 128, "hb%d" % t, 0, 512, ("hb%d" % t,), qn)
+        h = "hq%d" % (t + 1)
+        send("are%d" % t, lambda s: (codes(h, A + CAP * beta(s), A + CAP * beta(s) + CAP), codes(qn, CAP * s, CAP * s + CAP)), (qn + "c",), 0)
+        send("are%d" % t, lambda s: (plane(h, A + CAP * beta(s), A + CAP * beta(s) + CAP), plane(qn, CAP * s, CAP * s + CAP)), (qn + "s",), 1)
+        dma("y", [(codes(h, A + 112, HOME), codes(qn, CAP * me, CAP * me + CAP)), (plane(h, A + 112, HOME), plane(qn, CAP * me, CAP * me + CAP))], r=(qn + "c", qn + "s"), a=(h + "c", h + "s"))
+        arrive("are%d" % t, 14, (h + "c", h + "s"))
+        cp("nl%d" % (t + 1), "sn%d" % t, po=mine, co=(3, 4), ci=(15 + 16 * half, 16 + 16 * half), a=("nl%d" % (t + 1),))
+
+    q = quad[0]
+    tt("stm", "stt", "mask2", OP.mult, po=q)
+    total_of("n_0", "stm", po=q)
+    cp("ui_0", "n_0", po=q)
+    ts("e1_0", "ui_0", 3, OP.bitwise_and, po=q)
+    ts("e2_0", "ui_0", 127, OP.bitwise_and, 2, OP.logical_shift_right, po=q)
+    ts("e3_0", "ui_0", 7, OP.logical_shift_right, po=q)
+    ts("f1_0", "e1_0", 32.0, OP.mult, po=q)
+    tt("f2_0", "f1_0", "e2_0", OP.add, po=q)
+    ts("f3_0", "e3_0", 65536.0, OP.mult, T.a128[q[0]:q[1], 0:1], OP.add, r=("a128",), po=q)
+    tt("u_0", "f2_0", "f3_0", OP.add, po=q)
+    route(0, q)
+    quant("hq0", 0, 128, "xb", 0, 512, ("xb",), "hq0")
+    depart(0)
+    dma("y", [(T.nd[0:1, 0:A], ap("n_0", q))], r=("n_0",))
+    cp("nl1", "u_0", po=mine, pi=q, co=(2, 3), a=("nl1",))
+    constants()
+    slots(0)
+    hop(0)
+    for t in range(1, R + 1):
+        total_of("u_%d" % t, "nl%d" % t, po=mine, ci=(2, 11))
+        if t < R:
+            route(t, mine)
+            depart(t)
+            stand(t)
+            places(t)
+            pick("hq%d" % (t + 1), 0, A, "hq%d" % t, 0, HOME, "lu_%d" % t, ("hq%d" % t,), ("hq%d" % (t + 1),))
+            slots(t)
+            hop(t)
+        else:
+            rows(t, mine)
+            places(t)
+            stand(t)
+            pick("fin", 0, A, "hq%d" % t, 0, HOME, "lu_%d" % t, ("hq%d" % t,), ("fin",))
+            run("t", lambda: TE.matmul_mx(T.z0[:, 0:128], T.wqc[:], T.wqs[:], T.finc[:, 0:128], T.fins[:, 0:128], True, True), r=("wqc", "wqs", "finc", "fins"), w=("z0",))
+            dma("y", [(T.oc[:, 0:4 * A], codes("fin", 0, A))], r=("finc",))
+            dma("s", [(T.osc[4 * k:4 * k + 4, 0:A], T.fins[32 * k:32 * k + 4, 0:A]) for k in range(4)], r=("fins",))
+            run("v", lambda: V.tensor_copy(T.yb[:], T.z0[:, 0:A]), r=("z0",), w=("yb",))
+            dma("y", [(T.y[:, :], T.yb[:])], r=("yb",))
+    for sem in total:
+        if waited.get(sem, 0) < total[sem]:
+            g.wait_ge(T.sem[sem], total[sem])
+
+
+_sb("mm", 128, _B)
+_sb("mn", 128, _B)
+SEMAPHORES = [_x for _x in SEMAPHORES]

@@ -14,57 +14,57 @@ def _sb(name, cols, ty):
 _F, _I, _U, _B, _Q, _S = "float32", "int32", "uint16", "bfloat16", "float8_e4m3fn_x4", "uint8"
 for _n, _c, _t in [
     ("iF", 516, _F), ("eF", 516, _B), ("iw", 128, _B), ("ia", 64, _I), ("ia2", 64, _I), ("ib", 64, _I), ("ib2", 64, _I), ("iab", 64, _I),
-    ("mask64", 64, _F), ("mask32", 32, _F), ("ip", 1, _I), ("ip15", 1, _I), ("ip5", 1, _I), ("ip31", 1, _I), ("r1", 1, _F),
-    ("tb", 1, _F), ("a128", 1, _F), ("il", 1, _I), ("il2", 1, _I), ("cl1", 1, _F), ("cl2", 1, _F), ("cloc", 1, _F), ("i8", 8, _I),
-    ("i82", 8, _I), ("mask8", 8, _F), ("ja", 64, _F), ("rowb", 64, _F), ("ct", 64, _F), ("rst32", 64, _F), ("rst16", 64, _F),
-    ("c128", 4, _F), ("ik", 32, _I), ("ik2", 32, _I), ("ikb", 32, _I), ("ik3", 32, _I), ("ku", 32, _U), ("i2", 2, _I), ("i22", 2, _I),
+    ("mask96", 96, _F), ("ip", 1, _I), ("ip15", 1, _I), ("ip5", 1, _I), ("ip31", 1, _I), ("r1", 1, _F), ("tb", 1, _F), ("a128", 1, _F),
+    ("il", 1, _I), ("il2", 1, _I), ("cl1", 1, _F), ("cl2", 1, _F), ("cloc", 1, _F), ("i8", 8, _I), ("i82", 8, _I), ("mask8", 8, _F),
+    ("ja", 64, _F), ("rowb", 64, _F), ("ct", 64, _F), ("rst32", 64, _F), ("rst16", 96, _F), ("c128", 4, _F), ("i32", 8, _I),
+    ("ik", 32, _I), ("ik2", 32, _I), ("ikb", 32, _I), ("ik3", 32, _I), ("ku", 32, _U), ("i2", 2, _I), ("i22", 2, _I),
     ("mask2", 2, _F), ("stt", 2, _I), ("stm", 2, _F), ("nxa", 32, _I), ("nxf", 32, _F), ("nrow", 512, _F), ("tab", 512, _F),
-    ("xb", 512, _B), ("kb", 2048, _B), ("wb", 512, _B), ("yb", 32, _F),
+    ("xb", 512, _B), ("kb", 2048, _B), ("wb", 512, _B), ("yb", 32, _F), ("m0", 128, _B), ("m1", 128, _B),
 ]:
     _sb(_n, _c, _t)
-for _n, _c in [("kn", 512), ("kj", 512), ("wq", 128), ("e0", 128), ("e1", 128), ("e2", 128), ("e3", 128), ("hq0", 128), ("fin", 128)]:
+for _n, _c in [("kn", 512), ("kj", 512), ("wq", 128), ("e0", 128), ("e1", 128), ("e2", 128), ("e3", 128), ("hq0", 128), ("fin", 128), ("la", N * A)]:
     _sb(_n + "c", _c, _Q)
     _sb(_n + "s", _c, _S)
 for _t in range(R):
     for _n, _c in [("sd", 128), ("ld", 128), ("kp", 128), ("qn", 128)]:
-        _sb("%s%dc" % (_n, _t), _c, _Q)
-        _sb("%s%ds" % (_n, _t), _c, _S)
+        if _n != "sd" or _t > 0:
+            _sb("%s%dc" % (_n, _t), _c, _Q)
+            _sb("%s%ds" % (_n, _t), _c, _S)
     _sb("hq%dc" % (_t + 1), HOME, _Q)
     _sb("hq%ds" % (_t + 1), HOME, _S)
     _sb("pk%d" % _t, 8, _I)
     _sb("vl%d" % _t, 12, _I)
     _sb("sn%d" % _t, 32, _F)
     _sb("nl%d" % (_t + 1), 12, _F)
-SMALL, WF, WI, WU = {}, [0], [0], [0]
+    _sb("hb%d" % _t, 512, _B)
+SMALL, WIDE = {}, {"f": ["smf", 0], "i": ["smi", 0], "u": ["smu", 0]}
 
 
 def _small(ty, name, cols):
-    c = {"f": WF, "i": WI, "u": WU}[ty]
-    SMALL[name] = ({"f": "smf", "i": "smi", "u": "smu"}[ty], c[0], c[0] + cols)
-    c[0] += cols + cols % 2
+    w = WIDE[ty]
+    SMALL[name] = (w[0], w[1], w[1] + cols)
+    w[1] += cols + cols % 2
 
 
 for _t in range(R + 1):
     for _n, _c in [("u", 1), ("bc", 64), ("bt", 64), ("ind", 64), ("cum", 64), ("hit", 64), ("pkr", 64), ("ipk", 64), ("hpk", 64), ("sp", 64),
                    ("q0", 8), ("n", 1), ("f1", 1), ("f2", 1), ("f3", 1), ("lm", 32), ("lsc", 32), ("vp", 8), ("pkf", 1), ("wf", 1), ("a1", 1),
-                   ("c1", 1), ("i0", 64), ("oh", 64), ("oht", 64), ("q1", 1), ("dp", 1), ("p0", 128), ("p1", 128), ("p2", 128), ("p3", 128),
-                   ("s4", 4), ("mx", 1), ("ne", 4), ("js", 4), ("d0", 64), ("dt", 64), ("ds", 64), ("lf", 8), ("l2", 2), ("gt", 32),
-                   ("n1", 32), ("n2", 32), ("j0", 128), ("j1", 128), ("j2", 128), ("j3", 128)]:
+                   ("c1", 1), ("i0", 96), ("oh", 64), ("oht", 64), ("q1", 1), ("dp", 1), ("p0", 128), ("p1", 128), ("p2", 128), ("p3", 128),
+                   ("s4", 4), ("mx", 1), ("ne", 4), ("js", 4), ("d0", 96), ("dt", 96), ("ds", 96), ("lf", 8), ("gt", 32),
+                   ("n1", 32), ("n2", 32), ("j0", 128), ("j1", 128), ("j2", 128)]:
         _small("f", "%s_%d" % (_n, _t), _c)
-    for _n, _c in [("ri", 64), ("be", 64), ("lo", 64), ("sr", 8), ("ui", 1), ("e1", 1), ("e2", 1), ("e3", 1), ("e4", 1), ("lr", 32),
+    for _n, _c in [("ri", 64), ("be", 64), ("lo", 64), ("sr", 8), ("sx", 8), ("ui", 1), ("e1", 1), ("e2", 1), ("e3", 1), ("e4", 1), ("lr", 32),
                    ("pki", 1), ("wi", 1), ("ai", 1)]:
         _small("i", "%s_%d" % (_n, _t), _c)
     for _n, _c in [("su", 8), ("lu", 2), ("ko", 8), ("l2u", 2)]:
         _small("u", "%s_%d" % (_n, _t), _c)
-for _n, _c in [("x1", 32), ("x2", 32), ("x3", 32)]:
-    _small("i", _n, _c)
-for _n, _c in [("y1", 32), ("y2", 32), ("y3", 32)]:
-    _small("f", _n, _c)
-_sb("smf", WF[0], _F)
-_sb("smi", WI[0], _I)
-_sb("smu", WU[0], _U)
-for _t in range(R):
-    _sb("hb%d" % _t, 512, _B)
+for _n in ("x1", "x2", "x3"):
+    _small("i", _n, 32)
+for _n in ("y1", "y2", "y3"):
+    _small("f", _n, 32)
+_sb("smf", WIDE["f"][1], _F)
+_sb("smi", WIDE["i"][1], _I)
+_sb("smu", WIDE["u"][1], _U)
 for _b in range(4):
     SCRATCH["z%d" % _b] = ("psum", [128, 512], "float32")
     SCRATCH["d%d" % _b] = ("psum", [128, 512], "float32")
@@ -131,18 +131,25 @@ def rank_program(g, core, T, topo):
         done(q, sem, total[sem], r, w, a)
 
     others = [(me + i) % N for i in range(1, N)]
+    NUMBERS = [[(i,) for i in range(6)] + [(6, 7)]]
+    CODES = [[(0, 1), (2, 3), (4, 5), (6, 7)], [(0, 1), (2, 3), (4, 5, 6, 7)]]
+    SCALES = [[(0, 1), (2, 3), (4, 5), (6, 7)], [(4, 5), (6, 7), (0, 1, 2, 3)]]
+    per = lambda plan: sum(len(l) for c in plan for l in c)
 
-    def send(sem, part, r, rot):
+    def send(sem, part, r, plan):
         before("g", r, ())
-        tr = []
-        for i, d in enumerate(others):
-            dst = T.cores[d]
-            rid, pid, _ = topo.addr(dst)
-            es = topo.engines(core, dst)
-            o, s = part(d)
-            tr.append(RemoteDMATransfer(dst_ids=[DstId(rid=rid, pnc=pid)], dma_engine_mask=1 << es[(i + rot) % len(es)], remote_sem=T.sem[sem], src=s, dst=o))
-        g.remote_dma_fused(tr, local_sem=T.sem["ls"])
-        total["ls"] = total.get("ls", 0) + len(tr)
+        todo = list(others)
+        for call in plan:
+            tr = []
+            for lanes in call:
+                d = todo.pop(0)
+                dst = T.cores[d]
+                rid, pid, _ = topo.addr(dst)
+                es = topo.engines(core, dst)
+                o, s = part(d)
+                tr.append(RemoteDMATransfer(dst_ids=[DstId(rid=rid, pnc=pid)], dma_engine_mask=sum(1 << es[k] for k in lanes), remote_sem=T.sem[sem], src=s, dst=o))
+                total["ls"] = total.get("ls", 0) + len(lanes)
+            g.remote_dma_fused(tr, local_sem=T.sem["ls"])
 
     def arrive(sem, n, keys):
         total[sem] = n
@@ -169,23 +176,23 @@ def rank_program(g, core, T, topo):
     def plane(name, lo, hi):
         return T[name + "s"][:, lo:hi]
 
-    def ts(o, i, s1, op0, s2=None, op1=None, r=(), w=(), po=None, pi=None, co=None, ci=None, a=()):
+    def ts(o, i, s1, op0, s2=None, op1=None, r=(), po=None, pi=None, co=None, ci=None, a=()):
         def fn():
             out, in0 = ap(o, po, co), ap(i, pi if pi else po, ci)
             if op1 is None:
                 return V.tensor_scalar(out, in0, s1, None, op0)
             return V.tensor_scalar(out, in0, s1, s2, op0, op1)
-        run("v", fn, r=tuple(r) + (i,), w=w if (w or a) else (o,), a=a)
+        run("v", fn, r=tuple(r) + (i,), w=() if a else (o,), a=a)
 
-    def tt(o, x, y, op, po=None, co=None, cx=None, cy=None, w=(), a=()):
-        run("v", lambda: V.tensor_tensor(ap(o, po, co), ap(x, po, cx), ap(y, po, cy), op), r=(x, y), w=w if (w or a) else (o,), a=a)
+    def tt(o, x, y, op, po=None, co=None, cx=None, cy=None, a=()):
+        run("v", lambda: V.tensor_tensor(ap(o, po, co), ap(x, po, cx), ap(y, po, cy), op), r=(x, y), w=() if a else (o,), a=a)
 
-    def cp(o, i, po=None, pi=None, co=None, ci=None, w=(), a=(), q="v"):
+    def cp(o, i, po=None, pi=None, co=None, ci=None, a=(), q="v"):
         def fn():
             if q == "v":
                 return V.tensor_copy(ap(o, po, co), ap(i, pi if pi else po, ci))
             return S.activation(ap(o, po, co), ap(i, pi if pi else po, ci), CP)
-        run(q, fn, r=(i,), w=w if (w or a) else (o,), a=a)
+        run(q, fn, r=(i,), w=() if a else (o,), a=a)
 
     def scan(o, d0, d1, c0=None, po=None):
         run("v", lambda: V.tensor_tensor_scan(ap(o, po), ap(d0, po, c0), ap(d1, po), 0.0, OP.mult, OP.add), r=(d0, d1), w=(o,))
@@ -196,14 +203,20 @@ def rank_program(g, core, T, topo):
     def trans(o, i, po=None):
         run("v", lambda: V.transpose(ap(o, po), ap(i, po)), r=(i,), w=(o,))
 
-    def pick(o, olo, ohi, i, ilo, ihi, lst, r, wkeys, c=None):
-        buf, lo, hi = SMALL.get(lst, (lst, 0, SCRATCH[lst][1][1] if lst not in SMALL else 0))
-        off = T[buf][:, lo:hi]
-        run("v", lambda: V.tensor_copy(words(o, olo, ohi), words(i, ilo, ihi).indirect(off)), r=tuple(k + "c" for k in r) + (lst,), a=tuple(k + "c" for k in wkeys))
-        run("s", lambda: S.activation(plane(o, olo, ohi), plane(i, ilo, ihi).indirect(off), CP), r=tuple(k + "s" for k in r) + (lst,), a=tuple(k + "s" for k in wkeys))
+    def pick(o, olo, ohi, i, ilo, ihi, lst):
+        off = ap(lst)
+        run("v", lambda: V.tensor_copy(words(o, olo, ohi), words(i, ilo, ihi).indirect(off)), r=(i + "c", lst), a=(o + "c",))
+        run("s", lambda: S.activation(plane(o, olo, ohi), plane(i, ilo, ihi).indirect(off), CP), r=(i + "s", lst), a=(o + "s",))
 
-    def quant(o, lo, hi, src, slo, shi, r, w):
-        run("v", lambda: V.quantize_mx(T[o + "c"][:, lo:hi], T[o + "s"][:, lo:hi], T[src][:, slo:shi]), r=r, a=(w + "c", w + "s"))
+    def quant(o, hi, src, slo, shi):
+        run("v", lambda: V.quantize_mx(T[o + "c"][:, 0:hi], T[o + "s"][:, 0:hi], T[src][:, slo:shi]), r=(src,), a=(o + "c", o + "s"))
+
+    def mm(o, x, y, ylo, yhi, start, stop, new):
+        run("t", lambda: TE.matmul_mx(T[o][:, 0:128], T[x + "c"][:, 0:128], T[x + "s"][:, 0:128], T[y + "c"][:, ylo:yhi], T[y + "s"][:, ylo:yhi], start, stop),
+            r=(x + "c", x + "s", y + "c", y + "s"), w=(o,) if new else (), a=() if new else (o,))
+
+    def both(o, olo, ohi, i, ilo, ihi):
+        dma("y", [(codes(o, olo, ohi), codes(i, ilo, ihi)), (plane(o, olo, ohi), plane(i, ilo, ihi))], r=(i + "c", i + "s"), a=(o + "c", o + "s"))
 
     def iota(name, pattern, base, cm):
         if SCRATCH[name][2] == "int32":
@@ -225,20 +238,13 @@ def rank_program(g, core, T, topo):
     iota("ip", [[1, 1]], 0, 1)
     iota("i2", [[16, 2]], 0, 1)
     iota("ja", [[0, 2], [1, A]], 1, 0)
-    iota("ia", [[0, 2], [1, 32]], 256, -1)
-    iota("ib", [[32, 2], [0, 32]], 0, 1)
-    iota("i8", [[-16, 8]], 256 - 16 * me, 1)
-    iota("il", [[1, 1]], 16 * (me + 7) + 15, -1)
-    iota("ik", [[1, 4], [4, 4], [0, 2]], 0, 16)
-    iota("ikb", [[0, 16], [256, 2]], 0, 0)
-    iota("iw", [[1, 128]], 0, 0)
     iota("iF", [[1, 516]], -3, -4)
     run("v", lambda: V.memset(ap("ct", None, (0, 32)), float((15 - me) * 65536)), a=("ct",))
     run("v", lambda: V.memset(ap("ct", None, (32, 64)), float((14 - me) * 65536)), a=("ct",))
     run("v", lambda: V.memset(T.rst32[:], 1.0), w=("rst32",))
     run("v", lambda: V.memset(T.rst32[:, 0:64:32], 0.0), w=("rst32",))
     run("v", lambda: V.memset(T.rst16[:], 1.0), w=("rst16",))
-    run("v", lambda: V.memset(T.rst16[:, 0:64:16], 0.0), w=("rst16",))
+    run("v", lambda: V.memset(T.rst16[:, 0:96:16], 0.0), w=("rst16",))
     run("v", lambda: V.memset(T.c128[:], 128.0), w=("c128",))
     ts("ip15", "ip", 15, OP.bitwise_and)
     ts("r1", "ip15", 1.0, OP.add)
@@ -251,17 +257,14 @@ def rank_program(g, core, T, topo):
     ts("rowb", "ja", 65536.0, OP.mult)
 
     def constants():
-        ts("ia2", "ia", 15, OP.bitwise_and)
-        ts("mask32", "ia2", 0.0, OP.is_equal, ci=(0, 32))
-        ts("ib2", "ib", 32, OP.bitwise_and)
-        tt("iab", "ia2", "ib2", OP.add)
-        ts("mask64", "iab", 0.0, OP.is_equal)
-        ts("i82", "i8", 112, OP.bitwise_and)
-        ts("mask8", "i82", 0.0, OP.is_equal)
-        ts("il2", "il", 112, OP.bitwise_and)
-        ts("cl1", "il2", 128.0, OP.mult, float(128 * 32 - 65536 * me), OP.add)
-        ts("cl2", "r1", 128.0, OP.mult)
-        tt("cloc", "cl1", "cl2", OP.add)
+        iota("ik", [[1, 4], [4, 4], [0, 2]], 0, 16)
+        iota("ikb", [[0, 16], [256, 2]], 0, 0)
+        iota("ia", [[0, 2], [1, 32]], 256, -1)
+        iota("ib", [[32, 2], [0, 32]], 0, 1)
+        iota("i8", [[-16, 8]], 256 - 16 * me, 1)
+        iota("i32", [[A, N]], 0, 0)
+        iota("il", [[1, 1]], 16 * (me + 7) + 15, -1)
+        iota("iw", [[1, 128]], 0, 0)
         q = (0, 16)
         ts("x1", "nxa", 3, OP.bitwise_and, po=q)
         ts("x2", "nxa", 127, OP.bitwise_and, 2, OP.logical_shift_right, po=q)
@@ -272,17 +275,25 @@ def rank_program(g, core, T, topo):
         tt("nxf", "y2", "y3", OP.add, po=q)
         dma("y", [(T.nrow[0:1, 128 * j:128 * j + 128], T.nxf[j:16:4, :]) for j in range(4)], r=("nxf",), w=("nrow",))
         run("g", lambda: g.partition_broadcast(T.tab[:], T.nrow[0:1, :], 128), r=("nrow",), w=("tab",))
-        ts("eF", "iF", 0.0, OP.is_equal, 0.5, OP.mult)
-        for b in range(4):
-            quant("e%d" % b, 0, 128, "eF", 3 - b, 3 - b + 512, ("eF",), "e%d" % b)
+        quant("kn", 512, "kb", 0, 2048)
         ts("ik2", "ik", 255, OP.bitwise_and)
         tt("ik3", "ik2", "ikb", OP.add)
         cp("ku", "ik3")
-        quant("kn", 0, 512, "kb", 0, 2048, ("kb",), "kn")
-        pick("kj", 0, 512, "kn", 0, 512, "ku", ("kn",), ("kj",))
-        quant("wq", 0, 128, "wb", 0, 512, ("wb",), "wq")
-        dma("y", [(codes("fin", A, 128), codes("hq0", A, 128)), (plane("fin", A, 128), plane("hq0", A, 128))], r=("hq0c", "hq0s"), a=("finc", "fins"))
-        dma("y", [(codes("hq1", 0, A), codes("hq0", 0, A)), (plane("hq1", 0, A), plane("hq0", 0, A))], r=("hq0c", "hq0s"), a=("hq1c", "hq1s"))
+        pick("kj", 0, 512, "kn", 0, 512, "ku")
+        ts("eF", "iF", 0.0, OP.is_equal, 0.5, OP.mult)
+        for b in range(4):
+            quant("e%d" % b, 128, "eF", 3 - b, 3 - b + 512)
+        ts("ia2", "ia", 15, OP.bitwise_and)
+        ts("ib2", "ib", 32, OP.bitwise_and)
+        ts("mask96", "ia2", 0.0, OP.is_equal, co=(64, 96), ci=(0, 32), a=("mask96",))
+        tt("iab", "ia2", "ib2", OP.add)
+        ts("mask96", "iab", 0.0, OP.is_equal, co=(0, 64), a=("mask96",))
+        ts("i82", "i8", 112, OP.bitwise_and)
+        ts("mask8", "i82", 0.0, OP.is_equal)
+        ts("il2", "il", 112, OP.bitwise_and)
+        ts("cl1", "il2", 128.0, OP.mult, float(128 * 32 - 65536 * me), OP.add)
+        ts("cl2", "r1", 128.0, OP.mult)
+        tt("cloc", "cl1", "cl2", OP.add)
 
     def rows(t, q):
         n = "_%d" % t
@@ -304,24 +315,28 @@ def rank_program(g, core, T, topo):
         tt("hpk" + n, "hit" + n, "ipk" + n, OP.mult)
         scan("sp" + n, "rst32", "hpk" + n)
         for b in range(4):
-            cp("q0" + n, "sp" + n, po=(0, 32), pi=quad[b], co=(2 * b, 2 * b + 2), ci=(31, 64, 32), a=("q0" + n,), q="v" if b < 2 else "s")
+            cp("q0" + n, "sp" + n, po=(0, 32), pi=quad[b], co=(2 * b, 2 * b + 2), ci=(31, 64, 32), a=("q0" + n,))
         for b in quad:
             cp("pk%d" % t, "q0" + n, po=b, pi=(0, 32), a=("pk%d" % t,))
-        send("apk%d" % t, lambda d: (T["vl%d" % t][:, 3 + (me - d) % N:4 + (me - d) % N], T["pk%d" % t][:, (d - me - 1) % N:(d - me - 1) % N + 1]), ("pk%d" % t,), 2)
-        ts("sr" + n, "pk%d" % t, 7, OP.logical_shift_right, 511, OP.bitwise_and)
-        cp("su" + n, "sr" + n)
+        vl, pk = T["vl%d" % t], T["pk%d" % t]
+        send("apk%d" % t, lambda d: (vl[:, 3 + (me - d) % N:4 + (me - d) % N], pk[:, (d - me - 1) % N:(d - me - 1) % N + 1]), ("pk%d" % t,), NUMBERS)
+        if t > 0:
+            ts("sr" + n, "pk%d" % t, 7, OP.logical_shift_right, 511, OP.bitwise_and)
+            cp("su" + n, "sr" + n)
+
+    def expect(t, land):
+        cp("vl%d" % t, "pk%d" % t, co=(3, 4), ci=(7, 8), a=("vl%d" % t,))
+        arrive("apk%d" % t, per(NUMBERS), ("vl%d" % t,))
+        arrive("aco%d" % t, per(CODES) + per(SCALES), (land + "c", land + "s"))
 
     def depart(t):
-        hi = 128 if t == 0 else HOME
-        pick("sd%d" % t, 0, 128, "hq%d" % t, 0, hi, "su_%d" % t, ("hq%d" % t,), ("sd%d" % t,))
+        ld, sd, sem = "ld%d" % t, "sd%d" % t, "aco%d" % t
+        pick(sd, 0, 128, "hq%d" % t, 0, HOME, "su_%d" % t)
         at = lambda d: CAP * ((d - me - 1) % N)
-        send("aco%d" % t, lambda d: (codes("ld%d" % t, CAP * me, CAP * me + CAP), codes("sd%d" % t, at(d), at(d) + CAP)), ("sd%dc" % t,), 0)
-        send("aco%d" % t, lambda d: (plane("ld%d" % t, CAP * me, CAP * me + CAP), plane("sd%d" % t, at(d), at(d) + CAP)), ("sd%ds" % t,), 1)
-        dma("y", [(codes("ld%d" % t, CAP * me, CAP * me + CAP), codes("sd%d" % t, 112, 128)), (plane("ld%d" % t, CAP * me, CAP * me + CAP), plane("sd%d" % t, 112, 128))],
-            r=("sd%dc" % t, "sd%ds" % t), a=("ld%dc" % t, "ld%ds" % t))
-        cp("vl%d" % t, "pk%d" % t, co=(3, 4), ci=(7, 8), a=("vl%d" % t,))
-        arrive("apk%d" % t, 7, ("vl%d" % t,))
-        arrive("aco%d" % t, 14, ("ld%dc" % t, "ld%ds" % t))
+        send(sem, lambda d: (codes(ld, CAP * me, CAP * me + CAP), codes(sd, at(d), at(d) + CAP)), (sd + "c",), CODES)
+        send(sem, lambda d: (plane(ld, CAP * me, CAP * me + CAP), plane(sd, at(d), at(d) + CAP)), (sd + "s",), SCALES)
+        both(ld, CAP * me, CAP * me + CAP, sd, 112, 128)
+        expect(t, ld)
 
     def stand(t):
         n, q = "_%d" % t, mine
@@ -342,77 +357,76 @@ def rank_program(g, core, T, topo):
     def places(t):
         n = "_%d" % t
         ts("lr" + n, "ri" + n, 7, OP.logical_shift_right, 511, OP.bitwise_and, ci=(0, 32))
-        tt("lm" + n, "lr" + n, "mask32", OP.mult)
+        tt("lm" + n, "lr" + n, "mask96", OP.mult, cy=(64, 96))
         scan("lsc" + n, "rst16", "lm" + n, c0=(0, 32))
         cp("lu" + n, "lsc" + n, ci=(15, 32, 16))
 
     def slots(t):
         n = "_%d" % t
-        run("v", lambda: V.tensor_tensor(ap("vp" + n), ap("vl%d" % t, None, (3, 11)), T.mask8[:], OP.mult), r=("vl%d" % t, "mask8"), w=("vp" + n,))
+        tt("vp" + n, "vl%d" % t, "mask8", OP.mult, cx=(3, 11))
         total_of("pkf" + n, "vp" + n)
         cp("pki" + n, "pkf" + n)
         ts("wi" + n, "pki" + n, 127, OP.bitwise_and)
         ts("ai" + n, "pki" + n, 16, OP.logical_shift_right)
         cp("wf" + n, "wi" + n)
-        run("v", lambda: V.tensor_scalar(T.mm[:] if t % 2 == 0 else T.mn[:], T.iw[:], ap("wf" + n), None, OP.is_equal), r=("iw", "wf" + n), w=("mm%d" % (t % 2),))
+        ts("m%d" % (t % 2), "iw", ap("wf" + n), OP.is_equal, r=("wf" + n,))
         cp("a1" + n, "ai" + n)
         ts("c1" + n, "wf" + n, 1024.0, OP.add)
-        ts("i0" + n, "mask64", ap("c1" + n), OP.mult, -1024.0, OP.add, r=("c1" + n,))
+        ts("i0" + n, "mask96", ap("c1" + n), OP.mult, -1024.0, OP.add, r=("c1" + n,))
         ts("oh" + n, "ja", ap("a1" + n), OP.is_equal, r=("a1" + n,), co=(0, 32), ci=(0, 32), a=("oh" + n,))
         ts("q1" + n, "a1" + n, -128.0, OP.mult, T.cloc[:, 0:1], OP.add, r=("cloc",))
         tt("dp" + n, "q1" + n, "wf" + n, OP.subtract)
-        run("v", lambda: V.tensor_scalar(ap("oh" + n, None, (32, 64)), ap("oh" + n, None, (0, 32)), ap("dp" + n), None, OP.mult), r=("oh" + n, "dp" + n), a=("oh" + n,))
+        ts("oh" + n, "oh" + n, ap("dp" + n), OP.mult, r=("dp" + n,), co=(32, 64), ci=(0, 32), a=("oh" + n,))
         trans("oht" + n, "oh" + n)
 
     def hop(t):
-        n, ld, kp, qn = "_%d" % t, "ld%d" % t, "kp%d" % t, "qn%d" % t
+        n, ld, kp, qn, sn = "_%d" % t, "ld%d" % t, "kp%d" % t, "qn%d" % t, "sn%d" % t
+        m = "m%d" % (t % 2)
         for j in range(4):
-            run("t", lambda: TE.matmul_mx(T["z%d" % j][:, 0:128], T[ld + "c"][:, 0:128], T[ld + "s"][:, 0:128], T.kjc[:, 128 * j:128 * j + 128], T.kjs[:, 128 * j:128 * j + 128], True, True),
-                r=(ld + "c", ld + "s", "kjc", "kjs"), w=("z%d" % j,))
+            mm("z%d" % j, ld, "kj", 128 * j, 128 * j + 128, True, True, True)
         for b in range(4):
-            run("t", lambda: TE.matmul_mx(T["d%d" % b][:, 0:128], T["e%dc" % b][:], T["e%ds" % b][:], T[ld + "c"][:, 0:128], T[ld + "s"][:, 0:128], True, False),
-                r=(ld + "c", ld + "s", "e%dc" % b, "e%ds" % b), w=("d%d" % b,))
-        m = T.mm if t % 2 == 0 else T.mn
+            mm("d%d" % b, "e%d" % b, ld, 0, 128, True, False, True)
         for j in range(4):
-            run("v", lambda: V.tensor_tensor(ap("p%d" % j + n), T["z%d" % j][:, 0:128], m[:], OP.mult), r=("z%d" % j, "mm%d" % (t % 2)), w=("p%d" % j + n,))
-            run("s", lambda: S.activation(ap("j%d" % j + n), ap("p%d" % j + n), CP, accum_out=ap("s4" + n, None, (3 - j, 4 - j))), r=("p%d" % j + n,), w=("j%d" % j + n,), a=("s4" + n,))
+            tt("p%d" % j + n, "z%d" % j, m, OP.mult, cx=(0, 128))
+            if j < 3:
+                run("s", lambda: S.activation(ap("j%d" % j + n), ap("p%d" % j + n), CP, accum_out=ap("s4" + n, None, (3 - j, 4 - j))), r=("p%d" % j + n,), w=("j%d" % j + n,), a=("s4" + n,))
+        run("v", lambda: V.tensor_reduce(ap("s4" + n, None, (0, 1)), ap("p3" + n), X, OP.add), r=("p3" + n,), a=("s4" + n,))
         run("v", lambda: V.tensor_reduce(ap("mx" + n), ap("s4" + n), X, OP.max), r=("s4" + n,), w=("mx" + n,))
         ts("ne" + n, "s4" + n, ap("mx" + n), OP.not_equal, 1000000.0, OP.mult, r=("mx" + n,))
         run("v", lambda: V.tensor_tensor_scan(ap("js" + n), T.c128[:], ap("ne" + n), 0.0, OP.add, OP.min), r=("c128", "ne" + n), w=("js" + n,))
         ts("d0" + n, "i0" + n, ap("js" + n, None, (3, 4)), OP.add, 0.0, OP.max, r=("js" + n,))
         trans("dt" + n, "d0" + n)
         scan("ds" + n, "rst16", "dt" + n)
+        cp("l2u" + n, "ds" + n, ci=(79, 96, 16))
+        run("v", lambda: V.tensor_copy(ap("gt" + n), T.tab[:, 0:512].indirect(ap("l2u" + n))), r=("tab", "l2u" + n), w=("gt" + n,))
+        tt("n1" + n, "gt" + n, "oht" + n, OP.mult, cy=(0, 32))
+        tt("n2" + n, "n1" + n, "oht" + n, OP.add, cy=(32, 64))
+        scan(sn, "rst16", "n2" + n, c0=(0, 32))
+        beta = lambda s: (me - s - 1) % N
+        nl = "nl%d" % (t + 1)
+        send("adl%d" % t, lambda s: (T[nl][:, 4 + beta(s):5 + beta(s)], T[sn][:, 15 + 16 * (s % 2):16 + 16 * (s % 2)]), (sn,), NUMBERS)
+        arrive("adl%d" % t, per(NUMBERS), (nl,))
         for k in range(2):
             run("v", lambda: V.tensor_tensor(ap("lf" + n, (0, 32), (4 * k, 4 * k + 4)), ap("ds" + n, quad[2 * k], (15, 64, 16)), ap("ds" + n, quad[2 * k + 1], (15, 64, 16)), OP.add),
                 r=("ds" + n,), a=("lf" + n,))
         for b in quad:
             cp("ko" + n, "lf" + n, po=b, pi=(0, 32), a=("ko" + n,))
-        pick(kp, 0, 128, "kj", 0, 512, "ko" + n, ("kj",), (kp,))
+        pick(kp, 0, 128, "kj", 0, 512, "ko" + n)
         for b in range(4):
-            run("t", lambda: TE.matmul_mx(T["d%d" % b][:, 0:128], T["e%dc" % b][:], T["e%ds" % b][:], T[kp + "c"][:], T[kp + "s"][:], False, True),
-                r=(kp + "c", kp + "s", "e%dc" % b, "e%ds" % b), a=("d%d" % b,))
-        run("v", lambda: V.tensor_tensor(ap("l2" + n), ap("ds" + n, None, (15, 32, 16)), ap("ds" + n, None, (47, 64, 16)), OP.add), r=("ds" + n,), w=("l2" + n,))
-        cp("l2u" + n, "l2" + n)
-        run("v", lambda: V.tensor_copy(ap("gt" + n), T.tab[:, 0:512].indirect(ap("l2u" + n))), r=("tab", "l2u" + n), w=("gt" + n,))
-        tt("n1" + n, "gt" + n, "oht" + n, OP.mult, cy=(0, 32))
-        tt("n2" + n, "n1" + n, "oht" + n, OP.add, cy=(32, 64))
-        run("v", lambda: V.tensor_tensor_scan(T["sn%d" % t][:], T.rst16[:, 0:32], ap("n2" + n), 0.0, OP.mult, OP.add), r=("rst16", "n2" + n), w=("sn%d" % t,))
-        beta = lambda s: (me - s - 1) % N
-        send("adl%d" % t, lambda s: (T["nl%d" % (t + 1)][:, 4 + beta(s):5 + beta(s)], T["sn%d" % t][:, 15 + 16 * (s % 2):16 + 16 * (s % 2)]), ("sn%d" % t,), 2)
-        arrive("adl%d" % t, 7, ("nl%d" % (t + 1),))
+            mm("d%d" % b, "e%d" % b, kp, 0, 128, False, True, False)
         for b in range(4):
             o = T["hb%d" % t][:, b:512:4]
             if b % 2 == 0:
                 run("s", lambda: S.activation(o, T["d%d" % b][:, 0:128], CP), r=("d%d" % b,), a=("hb%d" % t,))
             else:
                 run("v", lambda: V.tensor_copy(o, T["d%d" % b][:, 0:128]), r=("d%d" % b,), a=("hb%d" % t,))
-        quant(qn, 0, 128, "hb%d" % t, 0, 512, ("hb%d" % t,), qn)
-        h = "hq%d" % (t + 1)
-        send("are%d" % t, lambda s: (codes(h, A + CAP * beta(s), A + CAP * beta(s) + CAP), codes(qn, CAP * s, CAP * s + CAP)), (qn + "c",), 0)
-        send("are%d" % t, lambda s: (plane(h, A + CAP * beta(s), A + CAP * beta(s) + CAP), plane(qn, CAP * s, CAP * s + CAP)), (qn + "s",), 1)
-        dma("y", [(codes(h, A + 112, HOME), codes(qn, CAP * me, CAP * me + CAP)), (plane(h, A + 112, HOME), plane(qn, CAP * me, CAP * me + CAP))], r=(qn + "c", qn + "s"), a=(h + "c", h + "s"))
-        arrive("are%d" % t, 14, (h + "c", h + "s"))
-        cp("nl%d" % (t + 1), "sn%d" % t, po=mine, co=(3, 4), ci=(15 + 16 * half, 16 + 16 * half), a=("nl%d" % (t + 1),))
+        quant(qn, 128, "hb%d" % t, 0, 512)
+        h, sem = "hq%d" % (t + 1), "are%d" % t
+        send(sem, lambda s: (codes(h, A + CAP * beta(s), A + CAP * beta(s) + CAP), codes(qn, CAP * s, CAP * s + CAP)), (qn + "c",), CODES)
+        send(sem, lambda s: (plane(h, A + CAP * beta(s), A + CAP * beta(s) + CAP), plane(qn, CAP * s, CAP * s + CAP)), (qn + "s",), SCALES)
+        both(h, A + 112, HOME, qn, CAP * me, CAP * me + CAP)
+        arrive(sem, per(CODES) + per(SCALES), (h + "c", h + "s"))
+        cp(nl, sn, po=mine, co=(3, 4), ci=(15 + 16 * half, 16 + 16 * half), a=(nl,))
 
     q = quad[0]
     tt("stm", "stt", "mask2", OP.mult, po=q)
@@ -425,13 +439,25 @@ def rank_program(g, core, T, topo):
     tt("f2_0", "f1_0", "e2_0", OP.add, po=q)
     ts("f3_0", "e3_0", 65536.0, OP.mult, T.a128[q[0]:q[1], 0:1], OP.add, r=("a128",), po=q)
     tt("u_0", "f2_0", "f3_0", OP.add, po=q)
+    quant("hq0", 128, "xb", 0, 512)
+    send("aco0", lambda d: (codes("la", A * me, A * me + A), codes("hq0", 0, A)), ("hq0c",), CODES)
     route(0, q)
-    quant("hq0", 0, 128, "xb", 0, 512, ("xb",), "hq0")
-    depart(0)
-    dma("y", [(T.nd[0:1, 0:A], ap("n_0", q))], r=("n_0",))
+    send("aco0", lambda d: (plane("la", A * me, A * me + A), plane("hq0", 0, A)), ("hq0s",), SCALES)
+    both("la", A * me, A * me + A, "hq0", 0, A)
+    expect(0, "la")
     cp("nl1", "u_0", po=mine, pi=q, co=(2, 3), a=("nl1",))
     constants()
+    quant("wq", 128, "wb", 0, 512)
+    dma("y", [(T.nd[0:1, 0:A], ap("n_0", q))], r=("n_0",))
+    both("fin", A, 128, "hq0", A, 128)
+    both("hq1", 0, A, "hq0", 0, A)
+    ts("sr_0", "vl0", 7, OP.logical_shift_right, 511, OP.bitwise_and, ci=(3, 11))
+    tt("sx_0", "sr_0", "i32", OP.add, co=(me, N), cx=(0, N - me), cy=(me, N), a=("sx_0",))
+    if me:
+        tt("sx_0", "sr_0", "i32", OP.add, co=(0, me), cx=(N - me, N), cy=(0, me), a=("sx_0",))
+    cp("su_0", "sx_0")
     slots(0)
+    pick("ld0", 0, 128, "la", 0, N * A, "su_0")
     hop(0)
     for t in range(1, R + 1):
         total_of("u_%d" % t, "nl%d" % t, po=mine, ci=(2, 11))
@@ -440,15 +466,15 @@ def rank_program(g, core, T, topo):
             depart(t)
             stand(t)
             places(t)
-            pick("hq%d" % (t + 1), 0, A, "hq%d" % t, 0, HOME, "lu_%d" % t, ("hq%d" % t,), ("hq%d" % (t + 1),))
+            pick("hq%d" % (t + 1), 0, A, "hq%d" % t, 0, HOME, "lu_%d" % t)
             slots(t)
             hop(t)
         else:
             rows(t, mine)
             places(t)
             stand(t)
-            pick("fin", 0, A, "hq%d" % t, 0, HOME, "lu_%d" % t, ("hq%d" % t,), ("fin",))
-            run("t", lambda: TE.matmul_mx(T.z0[:, 0:128], T.wqc[:], T.wqs[:], T.finc[:, 0:128], T.fins[:, 0:128], True, True), r=("wqc", "wqs", "finc", "fins"), w=("z0",))
+            pick("fin", 0, A, "hq%d" % t, 0, HOME, "lu_%d" % t)
+            mm("z0", "wq", "fin", 0, 128, True, True, True)
             dma("y", [(T.oc[:, 0:4 * A], codes("fin", 0, A))], r=("finc",))
             dma("s", [(T.osc[4 * k:4 * k + 4, 0:A], T.fins[32 * k:32 * k + 4, 0:A]) for k in range(4)], r=("fins",))
             run("v", lambda: V.tensor_copy(T.yb[:], T.z0[:, 0:A]), r=("z0",), w=("yb",))
@@ -456,8 +482,3 @@ def rank_program(g, core, T, topo):
     for sem in total:
         if waited.get(sem, 0) < total[sem]:
             g.wait_ge(T.sem[sem], total[sem])
-
-
-_sb("mm", 128, _B)
-_sb("mn", 128, _B)
-SEMAPHORES = [_x for _x in SEMAPHORES]

@@ -3,6 +3,7 @@ from concourse.mybir import dt, AluOpType, AxisListType, ActivationFunctionType
 
 R, A, P, CAP, N = 3, 32, 512, 16, 8
 HOME = A + N * CAP
+OWN, KEPT, STEP = 12, 13, 14
 
 SCRATCH = {}
 
@@ -13,20 +14,21 @@ def _sb(name, cols, ty):
 
 _F, _I, _U, _B, _Q, _S = "float32", "int32", "uint16", "bfloat16", "float8_e4m3fn_x4", "uint8"
 for _n, _c, _t in [
-    ("iF", 516, _F), ("eF", 516, _B), ("iw", 128, _B), ("ia", 64, _I), ("ia2", 64, _I), ("ib", 64, _I), ("ib2", 64, _I), ("iab", 64, _I),
-    ("mask96", 96, _F), ("ip", 1, _I), ("ip15", 1, _I), ("ip5", 1, _I), ("ip31", 1, _I), ("r1", 1, _F), ("tb", 1, _F), ("a128", 1, _F),
-    ("il", 1, _I), ("il2", 1, _I), ("cl1", 1, _F), ("cl2", 1, _F), ("cloc", 1, _F), ("i8", 8, _I), ("i82", 8, _I), ("mask8", 8, _F),
-    ("ja", 64, _F), ("rowb", 64, _F), ("ct", 64, _F), ("rst32", 64, _F), ("rst16", 96, _F), ("c128", 4, _F), ("i32", 8, _I),
-    ("ik", 32, _I), ("ik2", 32, _I), ("ikb", 32, _I), ("ik3", 32, _I), ("ku", 32, _U), ("i2", 2, _I), ("i22", 2, _I),
-    ("mask2", 2, _F), ("stt", 2, _I), ("stm", 2, _F), ("nxa", 32, _I), ("nxf", 32, _F), ("nrow", 512, _F), ("tab", 512, _F),
-    ("xb", 512, _B), ("kb", 2048, _B), ("wb", 512, _B), ("yb", 32, _F), ("m0", 128, _B), ("m1", 128, _B),
+    ("iF", 516, _B), ("eF", 516, _B), ("iw", 128, _B), ("ia", 32, _I), ("ia2", 32, _I), ("ic", 32, _I), ("ic2", 32, _I), ("mask", 64, _F),
+    ("ip", 1, _I), ("ip15", 1, _I), ("ip5", 1, _I), ("ip31", 1, _I), ("ip3", 1, _I),
+    ("r1", 1, _F), ("tb", 1, _F), ("a128", 1, _F), ("t4", 1, _F), ("il", 1, _I), ("il2", 1, _I), ("cl1", 1, _F), ("cl2", 1, _F),
+    ("cloc", 1, _F), ("i8", 8, _I), ("i82", 8, _I), ("mask8", 8, _F), ("ja", 64, _F), ("rowb", 64, _F), ("ct", 64, _F), ("rst32", 64, _F),
+    ("rst", 64, _F), ("one", 73, _F), ("c128", 4, _F), ("i32", 8, _I), ("ik", 32, _I), ("ik2", 32, _I), ("ikb", 32, _I), ("ik3", 32, _I),
+    ("ku", 32, _U), ("i2", 2, _I), ("i22", 2, _I), ("mask2", 2, _F), ("stt", 2, _I), ("nxa", 32, _I), ("nxf", 32, _F),
+    ("nrow", 512, _F), ("tab", 512, _F), ("xb", 512, _B), ("kb", 2048, _B), ("wb", 512, _B), ("yb", 32, _F), ("m0", 128, _B), ("m1", 128, _B),
+    ("kd", 2048, _F),
 ]:
     _sb(_n, _c, _t)
 for _n, _c in [("kn", 512), ("kj", 512), ("wq", 128), ("e0", 128), ("e1", 128), ("e2", 128), ("e3", 128), ("hq0", 128), ("fin", 128), ("la", N * A)]:
     _sb(_n + "c", _c, _Q)
     _sb(_n + "s", _c, _S)
 for _t in range(R):
-    for _n, _c in [("sd", 128), ("ld", 128), ("kp", 128), ("qn", 128)]:
+    for _n, _c in [("sd", 128), ("ld", 128), ("qn", 128)]:
         if _n != "sd" or _t > 0:
             _sb("%s%dc" % (_n, _t), _c, _Q)
             _sb("%s%ds" % (_n, _t), _c, _S)
@@ -35,7 +37,8 @@ for _t in range(R):
     _sb("pk%d" % _t, 8, _I)
     _sb("vl%d" % _t, 12, _I)
     _sb("sn%d" % _t, 32, _F)
-    _sb("nl%d" % (_t + 1), 12, _F)
+    _sb("nl%d" % (_t + 1), 80, _F)
+    _sb("dq%d" % _t, 512, _F)
     _sb("hb%d" % _t, 512, _B)
 SMALL, WIDE = {}, {"f": ["smf", 0], "i": ["smi", 0], "u": ["smu", 0]}
 
@@ -47,21 +50,21 @@ def _small(ty, name, cols):
 
 
 for _t in range(R + 1):
-    for _n, _c in [("u", 1), ("bc", 64), ("bt", 64), ("ind", 64), ("cum", 64), ("hit", 64), ("pkr", 64), ("ipk", 64), ("hpk", 64), ("sp", 64),
-                   ("q0", 8), ("n", 1), ("f1", 1), ("f2", 1), ("f3", 1), ("lm", 32), ("lsc", 32), ("vp", 8), ("pkf", 1), ("wf", 1), ("a1", 1),
-                   ("c1", 1), ("i0", 96), ("oh", 64), ("oht", 64), ("q1", 1), ("dp", 1), ("p0", 128), ("p1", 128), ("p2", 128), ("p3", 128),
-                   ("s4", 4), ("mx", 1), ("ne", 4), ("js", 4), ("d0", 96), ("dt", 96), ("ds", 96), ("lf", 8), ("gt", 32),
+    for _n, _c in [("u", 1), ("bc", 73), ("bt", 64), ("ind", 64), ("cum", 64), ("hit", 64), ("pkr", 64), ("ipk", 64), ("hpk", 64), ("sp", 64),
+                   ("q0", 8), ("n", 1), ("f1", 1), ("f2", 1), ("f3", 1), ("f4", 1), ("lm", 32), ("lsc", 32), ("vp", 8), ("pkf", 1), ("wf", 1), ("a1", 1),
+                   ("c1", 1), ("i0", 64), ("oh", 64), ("oht", 64), ("q1", 1), ("dp", 1), ("p0", 128), ("p1", 128), ("p2", 128), ("p3", 128),
+                   ("s4", 4), ("mx", 1), ("ne", 4), ("js", 4), ("d0", 64), ("dt", 64), ("ds", 64), ("lf", 32), ("gt", 32),
                    ("n1", 32), ("n2", 32), ("j0", 128), ("j1", 128), ("j2", 128)]:
         _small("f", "%s_%d" % (_n, _t), _c)
     for _n, _c in [("ri", 64), ("be", 64), ("lo", 64), ("sr", 8), ("sx", 8), ("ui", 1), ("e1", 1), ("e2", 1), ("e3", 1), ("e4", 1), ("lr", 32),
                    ("pki", 1), ("wi", 1), ("ai", 1)]:
         _small("i", "%s_%d" % (_n, _t), _c)
-    for _n, _c in [("su", 8), ("lu", 2), ("ko", 8), ("l2u", 2)]:
+    for _n, _c in [("su", 8), ("lu", 2), ("ko", 32), ("l2u", 2)]:
         _small("u", "%s_%d" % (_n, _t), _c)
-for _n in ("x1", "x2", "x3"):
-    _small("i", _n, 32)
-for _n in ("y1", "y2", "y3"):
-    _small("f", _n, 32)
+for _n, _c in [("x1", 32), ("x2", 32), ("x3", 32), ("g1", 2), ("g2", 2), ("g3", 2)]:
+    _small("i", _n, _c)
+for _n, _c in [("y1", 32), ("y2", 32), ("y3", 32), ("h1", 2), ("h2", 2), ("h3", 2), ("h4", 2), ("h5", 2), ("stm", 2)]:
+    _small("f", _n, _c)
 _sb("smf", WIDE["f"][1], _F)
 _sb("smi", WIDE["i"][1], _I)
 _sb("smu", WIDE["u"][1], _U)
@@ -187,21 +190,20 @@ def rank_program(g, core, T, topo):
     def tt(o, x, y, op, po=None, co=None, cx=None, cy=None, a=()):
         run("v", lambda: V.tensor_tensor(ap(o, po, co), ap(x, po, cx), ap(y, po, cy), op), r=(x, y), w=() if a else (o,), a=a)
 
-    def cp(o, i, po=None, pi=None, co=None, ci=None, a=(), q="v"):
-        def fn():
-            if q == "v":
-                return V.tensor_copy(ap(o, po, co), ap(i, pi if pi else po, ci))
-            return S.activation(ap(o, po, co), ap(i, pi if pi else po, ci), CP)
-        run(q, fn, r=(i,), w=() if a else (o,), a=a)
+    def cp(o, i, po=None, pi=None, co=None, ci=None, a=()):
+        run("v", lambda: V.tensor_copy(ap(o, po, co), ap(i, pi if pi else po, ci)), r=(i,), w=() if a else (o,), a=a)
 
-    def scan(o, d0, d1, c0=None, po=None):
-        run("v", lambda: V.tensor_tensor_scan(ap(o, po), ap(d0, po, c0), ap(d1, po), 0.0, OP.mult, OP.add), r=(d0, d1), w=(o,))
+    def scan(o, d0, d1, c0=None, c1=None, po=None):
+        run("v", lambda: V.tensor_tensor_scan(ap(o, po), ap(d0, po, c0), ap(d1, po, c1), 0.0, OP.mult, OP.add), r=(d0, d1), w=(o,))
 
     def total_of(o, i, po=None, ci=None):
         run("v", lambda: V.tensor_reduce(ap(o, po), ap(i, po, ci), X, OP.add), r=(i,), w=(o,))
 
-    def trans(o, i, po=None):
-        run("v", lambda: V.transpose(ap(o, po), ap(i, po)), r=(i,), w=(o,))
+    def trans(o, i, po=None, ci=None):
+        run("v", lambda: V.transpose(ap(o, po), ap(i, po, ci)), r=(i,), w=(o,))
+
+    def fill(o, c, value):
+        run("v", lambda: V.memset(ap(o, None, c), float(value)), w=(o,))
 
     def pick(o, olo, ohi, i, ilo, ihi, lst):
         off = ap(lst)
@@ -211,9 +213,9 @@ def rank_program(g, core, T, topo):
     def quant(o, hi, src, slo, shi):
         run("v", lambda: V.quantize_mx(T[o + "c"][:, 0:hi], T[o + "s"][:, 0:hi], T[src][:, slo:shi]), r=(src,), a=(o + "c", o + "s"))
 
-    def mm(o, x, y, ylo, yhi, start, stop, new):
-        run("t", lambda: TE.matmul_mx(T[o][:, 0:128], T[x + "c"][:, 0:128], T[x + "s"][:, 0:128], T[y + "c"][:, ylo:yhi], T[y + "s"][:, ylo:yhi], start, stop),
-            r=(x + "c", x + "s", y + "c", y + "s"), w=(o,) if new else (), a=() if new else (o,))
+    def mm(o, x, y, ylo, yhi):
+        run("t", lambda: TE.matmul_mx(T[o][:, 0:yhi - ylo], T[x + "c"][:, 0:128], T[x + "s"][:, 0:128], T[y + "c"][:, ylo:yhi], T[y + "s"][:, ylo:yhi], True, True),
+            r=(x + "c", x + "s", y + "c", y + "s"), w=(o,))
 
     def both(o, olo, ohi, i, ilo, ihi):
         dma("y", [(codes(o, olo, ohi), codes(i, ilo, ihi)), (plane(o, olo, ohi), plane(i, ilo, ihi))], r=(i + "c", i + "s"), a=(o + "c", o + "s"))
@@ -239,66 +241,76 @@ def rank_program(g, core, T, topo):
     iota("i2", [[16, 2]], 0, 1)
     iota("ja", [[0, 2], [1, A]], 1, 0)
     iota("iF", [[1, 516]], -3, -4)
-    run("v", lambda: V.memset(ap("ct", None, (0, 32)), float((15 - me) * 65536)), a=("ct",))
+    fill("ct", (0, 32), (15 - me) * 65536)
     run("v", lambda: V.memset(ap("ct", None, (32, 64)), float((14 - me) * 65536)), a=("ct",))
-    run("v", lambda: V.memset(T.rst32[:], 1.0), w=("rst32",))
-    run("v", lambda: V.memset(T.rst32[:, 0:64:32], 0.0), w=("rst32",))
-    run("v", lambda: V.memset(T.rst16[:], 1.0), w=("rst16",))
-    run("v", lambda: V.memset(T.rst16[:, 0:96:16], 0.0), w=("rst16",))
-    run("v", lambda: V.memset(T.c128[:], 128.0), w=("c128",))
+    fill("rst32", None, 1)
+    fill("rst32", (0, 64, 32), 0)
+    fill("rst", None, 1)
+    fill("rst", (0, 32, 4), 0)
+    fill("rst", (32, 64, 16), 0)
+    fill("c128", None, 128)
     ts("ip15", "ip", 15, OP.bitwise_and)
-    ts("r1", "ip15", 1.0, OP.add)
     ts("ip5", "ip", 5, OP.logical_shift_right)
-    ts("tb", "ip5", 2.0, OP.mult)
     ts("ip31", "ip", 31, OP.bitwise_and)
-    ts("a128", "ip31", 128.0, OP.mult)
     ts("i22", "i2", 16, OP.bitwise_and)
+    ts("r1", "ip15", 1.0, OP.add)
+    ts("tb", "ip5", 2.0, OP.mult)
+    ts("a128", "ip31", 128.0, OP.mult)
     ts("mask2", "i22", 0.0, OP.is_equal)
     ts("rowb", "ja", 65536.0, OP.mult)
+    ts("ip3", "ip", 3, OP.bitwise_and)
+    ts("cl2", "r1", 128.0, OP.mult)
+    ts("t4", "ip3", 1.0, OP.mult)
 
     def constants():
-        iota("ik", [[1, 4], [4, 4], [0, 2]], 0, 16)
-        iota("ikb", [[0, 16], [256, 2]], 0, 0)
-        iota("ia", [[0, 2], [1, 32]], 256, -1)
-        iota("ib", [[32, 2], [0, 32]], 0, 1)
-        iota("i8", [[-16, 8]], 256 - 16 * me, 1)
         iota("i32", [[A, N]], 0, 0)
-        iota("il", [[1, 1]], 16 * (me + 7) + 15, -1)
         iota("iw", [[1, 128]], 0, 0)
         q = (0, 16)
         ts("x1", "nxa", 3, OP.bitwise_and, po=q)
         ts("x2", "nxa", 127, OP.bitwise_and, 2, OP.logical_shift_right, po=q)
         ts("x3", "nxa", 7, OP.logical_shift_right, po=q)
         ts("y1", "x1", 32.0, OP.mult, po=q)
-        tt("y2", "y1", "x2", OP.add, po=q)
         ts("y3", "x3", 65536.0, OP.mult, po=q)
+        tt("y2", "y1", "x2", OP.add, po=q)
         tt("nxf", "y2", "y3", OP.add, po=q)
         dma("y", [(T.nrow[0:1, 128 * j:128 * j + 128], T.nxf[j:16:4, :]) for j in range(4)], r=("nxf",), w=("nrow",))
         run("g", lambda: g.partition_broadcast(T.tab[:], T.nrow[0:1, :], 128), r=("nrow",), w=("tab",))
         quant("kn", 512, "kb", 0, 2048)
         ts("ik2", "ik", 255, OP.bitwise_and)
+        ts("eF", "iF", 0.0, OP.is_equal, 0.5, OP.mult)
         tt("ik3", "ik2", "ikb", OP.add)
         cp("ku", "ik3")
         pick("kj", 0, 512, "kn", 0, 512, "ku")
-        ts("eF", "iF", 0.0, OP.is_equal, 0.5, OP.mult)
         for b in range(4):
             quant("e%d" % b, 128, "eF", 3 - b, 3 - b + 512)
-        ts("ia2", "ia", 15, OP.bitwise_and)
-        ts("ib2", "ib", 32, OP.bitwise_and)
-        ts("mask96", "ia2", 0.0, OP.is_equal, co=(64, 96), ci=(0, 32), a=("mask96",))
-        tt("iab", "ia2", "ib2", OP.add)
-        ts("mask96", "iab", 0.0, OP.is_equal, co=(0, 64), a=("mask96",))
+        for b in range(4):
+            mm("d%d" % b, "e%d" % b, "kj", 0, 512)
+            run("s", lambda: S.activation(T.kd[:, b:2048:4], T["d%d" % b][:, 0:512], CP), r=("d%d" % b,), a=("kd",))
+        ts("ia2", "ia", 3, OP.bitwise_and)
+        ts("ic2", "ic", 15, OP.bitwise_and)
         ts("i82", "i8", 112, OP.bitwise_and)
-        ts("mask8", "i82", 0.0, OP.is_equal)
         ts("il2", "il", 112, OP.bitwise_and)
+        ts("mask", "ia2", 0.0, OP.is_equal, co=(0, 32), a=("mask",))
+        ts("mask", "ic2", 0.0, OP.is_equal, co=(32, 64), a=("mask",))
+        ts("mask8", "i82", 0.0, OP.is_equal)
         ts("cl1", "il2", 128.0, OP.mult, float(128 * 32 - 65536 * me), OP.add)
-        ts("cl2", "r1", 128.0, OP.mult)
         tt("cloc", "cl1", "cl2", OP.add)
+
+    def steps():
+        fill("one", None, 1)
+        for t in range(1, R + 1):
+            nl = "nl%d" % t
+            for c, v in [((STEP, STEP + 64), 0), ((STEP, STEP + 1), (15 - me) * 65536), ((STEP + 32, STEP + 33), -65536)]:
+                run("v", lambda: V.memset(ap(nl, None, c), float(v)), r=(nl + "k",), a=(nl + "k",))
 
     def rows(t, q):
         n = "_%d" % t
-        ts("bc" + n, "ct", ap("u" + n, q), OP.add, r=("u" + n,), po=q)
-        trans("bt" + n, "bc" + n, q)
+        if t == 0:
+            ts("bc" + n, "ct", ap("u" + n, q), OP.add, r=("u" + n,), po=q, co=(9, 73))
+        else:
+            nl = "nl%d" % t
+            run("v", lambda: V.tensor_tensor_scan(ap("bc" + n, q), ap("one", q), ap(nl, q, (5, STEP + 64)), 0.0, OP.mult, OP.add), r=("one", nl, nl + "k"), w=("bc" + n,))
+        trans("bt" + n, "bc" + n, q, ci=(9, 73))
         for b in quad:
             cp("ri" + n, "bt" + n, po=b, pi=q, a=("ri" + n,))
 
@@ -306,10 +318,10 @@ def rank_program(g, core, T, topo):
         n = "_%d" % t
         rows(t, q)
         ts("be" + n, "ri" + n, 16, OP.logical_shift_right, 7, OP.bitwise_and)
-        ts("ind" + n, "be" + n, T.tb[:, 0:1], OP.is_equal, r=("tb",))
-        scan("cum" + n, "rst32", "ind" + n)
         ts("lo" + n, "ri" + n, 65535, OP.bitwise_and)
+        ts("ind" + n, "be" + n, T.tb[:, 0:1], OP.is_equal, r=("tb",))
         tt("pkr" + n, "lo" + n, "rowb", OP.add)
+        scan("cum" + n, "rst32", "ind" + n)
         tt("ipk" + n, "ind" + n, "pkr" + n, OP.mult)
         ts("hit" + n, "cum" + n, T.r1[:, 0:1], OP.is_equal, r=("r1",))
         tt("hpk" + n, "hit" + n, "ipk" + n, OP.mult)
@@ -340,25 +352,25 @@ def rank_program(g, core, T, topo):
 
     def stand(t):
         n, q = "_%d" % t, mine
-        cp("ui" + n, "u" + n, po=q)
+        cp("ui" + n, "bc" + n, po=q, ci=(8, 9))
         ts("e1" + n, "ui" + n, 31, OP.bitwise_and, po=q)
         ts("e2" + n, "ui" + n, 127, OP.bitwise_and, 5, OP.logical_shift_right, po=q)
         ts("e3" + n, "ui" + n, 16, OP.logical_shift_right, po=q)
+        ts("e4" + n, "ui" + n, 127, OP.bitwise_and, po=q)
         ts("f1" + n, "e1" + n, 4.0, OP.mult, po=q)
-        tt("f2" + n, "f1" + n, "e2" + n, OP.add, po=q)
         ts("f3" + n, "e3" + n, 128.0, OP.mult, po=q)
+        ts("f4" + n, "e3" + n, 65536.0, OP.mult, T.a128[q[0]:q[1], 0:1], OP.add, r=("a128",), po=q)
+        tt("f2" + n, "f1" + n, "e2" + n, OP.add, po=q)
+        if t < R:
+            run("v", lambda: V.tensor_tensor(ap("nl%d" % (t + 1), q, (KEPT, KEPT + 1)), ap("f4" + n, q), ap("e4" + n, q), OP.add), r=("f4" + n, "e4" + n), a=("nl%d" % (t + 1),))
         tt("n" + n, "f2" + n, "f3" + n, OP.add, po=q)
         dma("y", [(T.nd[t:t + 1, 0:A], ap("n" + n, q))], r=("n" + n,))
-        if t < R:
-            ts("e4" + n, "ui" + n, 127, OP.bitwise_and, po=q)
-            ts("f3" + n, "e3" + n, 65536.0, OP.mult, T.a128[q[0]:q[1], 0:1], OP.add, r=("a128",), po=q)
-            run("v", lambda: V.tensor_tensor(ap("nl%d" % (t + 1), q, (2, 3)), ap("f3" + n, q), ap("e4" + n, q), OP.add), r=("f3" + n, "e4" + n), a=("nl%d" % (t + 1),))
 
     def places(t):
         n = "_%d" % t
         ts("lr" + n, "ri" + n, 7, OP.logical_shift_right, 511, OP.bitwise_and, ci=(0, 32))
-        tt("lm" + n, "lr" + n, "mask96", OP.mult, cy=(64, 96))
-        scan("lsc" + n, "rst16", "lm" + n, c0=(0, 32))
+        tt("lm" + n, "lr" + n, "mask", OP.mult, cy=(32, 64))
+        scan("lsc" + n, "rst", "lm" + n, c0=(32, 64))
         cp("lu" + n, "lsc" + n, ci=(15, 32, 16))
 
     def slots(t):
@@ -369,88 +381,86 @@ def rank_program(g, core, T, topo):
         ts("wi" + n, "pki" + n, 127, OP.bitwise_and)
         ts("ai" + n, "pki" + n, 16, OP.logical_shift_right)
         cp("wf" + n, "wi" + n)
-        ts("m%d" % (t % 2), "iw", ap("wf" + n), OP.is_equal, r=("wf" + n,))
         cp("a1" + n, "ai" + n)
+        ts("m%d" % (t % 2), "iw", ap("wf" + n), OP.is_equal, r=("wf" + n,))
         ts("c1" + n, "wf" + n, 1024.0, OP.add)
-        ts("i0" + n, "mask96", ap("c1" + n), OP.mult, -1024.0, OP.add, r=("c1" + n,))
         ts("oh" + n, "ja", ap("a1" + n), OP.is_equal, r=("a1" + n,), co=(0, 32), ci=(0, 32), a=("oh" + n,))
         ts("q1" + n, "a1" + n, -128.0, OP.mult, T.cloc[:, 0:1], OP.add, r=("cloc",))
+        ts("i0" + n, "mask", ap("c1" + n), OP.mult, -1024.0, OP.add, r=("c1" + n,))
         tt("dp" + n, "q1" + n, "wf" + n, OP.subtract)
         ts("oh" + n, "oh" + n, ap("dp" + n), OP.mult, r=("dp" + n,), co=(32, 64), ci=(0, 32), a=("oh" + n,))
         trans("oht" + n, "oh" + n)
 
     def hop(t):
-        n, ld, kp, qn, sn = "_%d" % t, "ld%d" % t, "kp%d" % t, "qn%d" % t, "sn%d" % t
-        m = "m%d" % (t % 2)
+        n, ld, qn, sn, dq, hb = "_%d" % t, "ld%d" % t, "qn%d" % t, "sn%d" % t, "dq%d" % t, "hb%d" % t
+        nl, h = "nl%d" % (t + 1), "hq%d" % (t + 1)
         for j in range(4):
-            mm("z%d" % j, ld, "kj", 128 * j, 128 * j + 128, True, True, True)
+            mm("z%d" % j, ld, "kj", 128 * j, 128 * j + 128)
         for b in range(4):
-            mm("d%d" % b, "e%d" % b, ld, 0, 128, True, False, True)
+            mm("d%d" % b, "e%d" % b, ld, 0, 128)
         for j in range(4):
-            tt("p%d" % j + n, "z%d" % j, m, OP.mult, cx=(0, 128))
+            tt("p%d" % j + n, "z%d" % j, "m%d" % (t % 2), OP.mult, cx=(0, 128))
             if j < 3:
                 run("s", lambda: S.activation(ap("j%d" % j + n), ap("p%d" % j + n), CP, accum_out=ap("s4" + n, None, (3 - j, 4 - j))), r=("p%d" % j + n,), w=("j%d" % j + n,), a=("s4" + n,))
+        for b in range(4):
+            run("s", lambda: S.activation(T[dq][:, b:512:4], T["d%d" % b][:, 0:128], CP), r=("d%d" % b,), a=(dq,))
         run("v", lambda: V.tensor_reduce(ap("s4" + n, None, (0, 1)), ap("p3" + n), X, OP.add), r=("p3" + n,), a=("s4" + n,))
         run("v", lambda: V.tensor_reduce(ap("mx" + n), ap("s4" + n), X, OP.max), r=("s4" + n,), w=("mx" + n,))
         ts("ne" + n, "s4" + n, ap("mx" + n), OP.not_equal, 1000000.0, OP.mult, r=("mx" + n,))
         run("v", lambda: V.tensor_tensor_scan(ap("js" + n), T.c128[:], ap("ne" + n), 0.0, OP.add, OP.min), r=("c128", "ne" + n), w=("js" + n,))
         ts("d0" + n, "i0" + n, ap("js" + n, None, (3, 4)), OP.add, 0.0, OP.max, r=("js" + n,))
         trans("dt" + n, "d0" + n)
-        scan("ds" + n, "rst16", "dt" + n)
-        cp("l2u" + n, "ds" + n, ci=(79, 96, 16))
+        scan("ds" + n, "rst", "dt" + n)
+
+        def join(b):
+            cp("lf" + n, "ds" + n, po=(0, 32), pi=quad[b], co=(8 * b, 8 * b + 8), ci=(3, 32, 4), a=("lf" + n,))
+        cp("l2u" + n, "ds" + n, ci=(47, 64, 16))
+        join(0)
         run("v", lambda: V.tensor_copy(ap("gt" + n), T.tab[:, 0:512].indirect(ap("l2u" + n))), r=("tab", "l2u" + n), w=("gt" + n,))
+        join(1)
         tt("n1" + n, "gt" + n, "oht" + n, OP.mult, cy=(0, 32))
         tt("n2" + n, "n1" + n, "oht" + n, OP.add, cy=(32, 64))
-        scan(sn, "rst16", "n2" + n, c0=(0, 32))
+        scan(sn, "rst", "n2" + n, c0=(32, 64))
         beta = lambda s: (me - s - 1) % N
-        nl = "nl%d" % (t + 1)
-        send("adl%d" % t, lambda s: (T[nl][:, 4 + beta(s):5 + beta(s)], T[sn][:, 15 + 16 * (s % 2):16 + 16 * (s % 2)]), (sn,), NUMBERS)
+        send("adl%d" % t, lambda s: (T[nl][:, 5 + beta(s):6 + beta(s)], T[sn][:, 15 + 16 * (s % 2):16 + 16 * (s % 2)]), (sn,), NUMBERS)
         arrive("adl%d" % t, per(NUMBERS), (nl,))
-        for k in range(2):
-            run("v", lambda: V.tensor_tensor(ap("lf" + n, (0, 32), (4 * k, 4 * k + 4)), ap("ds" + n, quad[2 * k], (15, 64, 16)), ap("ds" + n, quad[2 * k + 1], (15, 64, 16)), OP.add),
-                r=("ds" + n,), a=("lf" + n,))
+        join(2)
+        join(3)
         for b in quad:
-            cp("ko" + n, "lf" + n, po=b, pi=(0, 32), a=("ko" + n,))
-        pick(kp, 0, 128, "kj", 0, 512, "ko" + n)
-        for b in range(4):
-            mm("d%d" % b, "e%d" % b, kp, 0, 128, False, True, False)
-        for b in range(4):
-            o = T["hb%d" % t][:, b:512:4]
-            if b % 2 == 0:
-                run("s", lambda: S.activation(o, T["d%d" % b][:, 0:128], CP), r=("d%d" % b,), a=("hb%d" % t,))
-            else:
-                run("v", lambda: V.tensor_copy(o, T["d%d" % b][:, 0:128]), r=("d%d" % b,), a=("hb%d" % t,))
-        quant(qn, 128, "hb%d" % t, 0, 512)
-        h, sem = "hq%d" % (t + 1), "are%d" % t
+            ts("ko" + n, "lf" + n, 4.0, OP.mult, T.t4[0:32, 0:1], OP.add, r=("t4",), po=b, pi=(0, 32), a=("ko" + n,))
+        run("v", lambda: V.tensor_tensor(T[hb][:], T.kd[:, 0:2048].indirect(ap("ko" + n)), T[dq][:], OP.add), r=("kd", "ko" + n, dq), w=(hb,))
+        quant(qn, 128, hb, 0, 512)
+        sem = "are%d" % t
         send(sem, lambda s: (codes(h, A + CAP * beta(s), A + CAP * beta(s) + CAP), codes(qn, CAP * s, CAP * s + CAP)), (qn + "c",), CODES)
         send(sem, lambda s: (plane(h, A + CAP * beta(s), A + CAP * beta(s) + CAP), plane(qn, CAP * s, CAP * s + CAP)), (qn + "s",), SCALES)
         both(h, A + 112, HOME, qn, CAP * me, CAP * me + CAP)
         arrive(sem, per(CODES) + per(SCALES), (h + "c", h + "s"))
-        cp(nl, sn, po=mine, co=(3, 4), ci=(15 + 16 * half, 16 + 16 * half), a=(nl,))
+        cp(nl, sn, po=mine, co=(OWN, OWN + 1), ci=(15 + 16 * half, 16 + 16 * half), a=(nl,))
 
     q = quad[0]
-    tt("stm", "stt", "mask2", OP.mult, po=q)
-    total_of("n_0", "stm", po=q)
-    cp("ui_0", "n_0", po=q)
-    ts("e1_0", "ui_0", 3, OP.bitwise_and, po=q)
-    ts("e2_0", "ui_0", 127, OP.bitwise_and, 2, OP.logical_shift_right, po=q)
-    ts("e3_0", "ui_0", 7, OP.logical_shift_right, po=q)
-    ts("f1_0", "e1_0", 32.0, OP.mult, po=q)
-    tt("f2_0", "f1_0", "e2_0", OP.add, po=q)
-    ts("f3_0", "e3_0", 65536.0, OP.mult, T.a128[q[0]:q[1], 0:1], OP.add, r=("a128",), po=q)
-    tt("u_0", "f2_0", "f3_0", OP.add, po=q)
     quant("hq0", 128, "xb", 0, 512)
     send("aco0", lambda d: (codes("la", A * me, A * me + A), codes("hq0", 0, A)), ("hq0c",), CODES)
+    iota("ik", [[1, 4], [4, 4], [0, 2]], 0, 16)
+    iota("ikb", [[0, 16], [256, 2]], 0, 0)
+    iota("ia", [[1, 8], [0, 4]], 256, -1)
+    iota("ic", [[1, 32]], 256, -1)
+    iota("i8", [[-16, 8]], 256 - 16 * me, 1)
+    iota("il", [[1, 1]], 16 * (me + 7) + 15, -1)
+    ts("g1", "stt", 3, OP.bitwise_and, po=q)
+    ts("g2", "stt", 127, OP.bitwise_and, 2, OP.logical_shift_right, po=q)
+    ts("g3", "stt", 7, OP.logical_shift_right, po=q)
+    ts("h1", "g1", 32.0, OP.mult, po=q)
+    ts("h3", "g3", 65536.0, OP.mult, T.a128[q[0]:q[1], 0:1], OP.add, r=("a128",), po=q)
+    tt("h2", "h1", "g2", OP.add, po=q)
+    tt("h4", "h2", "h3", OP.add, po=q)
+    tt("h5", "h4", "mask2", OP.mult, po=q)
+    total_of("u_0", "h5", po=q)
     route(0, q)
     send("aco0", lambda d: (plane("la", A * me, A * me + A), plane("hq0", 0, A)), ("hq0s",), SCALES)
     both("la", A * me, A * me + A, "hq0", 0, A)
     expect(0, "la")
-    cp("nl1", "u_0", po=mine, pi=q, co=(2, 3), a=("nl1",))
+    cp("nl1", "u_0", po=mine, pi=q, co=(KEPT, KEPT + 1), a=("nl1",))
     constants()
-    quant("wq", 128, "wb", 0, 512)
-    dma("y", [(T.nd[0:1, 0:A], ap("n_0", q))], r=("n_0",))
-    both("fin", A, 128, "hq0", A, 128)
-    both("hq1", 0, A, "hq0", 0, A)
     ts("sr_0", "vl0", 7, OP.logical_shift_right, 511, OP.bitwise_and, ci=(3, 11))
     tt("sx_0", "sr_0", "i32", OP.add, co=(me, N), cx=(0, N - me), cy=(me, N), a=("sx_0",))
     if me:
@@ -459,8 +469,14 @@ def rank_program(g, core, T, topo):
     slots(0)
     pick("ld0", 0, 128, "la", 0, N * A, "su_0")
     hop(0)
+    steps()
+    tt("stm", "stt", "mask2", OP.mult, po=q)
+    total_of("n_0", "stm", po=q)
+    dma("y", [(T.nd[0:1, 0:A], ap("n_0", q))], r=("n_0",))
+    quant("wq", 128, "wb", 0, 512)
+    both("fin", A, 128, "hq0", A, 128)
+    both("hq1", 0, A, "hq0", 0, A)
     for t in range(1, R + 1):
-        total_of("u_%d" % t, "nl%d" % t, po=mine, ci=(2, 11))
         if t < R:
             route(t, mine)
             depart(t)
@@ -474,7 +490,7 @@ def rank_program(g, core, T, topo):
             places(t)
             stand(t)
             pick("fin", 0, A, "hq%d" % t, 0, HOME, "lu_%d" % t)
-            mm("z0", "wq", "fin", 0, 128, True, True, True)
+            mm("z0", "wq", "fin", 0, 128)
             dma("y", [(T.oc[:, 0:4 * A], codes("fin", 0, A))], r=("finc",))
             dma("s", [(T.osc[4 * k:4 * k + 4, 0:A], T.fins[32 * k:32 * k + 4, 0:A]) for k in range(4)], r=("fins",))
             run("v", lambda: V.tensor_copy(T.yb[:], T.z0[:, 0:A]), r=("z0",), w=("yb",))

@@ -3,6 +3,7 @@ from concourse.mybir import dt, AluOpType, AxisListType, ActivationFunctionType
 
 R, A, P, CAP, N = 3, 32, 512, 16, 8
 HOME = A + N * CAP
+FIRST, REST = (1, 2), (3,)
 OWN, KEPT, STEP = 12, 13, 14
 
 SCRATCH = {}
@@ -14,12 +15,12 @@ def _sb(name, cols, ty):
 
 _F, _I, _U, _B, _Q, _S = "float32", "int32", "uint16", "bfloat16", "float8_e4m3fn_x4", "uint8"
 for _n, _c, _t in [
-    ("iF", 516, _B), ("eF", 516, _B), ("iw", 128, _B), ("ia", 32, _I), ("ia2", 32, _I), ("ic", 32, _I), ("ic2", 32, _I), ("mask", 64, _F),
-    ("ip", 1, _I), ("ip15", 1, _I), ("ip5", 1, _I), ("ip31", 1, _I), ("ip3", 1, _I),
-    ("r1", 1, _F), ("tb", 1, _F), ("a128", 1, _F), ("t4", 1, _F), ("il", 1, _I), ("il2", 1, _I), ("cl1", 1, _F), ("cl2", 1, _F),
-    ("cloc", 1, _F), ("i8", 8, _I), ("i82", 8, _I), ("mask8", 8, _F), ("ja", 64, _F), ("rowb", 64, _F), ("ct", 64, _F), ("rst32", 64, _F),
-    ("rst", 64, _F), ("one", 73, _F), ("c128", 4, _F), ("i32", 8, _I), ("ik", 32, _I), ("ik2", 32, _I), ("ikb", 32, _I), ("ik3", 32, _I),
-    ("ku", 32, _U), ("i2", 2, _I), ("i22", 2, _I), ("mask2", 2, _F), ("stt", 2, _I), ("nxa", 32, _I), ("nxf", 32, _F),
+    ("eF", 516, _B), ("iw", 128, _B), ("ia", 32, _I), ("ia2", 32, _I), ("ic", 32, _I), ("ic2", 32, _I), ("mask", 64, _F),
+    ("ip", 1, _I), ("ip15", 1, _I), ("ip5", 1, _I), ("ip31", 1, _I), ("ip3", 1, _I), ("ipf", 1, _F),
+    ("r1", 1, _F), ("tb", 1, _F), ("af", 1, _F), ("t4", 1, _F), ("cl1", 1, _F), ("r4", 1, _F),
+    ("cloc", 1, _F), ("i8", 8, _I), ("i82", 8, _I), ("mask8", 8, _F), ("ja", 64, _F), ("rowb", 64, _F), ("rowx", 64, _F), ("ct", 64, _F),
+    ("rst32", 64, _F), ("rst", 64, _F), ("one", 73, _F), ("c1s", 4, _F), ("ik", 32, _I),
+    ("ku", 32, _U), ("stt", 3, _I), ("nxa", 32, _I), ("nxf", 32, _F), ("nxt", 32, _F),
     ("nrow", 512, _F), ("tab", 512, _F), ("xb", 512, _B), ("kb", 2048, _B), ("wb", 512, _B), ("yb", 32, _F), ("m0", 128, _B), ("m1", 128, _B),
     ("kd", 2048, _F),
 ]:
@@ -51,20 +52,15 @@ def _small(ty, name, cols):
 
 for _t in range(R + 1):
     for _n, _c in [("u", 1), ("bc", 73), ("bt", 64), ("ind", 64), ("cum", 64), ("hit", 64), ("pkr", 64), ("ipk", 64), ("hpk", 64), ("sp", 64),
-                   ("q0", 8), ("n", 1), ("f1", 1), ("f2", 1), ("f3", 1), ("f4", 1), ("lm", 32), ("lsc", 32), ("vp", 8), ("pkf", 1), ("wf", 1), ("a1", 1),
+                   ("q0", 8), ("n", 1), ("lm", 32), ("lsc", 32), ("vp", 8), ("pkf", 1), ("vf", 1), ("a1", 1),
                    ("c1", 1), ("i0", 64), ("oh", 64), ("oht", 64), ("q1", 1), ("dp", 1), ("p0", 128), ("p1", 128), ("p2", 128), ("p3", 128),
-                   ("s4", 4), ("mx", 1), ("ne", 4), ("js", 4), ("d0", 64), ("dt", 64), ("ds", 64), ("lf", 32), ("gt", 32),
-                   ("n1", 32), ("n2", 32), ("j0", 128), ("j1", 128), ("j2", 128)]:
+                   ("s4", 4), ("mx", 1), ("ne", 4), ("js", 4), ("d0", 64), ("dt", 64), ("ds", 64), ("lf", 32),
+                   ("n1", 32), ("j0", 128), ("j1", 128), ("j2", 128)]:
         _small("f", "%s_%d" % (_n, _t), _c)
-    for _n, _c in [("ri", 64), ("be", 64), ("lo", 64), ("sr", 8), ("sx", 8), ("ui", 1), ("e1", 1), ("e2", 1), ("e3", 1), ("e4", 1), ("lr", 32),
-                   ("pki", 1), ("wi", 1), ("ai", 1)]:
+    for _n, _c in [("ri", 64), ("be", 64), ("lo", 64), ("sr", 8), ("ui", 1), ("ni", 1), ("lr", 32), ("pki", 1), ("vi", 1), ("ai", 1)]:
         _small("i", "%s_%d" % (_n, _t), _c)
     for _n, _c in [("su", 8), ("lu", 2), ("ko", 32), ("l2u", 2)]:
         _small("u", "%s_%d" % (_n, _t), _c)
-for _n, _c in [("x1", 32), ("x2", 32), ("x3", 32), ("g1", 2), ("g2", 2), ("g3", 2)]:
-    _small("i", _n, _c)
-for _n, _c in [("y1", 32), ("y2", 32), ("y3", 32), ("h1", 2), ("h2", 2), ("h3", 2), ("h4", 2), ("h5", 2), ("stm", 2)]:
-    _small("f", _n, _c)
 _sb("smf", WIDE["f"][1], _F)
 _sb("smi", WIDE["i"][1], _I)
 _sb("smu", WIDE["u"][1], _U)
@@ -202,8 +198,8 @@ def rank_program(g, core, T, topo):
     def trans(o, i, po=None, ci=None):
         run("v", lambda: V.transpose(ap(o, po), ap(i, po, ci)), r=(i,), w=(o,))
 
-    def fill(o, c, value):
-        run("v", lambda: V.memset(ap(o, None, c), float(value)), w=(o,))
+    def fill(o, c, value, a=()):
+        run("v", lambda: V.memset(ap(o, None, c), float(value)), w=() if a else (o,), a=a)
 
     def pick(o, olo, ohi, i, ilo, ihi, lst):
         off = ap(lst)
@@ -229,79 +225,73 @@ def rank_program(g, core, T, topo):
     quad = [(32 * b, 32 * b + 32) for b in range(4)]
     mine = quad[me // 2]
     half = me % 2
+    later = []
 
-    dma("y", [(T.stt[0:16, 0:2], T.st[:, :]), (T.stt[16:32, 0:2], T.st[:, :])], w=("stt",))
+    def gap():
+        if later:
+            later.pop(0)()
+
+    dma("y", [(T.stt[0:16, 1:3], T.st[:, :]), (T.stt[16:32, 0:2], T.st[:, :])], w=("stt",))
     dma("s", [(T.xb[:, 0:4 * A], T.x[:, :])], a=("xb",))
-    dma("y", [(T.nxa[0:16, :], T.nx[:, :])], w=("nxa",))
-    dma("s", [(T.kb[:], T.ky[:, :])], w=("kb",))
+    dma("y", [(T.nxa[0:16, :], T.nx[:, :]), (T.nxa[16:32, :], T.nx[:, :])], w=("nxa",))
+    dma("y", [(T.kb[:], T.ky[:, :])], w=("kb",))
     dma("y", [(T.wb[:], T.w[:, :])], w=("wb",))
 
     run("v", lambda: V.memset(T.xb[:, 4 * A:512], 0.0), a=("xb",))
     iota("ip", [[1, 1]], 0, 1)
-    iota("i2", [[16, 2]], 0, 1)
     iota("ja", [[0, 2], [1, A]], 1, 0)
-    iota("iF", [[1, 516]], -3, -4)
-    fill("ct", (0, 32), (15 - me) * 65536)
-    run("v", lambda: V.memset(ap("ct", None, (32, 64)), float((14 - me) * 65536)), a=("ct",))
-    fill("rst32", None, 1)
-    fill("rst32", (0, 64, 32), 0)
-    fill("rst", None, 1)
-    fill("rst", (0, 32, 4), 0)
-    fill("rst", (32, 64, 16), 0)
-    fill("c128", None, 128)
+    iota("iw", [[1, 128]], 0, 0)
+    iota("i8", [[-16, 8]], 256 - 16 * me, 1)
+    iota("ik", [[1, 4], [64, 8]], 0, 0)
+    iota("ia", [[1, 8], [0, 4]], 256, -1)
+    iota("ic", [[1, 32]], 256, -1)
+    fill("ct", (0, 32), (15 - me) * 32768)
+    fill("ct", (32, 64), (14 - me) * 32768, a=("ct",))
+    ts("ip31", "ip", 31, OP.bitwise_and)
     ts("ip15", "ip", 15, OP.bitwise_and)
     ts("ip5", "ip", 5, OP.logical_shift_right)
-    ts("ip31", "ip", 31, OP.bitwise_and)
-    ts("i22", "i2", 16, OP.bitwise_and)
+    cp("af", "ip31")
     ts("r1", "ip15", 1.0, OP.add)
     ts("tb", "ip5", 2.0, OP.mult)
-    ts("a128", "ip31", 128.0, OP.mult)
-    ts("mask2", "i22", 0.0, OP.is_equal)
-    ts("rowb", "ja", 65536.0, OP.mult)
-    ts("ip3", "ip", 3, OP.bitwise_and)
-    ts("cl2", "r1", 128.0, OP.mult)
-    ts("t4", "ip3", 1.0, OP.mult)
+    ts("rowx", "ja", 32768.0, OP.mult, float(A * me), OP.add)
+    quant("hq0", 128, "xb", 0, 512)
 
-    def constants():
-        iota("i32", [[A, N]], 0, 0)
-        iota("iw", [[1, 128]], 0, 0)
-        q = (0, 16)
-        ts("x1", "nxa", 3, OP.bitwise_and, po=q)
-        ts("x2", "nxa", 127, OP.bitwise_and, 2, OP.logical_shift_right, po=q)
-        ts("x3", "nxa", 7, OP.logical_shift_right, po=q)
-        ts("y1", "x1", 32.0, OP.mult, po=q)
-        ts("y3", "x3", 65536.0, OP.mult, po=q)
-        tt("y2", "y1", "x2", OP.add, po=q)
-        tt("nxf", "y2", "y3", OP.add, po=q)
-        dma("y", [(T.nrow[0:1, 128 * j:128 * j + 128], T.nxf[j:16:4, :]) for j in range(4)], r=("nxf",), w=("nrow",))
+    later.append(lambda: fill("rst32", None, 1))
+    later.append(lambda: fill("rst32", (0, 64, 32), 0))
+    later.append(lambda: fill("eF", None, 0))
+    later.append(lambda: cp("ipf", "ip"))
+    later.append(lambda: ts("ip3", "ip", 3, OP.bitwise_and))
+    later.append(lambda: run("v", lambda: V.tensor_scalar(T.eF[:, 3:515:4], T.iw[:], T.ipf[:, 0:1], 0.5, OP.is_equal, OP.mult), r=("iw", "ipf"), w=("eF",)))
+    later.append(lambda: ts("t4", "ip3", 1.0, OP.mult))
+    later.append(lambda: ts("ia2", "ia", 3, OP.bitwise_and))
+    later.append(lambda: ts("ic2", "ic", 15, OP.bitwise_and))
+    later.append(lambda: ts("nxf", "nxa", 256.0, OP.mult, po=(0, 32)))
+    later.append(lambda: ts("mask", "ia2", 0.0, OP.is_equal, co=(0, 32), a=("mask",)))
+    later.append(lambda: trans("nxt", "nxf", (0, 32)))
+    later.append(lambda: ts("mask", "ic2", 0.0, OP.is_equal, co=(32, 64), a=("mask",)))
+    later.append(lambda: ts("r4", "ip15", 4.0, OP.mult))
+    later.append(lambda: ts("i82", "i8", 112, OP.bitwise_and))
+    later.append(lambda: ts("ku", "ik", T.r4[:, 0:1], OP.add, r=("r4",)))
+    later.append(lambda: ts("mask8", "i82", 0.0, OP.is_equal))
+    later.append(lambda: ts("cl1", "i82", -1.0, OP.mult, float(A + (N - 1) * CAP - 32768 * me), OP.add, ci=(0, 1)))
+    later.append(lambda: tt("cloc", "cl1", "r1", OP.add))
+
+    def table():
+        dma("y", [(T.nrow[0:1, :], T.nxt[0:32, 0:16])], r=("nxt",), w=("nrow",))
         run("g", lambda: g.partition_broadcast(T.tab[:], T.nrow[0:1, :], 128), r=("nrow",), w=("tab",))
-        quant("kn", 512, "kb", 0, 2048)
-        ts("ik2", "ik", 255, OP.bitwise_and)
-        ts("eF", "iF", 0.0, OP.is_equal, 0.5, OP.mult)
-        tt("ik3", "ik2", "ikb", OP.add)
-        cp("ku", "ik3")
-        pick("kj", 0, 512, "kn", 0, 512, "ku")
-        for b in range(4):
-            quant("e%d" % b, 128, "eF", 3 - b, 3 - b + 512)
-        for b in range(4):
-            mm("d%d" % b, "e%d" % b, "kj", 0, 512)
-            run("s", lambda: S.activation(T.kd[:, b:2048:4], T["d%d" % b][:, 0:512], CP), r=("d%d" % b,), a=("kd",))
-        ts("ia2", "ia", 3, OP.bitwise_and)
-        ts("ic2", "ic", 15, OP.bitwise_and)
-        ts("i82", "i8", 112, OP.bitwise_and)
-        ts("il2", "il", 112, OP.bitwise_and)
-        ts("mask", "ia2", 0.0, OP.is_equal, co=(0, 32), a=("mask",))
-        ts("mask", "ic2", 0.0, OP.is_equal, co=(32, 64), a=("mask",))
-        ts("mask8", "i82", 0.0, OP.is_equal)
-        ts("cl1", "il2", 128.0, OP.mult, float(128 * 32 - 65536 * me), OP.add)
-        tt("cloc", "cl1", "cl2", OP.add)
 
-    def steps():
-        fill("one", None, 1)
-        for t in range(1, R + 1):
-            nl = "nl%d" % t
-            for c, v in [((STEP, STEP + 64), 0), ((STEP, STEP + 1), (15 - me) * 65536), ((STEP + 32, STEP + 33), -65536)]:
-                run("v", lambda: V.memset(ap(nl, None, c), float(v)), r=(nl + "k",), a=(nl + "k",))
+    def unpack(b):
+        quant("e%d" % b, 128, "eF", 3 - b, 3 - b + 512)
+
+    def unpack_keys(parts):
+        for b in parts:
+            mm("d%d" % b, "e%d" % b, "kn", 0, 512)
+            run("s", lambda: S.activation(T.kd[:, b:2048:4], T["d%d" % b][:, 0:512], CP), r=("d%d" % b,), a=("kd",))
+
+    def steps(t):
+        nl = "nl%d" % t
+        for c, v in [((STEP, STEP + 64), 0), ((STEP, STEP + 1), (15 - me) * 32768), ((STEP + 32, STEP + 33), -32768)]:
+            run("v", lambda: V.memset(ap(nl, None, c), float(v)), r=(nl + "k",), a=(nl + "k",))
 
     def rows(t, q):
         n = "_%d" % t
@@ -310,22 +300,28 @@ def rank_program(g, core, T, topo):
         else:
             nl = "nl%d" % t
             run("v", lambda: V.tensor_tensor_scan(ap("bc" + n, q), ap("one", q), ap(nl, q, (5, STEP + 64)), 0.0, OP.mult, OP.add), r=("one", nl, nl + "k"), w=("bc" + n,))
+        gap()
         trans("bt" + n, "bc" + n, q, ci=(9, 73))
+        gap()
         for b in quad:
             cp("ri" + n, "bt" + n, po=b, pi=q, a=("ri" + n,))
 
     def route(t, q):
         n = "_%d" % t
         rows(t, q)
-        ts("be" + n, "ri" + n, 16, OP.logical_shift_right, 7, OP.bitwise_and)
-        ts("lo" + n, "ri" + n, 65535, OP.bitwise_and)
+        gap()
+        ts("be" + n, "ri" + n, 15, OP.logical_shift_right, 7, OP.bitwise_and)
+        ts("lo" + n, "ri" + n, 32767, OP.bitwise_and)
         ts("ind" + n, "be" + n, T.tb[:, 0:1], OP.is_equal, r=("tb",))
-        tt("pkr" + n, "lo" + n, "rowb", OP.add)
+        tt("pkr" + n, "lo" + n, "rowb" if t else "rowx", OP.add)
         scan("cum" + n, "rst32", "ind" + n)
         tt("ipk" + n, "ind" + n, "pkr" + n, OP.mult)
         ts("hit" + n, "cum" + n, T.r1[:, 0:1], OP.is_equal, r=("r1",))
+        gap()
         tt("hpk" + n, "hit" + n, "ipk" + n, OP.mult)
+        gap()
         scan("sp" + n, "rst32", "hpk" + n)
+        gap()
         for b in range(4):
             cp("q0" + n, "sp" + n, po=(0, 32), pi=quad[b], co=(2 * b, 2 * b + 2), ci=(31, 64, 32), a=("q0" + n,))
         for b in quad:
@@ -333,7 +329,7 @@ def rank_program(g, core, T, topo):
         vl, pk = T["vl%d" % t], T["pk%d" % t]
         send("apk%d" % t, lambda d: (vl[:, 3 + (me - d) % N:4 + (me - d) % N], pk[:, (d - me - 1) % N:(d - me - 1) % N + 1]), ("pk%d" % t,), NUMBERS)
         if t > 0:
-            ts("sr" + n, "pk%d" % t, 7, OP.logical_shift_right, 511, OP.bitwise_and)
+            ts("sr" + n, "pk%d" % t, 255, OP.bitwise_and)
             cp("su" + n, "sr" + n)
 
     def expect(t, land):
@@ -353,74 +349,86 @@ def rank_program(g, core, T, topo):
     def stand(t):
         n, q = "_%d" % t, mine
         cp("ui" + n, "bc" + n, po=q, ci=(8, 9))
-        ts("e1" + n, "ui" + n, 31, OP.bitwise_and, po=q)
-        ts("e2" + n, "ui" + n, 127, OP.bitwise_and, 5, OP.logical_shift_right, po=q)
-        ts("e3" + n, "ui" + n, 16, OP.logical_shift_right, po=q)
-        ts("e4" + n, "ui" + n, 127, OP.bitwise_and, po=q)
-        ts("f1" + n, "e1" + n, 4.0, OP.mult, po=q)
-        ts("f3" + n, "e3" + n, 128.0, OP.mult, po=q)
-        ts("f4" + n, "e3" + n, 65536.0, OP.mult, T.a128[q[0]:q[1], 0:1], OP.add, r=("a128",), po=q)
-        tt("f2" + n, "f1" + n, "e2" + n, OP.add, po=q)
+        ts("ni" + n, "ui" + n, 8, OP.logical_shift_right, po=q)
+        cp("n" + n, "ni" + n, po=q)
         if t < R:
-            run("v", lambda: V.tensor_tensor(ap("nl%d" % (t + 1), q, (KEPT, KEPT + 1)), ap("f4" + n, q), ap("e4" + n, q), OP.add), r=("f4" + n, "e4" + n), a=("nl%d" % (t + 1),))
-        tt("n" + n, "f2" + n, "f3" + n, OP.add, po=q)
+            ts("nl%d" % (t + 1), "ni" + n, 256.0, OP.mult, T.af[q[0]:q[1], 0:1], OP.add, r=("af",), po=q, co=(KEPT, KEPT + 1), a=("nl%d" % (t + 1),))
         dma("y", [(T.nd[t:t + 1, 0:A], ap("n" + n, q))], r=("n" + n,))
 
     def places(t):
         n = "_%d" % t
-        ts("lr" + n, "ri" + n, 7, OP.logical_shift_right, 511, OP.bitwise_and, ci=(0, 32))
+        ts("lr" + n, "ri" + n, 255, OP.bitwise_and, ci=(0, 32))
         tt("lm" + n, "lr" + n, "mask", OP.mult, cy=(32, 64))
         scan("lsc" + n, "rst", "lm" + n, c0=(32, 64))
         cp("lu" + n, "lsc" + n, ci=(15, 32, 16))
 
     def slots(t):
         n = "_%d" % t
+        if t == 0:
+            ts("sr_0", "vl0", 255, OP.bitwise_and, ci=(3, 11))
         tt("vp" + n, "vl%d" % t, "mask8", OP.mult, cx=(3, 11))
+        if t == 0:
+            cp("su_0", "sr_0", co=(me, N), ci=(0, N - me), a=("su_0",))
         total_of("pkf" + n, "vp" + n)
+        if t == 0 and me:
+            cp("su_0", "sr_0", co=(0, me), ci=(N - me, N), a=("su_0",))
         cp("pki" + n, "pkf" + n)
-        ts("wi" + n, "pki" + n, 127, OP.bitwise_and)
-        ts("ai" + n, "pki" + n, 16, OP.logical_shift_right)
-        cp("wf" + n, "wi" + n)
+        if t == 0:
+            pick("ld0", 0, 128, "la", 0, N * A, "su_0")
+        ts("vi" + n, "pki" + n, 32512, OP.bitwise_and)
+        ts("ai" + n, "pki" + n, 15, OP.logical_shift_right)
+        ts("vf" + n, "vi" + n, 1.0 / 256, OP.mult)
         cp("a1" + n, "ai" + n)
-        ts("m%d" % (t % 2), "iw", ap("wf" + n), OP.is_equal, r=("wf" + n,))
-        ts("c1" + n, "wf" + n, 1024.0, OP.add)
-        ts("oh" + n, "ja", ap("a1" + n), OP.is_equal, r=("a1" + n,), co=(0, 32), ci=(0, 32), a=("oh" + n,))
-        ts("q1" + n, "a1" + n, -128.0, OP.mult, T.cloc[:, 0:1], OP.add, r=("cloc",))
-        ts("i0" + n, "mask", ap("c1" + n), OP.mult, -1024.0, OP.add, r=("c1" + n,))
-        tt("dp" + n, "q1" + n, "wf" + n, OP.subtract)
-        ts("oh" + n, "oh" + n, ap("dp" + n), OP.mult, r=("dp" + n,), co=(32, 64), ci=(0, 32), a=("oh" + n,))
-        trans("oht" + n, "oh" + n)
+        ts("m%d" % (t % 2), "iw", ap("vf" + n), OP.is_equal, r=("vf" + n,))
+        later.append(lambda: ts("c1" + n, "vf" + n, 4.0, OP.mult, 1024.0, OP.add))
+        later.append(lambda: tt("q1" + n, "cloc", "a1" + n, OP.subtract))
+        later.append(lambda: ts("i0" + n, "mask", ap("c1" + n), OP.mult, -1024.0, OP.add, r=("c1" + n,)))
+        later.append(lambda: tt("dp" + n, "q1" + n, "vi" + n, OP.subtract))
+        later.append(lambda: ts("oh" + n, "ja", ap("a1" + n), OP.is_equal, r=("a1" + n,), co=(0, 32), ci=(0, 32), a=("oh" + n,)))
+        later.append(lambda: ts("oh" + n, "ja", ap("a1" + n), OP.is_equal, ap("dp" + n), OP.mult, r=("a1" + n, "dp" + n), co=(32, 64), ci=(0, 32), a=("oh" + n,)))
+        later.append(lambda: trans("oht" + n, "oh" + n))
+        while t and later:
+            gap()
 
     def hop(t):
         n, ld, qn, sn, dq, hb = "_%d" % t, "ld%d" % t, "qn%d" % t, "sn%d" % t, "dq%d" % t, "hb%d" % t
         nl, h = "nl%d" % (t + 1), "hq%d" % (t + 1)
         for j in range(4):
             mm("z%d" % j, ld, "kj", 128 * j, 128 * j + 128)
-        for b in range(4):
-            mm("d%d" % b, "e%d" % b, ld, 0, 128)
         for j in range(4):
             tt("p%d" % j + n, "z%d" % j, "m%d" % (t % 2), OP.mult, cx=(0, 128))
             if j < 3:
                 run("s", lambda: S.activation(ap("j%d" % j + n), ap("p%d" % j + n), CP, accum_out=ap("s4" + n, None, (3 - j, 4 - j))), r=("p%d" % j + n,), w=("j%d" % j + n,), a=("s4" + n,))
+        if t == 0:
+            unpack_keys(REST)
+        for b in range(4):
+            mm("d%d" % b, "e%d" % b, ld, 0, 128)
         for b in range(4):
             run("s", lambda: S.activation(T[dq][:, b:512:4], T["d%d" % b][:, 0:128], CP), r=("d%d" % b,), a=(dq,))
         run("v", lambda: V.tensor_reduce(ap("s4" + n, None, (0, 1)), ap("p3" + n), X, OP.add), r=("p3" + n,), a=("s4" + n,))
+        gap()
         run("v", lambda: V.tensor_reduce(ap("mx" + n), ap("s4" + n), X, OP.max), r=("s4" + n,), w=("mx" + n,))
+        gap()
         ts("ne" + n, "s4" + n, ap("mx" + n), OP.not_equal, 1000000.0, OP.mult, r=("mx" + n,))
-        run("v", lambda: V.tensor_tensor_scan(ap("js" + n), T.c128[:], ap("ne" + n), 0.0, OP.add, OP.min), r=("c128", "ne" + n), w=("js" + n,))
+        gap()
+        run("v", lambda: V.tensor_tensor_scan(ap("js" + n), T.c1s[:], ap("ne" + n), 0.0, OP.add, OP.min), r=("c1s", "ne" + n), w=("js" + n,))
+        gap()
         ts("d0" + n, "i0" + n, ap("js" + n, None, (3, 4)), OP.add, 0.0, OP.max, r=("js" + n,))
+        gap()
         trans("dt" + n, "d0" + n)
+        gap()
         scan("ds" + n, "rst", "dt" + n)
+        gap()
 
         def join(b):
             cp("lf" + n, "ds" + n, po=(0, 32), pi=quad[b], co=(8 * b, 8 * b + 8), ci=(3, 32, 4), a=("lf" + n,))
         cp("l2u" + n, "ds" + n, ci=(47, 64, 16))
         join(0)
-        run("v", lambda: V.tensor_copy(ap("gt" + n), T.tab[:, 0:512].indirect(ap("l2u" + n))), r=("tab", "l2u" + n), w=("gt" + n,))
+        run("v", lambda: V.tensor_tensor(ap("n1" + n), T.tab[:, 0:512].indirect(ap("l2u" + n)), ap("oht" + n, None, (0, 32)), OP.mult), r=("tab", "l2u" + n, "oht" + n), w=("n1" + n,))
         join(1)
-        tt("n1" + n, "gt" + n, "oht" + n, OP.mult, cy=(0, 32))
-        tt("n2" + n, "n1" + n, "oht" + n, OP.add, cy=(32, 64))
-        scan(sn, "rst", "n2" + n, c0=(32, 64))
+        for i in range(2):
+            lo, hi = CAP * i, CAP * i + CAP
+            run("v", lambda: V.tensor_tensor_scan(T[sn][:, lo:hi], ap("oht" + n, None, (32 + lo, 32 + hi)), ap("n1" + n, None, (lo, hi)), 0.0, OP.add, OP.add), r=("n1" + n, "oht" + n), a=(sn,))
         beta = lambda s: (me - s - 1) % N
         send("adl%d" % t, lambda s: (T[nl][:, 5 + beta(s):6 + beta(s)], T[sn][:, 15 + 16 * (s % 2):16 + 16 * (s % 2)]), (sn,), NUMBERS)
         arrive("adl%d" % t, per(NUMBERS), (nl,))
@@ -438,42 +446,32 @@ def rank_program(g, core, T, topo):
         cp(nl, sn, po=mine, co=(OWN, OWN + 1), ci=(15 + 16 * half, 16 + 16 * half), a=(nl,))
 
     q = quad[0]
-    quant("hq0", 128, "xb", 0, 512)
     send("aco0", lambda d: (codes("la", A * me, A * me + A), codes("hq0", 0, A)), ("hq0c",), CODES)
-    iota("ik", [[1, 4], [4, 4], [0, 2]], 0, 16)
-    iota("ikb", [[0, 16], [256, 2]], 0, 0)
-    iota("ia", [[1, 8], [0, 4]], 256, -1)
-    iota("ic", [[1, 32]], 256, -1)
-    iota("i8", [[-16, 8]], 256 - 16 * me, 1)
-    iota("il", [[1, 1]], 16 * (me + 7) + 15, -1)
-    ts("g1", "stt", 3, OP.bitwise_and, po=q)
-    ts("g2", "stt", 127, OP.bitwise_and, 2, OP.logical_shift_right, po=q)
-    ts("g3", "stt", 7, OP.logical_shift_right, po=q)
-    ts("h1", "g1", 32.0, OP.mult, po=q)
-    ts("h3", "g3", 65536.0, OP.mult, T.a128[q[0]:q[1], 0:1], OP.add, r=("a128",), po=q)
-    tt("h2", "h1", "g2", OP.add, po=q)
-    tt("h4", "h2", "h3", OP.add, po=q)
-    tt("h5", "h4", "mask2", OP.mult, po=q)
-    total_of("u_0", "h5", po=q)
+    ts("u_0", "stt", 256.0, OP.mult, T.af[q[0]:q[1], 0:1], OP.add, r=("af",), po=q, ci=(1, 2))
     route(0, q)
     send("aco0", lambda d: (plane("la", A * me, A * me + A), plane("hq0", 0, A)), ("hq0s",), SCALES)
     both("la", A * me, A * me + A, "hq0", 0, A)
     expect(0, "la")
-    cp("nl1", "u_0", po=mine, pi=q, co=(KEPT, KEPT + 1), a=("nl1",))
-    constants()
-    ts("sr_0", "vl0", 7, OP.logical_shift_right, 511, OP.bitwise_and, ci=(3, 11))
-    tt("sx_0", "sr_0", "i32", OP.add, co=(me, N), cx=(0, N - me), cy=(me, N), a=("sx_0",))
-    if me:
-        tt("sx_0", "sr_0", "i32", OP.add, co=(0, me), cx=(N - me, N), cy=(0, me), a=("sx_0",))
-    cp("su_0", "sx_0")
+    unpack(0)
+    quant("kn", 512, "kb", 0, 2048)
+    unpack_keys((0,))
+    while later:
+        gap()
+    pick("kj", 0, 512, "kn", 0, 512, "ku")
+    table()
+    for b in range(1, 4):
+        unpack(b)
+    unpack_keys(FIRST)
+    fill("c1s", None, 1)
+    fill("rst", None, 1)
+    fill("rst", (0, 32, 4), 0)
+    fill("rst", (32, 64, 16), 0)
+    steps(1)
+    fill("one", None, 1)
+    ts("rowb", "ja", 32768.0, OP.mult)
     slots(0)
-    pick("ld0", 0, 128, "la", 0, N * A, "su_0")
     hop(0)
-    steps()
-    tt("stm", "stt", "mask2", OP.mult, po=q)
-    total_of("n_0", "stm", po=q)
-    dma("y", [(T.nd[0:1, 0:A], ap("n_0", q))], r=("n_0",))
-    quant("wq", 128, "wb", 0, 512)
+    cp("nl1", "u_0", po=mine, pi=q, co=(KEPT, KEPT + 1), a=("nl1",))
     both("fin", A, 128, "hq0", A, 128)
     both("hq1", 0, A, "hq0", 0, A)
     for t in range(1, R + 1):
@@ -483,6 +481,11 @@ def rank_program(g, core, T, topo):
             stand(t)
             places(t)
             pick("hq%d" % (t + 1), 0, A, "hq%d" % t, 0, HOME, "lu_%d" % t)
+            steps(t + 1)
+            if t == 1:
+                cp("n_0", "stt", po=q, ci=(1, 2))
+                dma("y", [(T.nd[0:1, 0:A], ap("n_0", q))], r=("n_0",))
+                quant("wq", 128, "wb", 0, 512)
             slots(t)
             hop(t)
         else:

@@ -5,6 +5,15 @@ R, A, P, CAP, N = 3, 32, 512, 16, 8
 HOME = A + N * CAP
 FIRST, REST = (1, 2), (3,)
 OWN, KEPT, STEP = 12, 13, 14
+RANK = 32768
+TURN, GATE = 2 ** 18, 2 ** 24
+FLOOR = 2.0 ** -17 - 0.5
+HELPERS = 2
+XKEEP = 4
+KEEP = 1
+HALF = N * CAP // HELPERS
+HAND = 4
+LEGS = ["x", "b0", "f1", "b1", "f2", "b2"]
 
 SCRATCH = {}
 
@@ -17,9 +26,9 @@ _F, _I, _U, _B, _Q, _S = "float32", "int32", "uint16", "bfloat16", "float8_e4m3f
 for _n, _c, _t in [
     ("eF", 516, _B), ("iw", 128, _B), ("ia", 32, _I), ("ia2", 32, _I), ("ic", 32, _I), ("ic2", 32, _I), ("mask", 64, _F),
     ("ip", 1, _I), ("ip15", 1, _I), ("ip5", 1, _I), ("ip31", 1, _I), ("ip3", 1, _I), ("ipf", 1, _F),
-    ("r1", 1, _F), ("tb", 1, _F), ("af", 1, _F), ("t4", 1, _F), ("cl1", 1, _F), ("r4", 1, _F),
+    ("r1", 1, _F), ("k0", 1, _F), ("tb", 1, _F), ("af", 1, _F), ("t4", 1, _F), ("cl1", 1, _F), ("r4", 1, _F),
     ("cloc", 1, _F), ("i8", 8, _I), ("i82", 8, _I), ("mask8", 8, _F), ("ja", 64, _F), ("rowb", 64, _F), ("rowx", 64, _F), ("ct", 64, _F),
-    ("rst32", 64, _F), ("rst", 64, _F), ("one", 73, _F), ("c1s", 4, _F), ("ik", 32, _I),
+    ("rst", 64, _F), ("one", 73, _F), ("c1s", 4, _F), ("ik", 32, _I),
     ("ku", 32, _U), ("stt", 3, _I), ("nxa", 32, _I), ("nxf", 32, _F), ("nxt", 32, _F),
     ("nrow", 512, _F), ("tab", 512, _F), ("xb", 512, _B), ("kb", 2048, _B), ("wb", 512, _B), ("yb", 32, _F), ("m0", 128, _B), ("m1", 128, _B),
     ("kd", 2048, _F),
@@ -41,6 +50,9 @@ for _t in range(R):
     _sb("nl%d" % (_t + 1), 80, _F)
     _sb("dq%d" % _t, 512, _F)
     _sb("hb%d" % _t, 512, _B)
+_sb("hxc", A, _Q)
+for _l in LEGS:
+    _sb("h%ss" % _l, A if _l == "x" else HALF, _S)
 SMALL, WIDE = {}, {"f": ["smf", 0], "i": ["smi", 0], "u": ["smu", 0]}
 
 
@@ -51,13 +63,13 @@ def _small(ty, name, cols):
 
 
 for _t in range(R + 1):
-    for _n, _c in [("u", 1), ("bc", 73), ("bt", 64), ("ind", 64), ("cum", 64), ("hit", 64), ("pkr", 64), ("ipk", 64), ("hpk", 64), ("sp", 64),
+    for _n, _c in [("u", 1), ("bc", 73), ("bt", 64), ("pkq", 64), ("ind", 64), ("cum", 64), ("pkr", 64), ("sp", 64),
                    ("q0", 8), ("n", 1), ("lm", 32), ("lsc", 32), ("vp", 8), ("pkf", 1), ("vf", 1), ("a1", 1),
                    ("c1", 1), ("i0", 64), ("oh", 64), ("oht", 64), ("q1", 1), ("dp", 1), ("p0", 128), ("p1", 128), ("p2", 128), ("p3", 128),
                    ("s4", 4), ("mx", 1), ("ne", 4), ("js", 4), ("d0", 64), ("dt", 64), ("ds", 64), ("lf", 32),
                    ("n1", 32), ("j0", 128), ("j1", 128), ("j2", 128)]:
         _small("f", "%s_%d" % (_n, _t), _c)
-    for _n, _c in [("ri", 64), ("be", 64), ("lo", 64), ("sr", 8), ("ui", 1), ("ni", 1), ("lr", 32), ("pki", 1), ("vi", 1), ("ai", 1)]:
+    for _n, _c in [("li", 32), ("be", 64), ("sr", 8), ("ui", 1), ("ni", 1), ("lr", 32), ("pki", 1), ("vi", 1), ("ai", 1)]:
         _small("i", "%s_%d" % (_n, _t), _c)
     for _n, _c in [("su", 8), ("lu", 2), ("ko", 32), ("l2u", 2)]:
         _small("u", "%s_%d" % (_n, _t), _c)
@@ -68,14 +80,97 @@ for _b in range(4):
     SCRATCH["z%d" % _b] = ("psum", [128, 512], "float32")
     SCRATCH["d%d" % _b] = ("psum", [128, 512], "float32")
 
-SEMAPHORES = ["qv", "qs", "qt", "qg", "ls"] + ["m%d" % _k for _k in range(40)]
+SEMAPHORES = ["qv", "qs", "qt", "qg", "ls"] + ["m%d" % _k for _k in range(40)] + ["h" + _l for _l in LEGS]
 for _t in range(R):
     SEMAPHORES += ["apk%d" % _t, "aco%d" % _t, "adl%d" % _t, "are%d" % _t]
+
+
+def helpers_of(core, T, topo):
+    can = [c for c in topo.cores_of(core) if T.rank_of(c) is None and all(topo.may_write(c, r) for r in T.cores)]
+    return sorted(can, key=lambda c: topo.die(c) == topo.die(core))[:HELPERS]
+
+
+def lanes(n, width=8):
+    calls = []
+    while n:
+        k = 1
+        while 2 * k <= min(n, width):
+            k *= 2
+        w = width // k
+        calls.append([tuple(range(w * i, w * i + w)) for i in range(k)])
+        n -= k
+    return calls
+
+
+def parts(leg, s):
+    out = {"c": [], "s": []}
+    if leg == "x":
+        to = [((s + 1 + b) % N, 0) for b in range(N - 1)]
+        cut = XKEEP + (N - XKEEP) // 2
+        out["c"] = [(None, to[:XKEEP], lanes(XKEEP)), (0, to[XKEEP:cut], lanes(cut - XKEEP)), (1, to[cut:], lanes(N - 1 - cut))]
+        m = (N - 1) // 2
+        out["s"] = [(0, to[:m], lanes(m)), (1, to[m:], lanes(N - 1 - m))]
+        return out
+    to = [((s + i) % N, (s + i) % N) for i in range(1, N)]
+    out["c"].append((None, to, [[(i,) for i in range(6)] + [(6, 7)]]))
+    by = [[e for e in to if e[1] * HELPERS // N == h] for h in range(HELPERS)]
+    own = max(by, key=len)[-KEEP:]
+    out["s"].append((None, own, [[(6, 7)]]))
+    for h in range(HELPERS):
+        l = [e for e in by[h] if e not in own]
+        out["s"].append((h, l, lanes(len(l))))
+    return out
+
+
+def landing(leg, s, d):
+    if leg == "x":
+        return "la", A * s, A
+    if leg[0] == "f":
+        return "ld" + leg[1], CAP * s, CAP
+    return "hq%d" % (int(leg[1]) + 1), A + CAP * ((s - d - 1) % N), CAP
+
+
+def sem_of(leg):
+    return "aco0" if leg == "x" else {"f": "aco", "b": "are"}[leg[0]] + leg[1]
+
+
+def issue(g, core, T, topo, leg, s, what, src, first, entries, calls, total):
+    todo = list(entries)
+    for call in calls:
+        tr = []
+        for at in call:
+            d, b = todo.pop(0)
+            dst = T.cores[d]
+            rid, pid, _ = topo.addr(dst)
+            es = topo.engines(core, dst)
+            name, lo, n = landing(leg, s, d)
+            c = CAP * (b - first)
+            o, i = T[name + what][:, lo:lo + n], T[src][:, c:c + n]
+            if what == "c":
+                o, i = o.bitcast(dt.uint8), i.bitcast(dt.uint8)
+            tr.append(RemoteDMATransfer(dst_ids=[DstId(rid=rid, pnc=pid)], dma_engine_mask=sum(1 << es[k] for k in at), remote_sem=T.sem[sem_of(leg)], src=i, dst=o))
+            total["ls"] = total.get("ls", 0) + len(at)
+        g.remote_dma_fused(tr, local_sem=T.sem["ls"])
+
+
+def helper_program(g, core, T, topo):
+    rank = [c for c in topo.cores_of(core) if T.rank_of(c) is not None]
+    if not rank or core not in helpers_of(rank[0], T, topo):
+        return
+    me, s, total = helpers_of(rank[0], T, topo).index(core), T.rank_of(rank[0]), {}
+    for leg in LEGS:
+        g.wait_ge(T.sem["h" + leg], HAND * (2 if leg == "x" else 1))
+        for what, l in parts(leg, s).items():
+            for h, entries, calls in l:
+                if h == me:
+                    issue(g, core, T, topo, leg, s, what, "h" + leg + what, 0 if leg == "x" else N // HELPERS * me, entries, calls, total)
+    g.wait_ge(T.sem["ls"], total["ls"])
 
 
 def rank_program(g, core, T, topo):
     me = T.rank_of(core)
     if me is None:
+        helper_program(g, core, T, topo)
         return
     OP, X, CP = AluOpType, AxisListType.X, ActivationFunctionType.Copy
     V, S, TE, Y = g.vector, g.scalar, g.tensor, g.sync
@@ -130,9 +225,8 @@ def rank_program(g, core, T, topo):
         done(q, sem, total[sem], r, w, a)
 
     others = [(me + i) % N for i in range(1, N)]
+    helpers = helpers_of(core, T, topo)
     NUMBERS = [[(i,) for i in range(6)] + [(6, 7)]]
-    CODES = [[(0, 1), (2, 3), (4, 5), (6, 7)], [(0, 1), (2, 3), (4, 5, 6, 7)]]
-    SCALES = [[(0, 1), (2, 3), (4, 5), (6, 7)], [(4, 5), (6, 7), (0, 1, 2, 3)]]
     per = lambda plan: sum(len(l) for c in plan for l in c)
 
     def send(sem, part, r, plan):
@@ -140,15 +234,48 @@ def rank_program(g, core, T, topo):
         todo = list(others)
         for call in plan:
             tr = []
-            for lanes in call:
+            for at in call:
                 d = todo.pop(0)
                 dst = T.cores[d]
                 rid, pid, _ = topo.addr(dst)
                 es = topo.engines(core, dst)
                 o, s = part(d)
-                tr.append(RemoteDMATransfer(dst_ids=[DstId(rid=rid, pnc=pid)], dma_engine_mask=sum(1 << es[k] for k in lanes), remote_sem=T.sem[sem], src=s, dst=o))
-                total["ls"] = total.get("ls", 0) + len(lanes)
+                tr.append(RemoteDMATransfer(dst_ids=[DstId(rid=rid, pnc=pid)], dma_engine_mask=sum(1 << es[k] for k in at), remote_sem=T.sem[sem], src=s, dst=o))
+                total["ls"] = total.get("ls", 0) + len(at)
             g.remote_dma_fused(tr, local_sem=T.sem["ls"])
+
+    def hand(leg, what, src):
+        before("g", (src + what,), ())
+        free = [k for k in topo.engines(core, helpers[0]) if k not in topo.engines(core, T.cores[others[0]])]
+        tr = []
+        for h, c in enumerate(helpers):
+            rid, pid, _ = topo.addr(c)
+            n, lo = (A, 0) if leg == "x" else (HALF, HALF * h)
+            o, i = T["h" + leg + what][:, 0:n], T[src + what][:, lo:lo + n]
+            if what == "c":
+                o, i = o.bitcast(dt.uint8), i.bitcast(dt.uint8)
+            tr.append(RemoteDMATransfer(dst_ids=[DstId(rid=rid, pnc=pid)], dma_engine_mask=sum(1 << k for k in free[HAND * h:HAND * h + HAND]), remote_sem=T.sem["h" + leg], src=i, dst=o))
+            total["ls"] = total.get("ls", 0) + HAND
+        g.remote_dma_fused(tr, local_sem=T.sem["ls"])
+
+    def direct(leg, what, src):
+        before("g", (src + what,), ())
+        for h, entries, calls in parts(leg, me)[what]:
+            if h is None:
+                issue(g, core, T, topo, leg, me, what, src + what, 0, entries, calls, total)
+
+    def coming(leg):
+        n = 0
+        for s in others:
+            for l in parts(leg, s).values():
+                for h, entries, calls in l:
+                    n += sum(len(at) for (d, b), at in zip(entries, [at for call in calls for at in call]) if d == me)
+        return n
+
+    def leave(leg, src):
+        hand(leg, "s", src)
+        direct(leg, "c", src)
+        direct(leg, "s", src)
 
     def arrive(sem, n, keys):
         total[sem] = n
@@ -239,29 +366,29 @@ def rank_program(g, core, T, topo):
 
     run("v", lambda: V.memset(T.xb[:, 4 * A:512], 0.0), a=("xb",))
     iota("ip", [[1, 1]], 0, 1)
-    iota("ja", [[0, 2], [1, A]], 1, 0)
+    iota("ja", [[0, 2], [-1, A]], A, 0)
     iota("iw", [[1, 128]], 0, 0)
     iota("i8", [[-16, 8]], 256 - 16 * me, 1)
     iota("ik", [[1, 4], [64, 8]], 0, 0)
     iota("ia", [[1, 8], [0, 4]], 256, -1)
     iota("ic", [[1, 32]], 256, -1)
-    fill("ct", (0, 32), (15 - me) * 32768)
-    fill("ct", (32, 64), (14 - me) * 32768, a=("ct",))
+    fill("ct", (0, 32), 0)
+    fill("ct", (32, 64), -RANK, a=("ct",))
     ts("ip31", "ip", 31, OP.bitwise_and)
     ts("ip15", "ip", 15, OP.bitwise_and)
     ts("ip5", "ip", 5, OP.logical_shift_right)
     cp("af", "ip31")
-    ts("r1", "ip15", 1.0, OP.add)
+    ts("k0", "ip15", float(-GATE), OP.mult)
     ts("tb", "ip5", 2.0, OP.mult)
-    ts("rowx", "ja", 32768.0, OP.mult, float(A * me), OP.add)
+    ts("rowx", "ja", float(TURN), OP.mult, float(A * me), OP.add)
+    fill("one", None, 1)
     quant("hq0", 128, "xb", 0, 512)
 
-    later.append(lambda: fill("rst32", None, 1))
-    later.append(lambda: fill("rst32", (0, 64, 32), 0))
     later.append(lambda: fill("eF", None, 0))
     later.append(lambda: cp("ipf", "ip"))
     later.append(lambda: ts("ip3", "ip", 3, OP.bitwise_and))
     later.append(lambda: run("v", lambda: V.tensor_scalar(T.eF[:, 3:515:4], T.iw[:], T.ipf[:, 0:1], 0.5, OP.is_equal, OP.mult), r=("iw", "ipf"), w=("eF",)))
+    tiles = len(later)
     later.append(lambda: ts("t4", "ip3", 1.0, OP.mult))
     later.append(lambda: ts("ia2", "ia", 3, OP.bitwise_and))
     later.append(lambda: ts("ic2", "ic", 15, OP.bitwise_and))
@@ -273,8 +400,10 @@ def rank_program(g, core, T, topo):
     later.append(lambda: ts("i82", "i8", 112, OP.bitwise_and))
     later.append(lambda: ts("ku", "ik", T.r4[:, 0:1], OP.add, r=("r4",)))
     later.append(lambda: ts("mask8", "i82", 0.0, OP.is_equal))
-    later.append(lambda: ts("cl1", "i82", -1.0, OP.mult, float(A + (N - 1) * CAP - 32768 * me), OP.add, ci=(0, 1)))
+    later.append(lambda: ts("cl1", "i82", -1.0, OP.mult, float(A + (N - 1) * CAP - RANK * me - A - 1), OP.add, ci=(0, 1)))
+    later.append(lambda: ts("r1", "ip15", 1.0, OP.add))
     later.append(lambda: tt("cloc", "cl1", "r1", OP.add))
+    tiles = len(later) - tiles
 
     def table():
         dma("y", [(T.nrow[0:1, :], T.nxt[0:32, 0:16])], r=("nxt",), w=("nrow",))
@@ -290,7 +419,7 @@ def rank_program(g, core, T, topo):
 
     def steps(t):
         nl = "nl%d" % t
-        for c, v in [((STEP, STEP + 64), 0), ((STEP, STEP + 1), (15 - me) * 32768), ((STEP + 32, STEP + 33), -32768)]:
+        for c, v in [((STEP, STEP + 64), 0), ((STEP + 32, STEP + 33), -RANK)]:
             run("v", lambda: V.memset(ap(nl, None, c), float(v)), r=(nl + "k",), a=(nl + "k",))
 
     def rows(t, q):
@@ -303,47 +432,47 @@ def rank_program(g, core, T, topo):
         gap()
         trans("bt" + n, "bc" + n, q, ci=(9, 73))
         gap()
-        for b in quad:
-            cp("ri" + n, "bt" + n, po=b, pi=q, a=("ri" + n,))
 
     def route(t, q):
         n = "_%d" % t
         rows(t, q)
+        for b in quad:
+            ts("be" + n, "bt" + n, 1.0 / RANK, OP.mult, FLOOR, OP.add, po=b, pi=q, a=("be" + n,))
+        tt("pkq" + n, "bt" + n, "rowb" if t else "rowx", OP.add, po=q)
         gap()
-        ts("be" + n, "ri" + n, 15, OP.logical_shift_right, 7, OP.bitwise_and)
-        ts("lo" + n, "ri" + n, 32767, OP.bitwise_and)
-        ts("ind" + n, "be" + n, T.tb[:, 0:1], OP.is_equal, r=("tb",))
-        tt("pkr" + n, "lo" + n, "rowb" if t else "rowx", OP.add)
-        scan("cum" + n, "rst32", "ind" + n)
-        tt("ipk" + n, "ind" + n, "pkr" + n, OP.mult)
-        ts("hit" + n, "cum" + n, T.r1[:, 0:1], OP.is_equal, r=("r1",))
+        ts("ind" + n, "be" + n, T.tb[:, 0:1], OP.is_equal, float(GATE), OP.mult, r=("tb",))
+        for b in quad:
+            cp("pkr" + n, "pkq" + n, po=b, pi=q, a=("pkr" + n,))
+        two = [(0, A), (A, 2 * A)]
+        for c in two:
+            run("v", lambda: V.tensor_tensor_scan(ap("cum" + n, None, c), ap("one", None, (0, A)), ap("ind" + n, None, c), T.k0[:, 0:1], OP.mult, OP.add),
+                r=("one", "ind" + n, "k0"), a=("cum" + n,))
         gap()
-        tt("hpk" + n, "hit" + n, "ipk" + n, OP.mult)
-        gap()
-        scan("sp" + n, "rst32", "hpk" + n)
+        for c in two:
+            run("v", lambda: V.tensor_tensor_scan(ap("sp" + n, None, c), ap("pkr" + n, None, c), ap("cum" + n, None, c), 0.0, OP.max, OP.min),
+                r=("pkr" + n, "cum" + n), a=("sp" + n,))
         gap()
         for b in range(4):
-            cp("q0" + n, "sp" + n, po=(0, 32), pi=quad[b], co=(2 * b, 2 * b + 2), ci=(31, 64, 32), a=("q0" + n,))
+            ts("q0" + n, "sp" + n, 0.0, OP.max, po=(0, 32), pi=quad[b], co=(2 * b, 2 * b + 2), ci=(31, 64, 32), a=("q0" + n,))
+        gap()
         for b in quad:
             cp("pk%d" % t, "q0" + n, po=b, pi=(0, 32), a=("pk%d" % t,))
         vl, pk = T["vl%d" % t], T["pk%d" % t]
-        send("apk%d" % t, lambda d: (vl[:, 3 + (me - d) % N:4 + (me - d) % N], pk[:, (d - me - 1) % N:(d - me - 1) % N + 1]), ("pk%d" % t,), NUMBERS)
+        send("apk%d" % t, lambda d: (vl[:, 3 + (me - d) % N:4 + (me - d) % N], pk[:, d:d + 1]), ("pk%d" % t,), NUMBERS)
         if t > 0:
             ts("sr" + n, "pk%d" % t, 255, OP.bitwise_and)
             cp("su" + n, "sr" + n)
 
     def expect(t, land):
-        cp("vl%d" % t, "pk%d" % t, co=(3, 4), ci=(7, 8), a=("vl%d" % t,))
+        cp("vl%d" % t, "pk%d" % t, co=(3, 4), ci=(me, me + 1), a=("vl%d" % t,))
         arrive("apk%d" % t, per(NUMBERS), ("vl%d" % t,))
-        arrive("aco%d" % t, per(CODES) + per(SCALES), (land + "c", land + "s"))
+        arrive("aco%d" % t, coming("f%d" % t if t else "x"), (land + "c", land + "s"))
 
     def depart(t):
-        ld, sd, sem = "ld%d" % t, "sd%d" % t, "aco%d" % t
+        ld, sd = "ld%d" % t, "sd%d" % t
         pick(sd, 0, 128, "hq%d" % t, 0, HOME, "su_%d" % t)
-        at = lambda d: CAP * ((d - me - 1) % N)
-        send(sem, lambda d: (codes(ld, CAP * me, CAP * me + CAP), codes(sd, at(d), at(d) + CAP)), (sd + "c",), CODES)
-        send(sem, lambda d: (plane(ld, CAP * me, CAP * me + CAP), plane(sd, at(d), at(d) + CAP)), (sd + "s",), SCALES)
-        both(ld, CAP * me, CAP * me + CAP, sd, 112, 128)
+        leave("f%d" % t, sd)
+        both(ld, CAP * me, CAP * me + CAP, sd, CAP * me, CAP * me + CAP)
         expect(t, ld)
 
     def stand(t):
@@ -357,7 +486,9 @@ def rank_program(g, core, T, topo):
 
     def places(t):
         n = "_%d" % t
-        ts("lr" + n, "ri" + n, 255, OP.bitwise_and, ci=(0, 32))
+        for b in quad:
+            cp("li" + n, "bt" + n, po=b, pi=mine, ci=(0, A), a=("li" + n,))
+        ts("lr" + n, "li" + n, 255, OP.bitwise_and)
         tt("lm" + n, "lr" + n, "mask", OP.mult, cy=(32, 64))
         scan("lsc" + n, "rst", "lm" + n, c0=(32, 64))
         cp("lu" + n, "lsc" + n, ci=(15, 32, 16))
@@ -376,12 +507,12 @@ def rank_program(g, core, T, topo):
         if t == 0:
             pick("ld0", 0, 128, "la", 0, N * A, "su_0")
         ts("vi" + n, "pki" + n, 32512, OP.bitwise_and)
-        ts("ai" + n, "pki" + n, 15, OP.logical_shift_right)
+        ts("ai" + n, "pki" + n, 18, OP.logical_shift_right)
         ts("vf" + n, "vi" + n, 1.0 / 256, OP.mult)
         cp("a1" + n, "ai" + n)
         ts("m%d" % (t % 2), "iw", ap("vf" + n), OP.is_equal, r=("vf" + n,))
         later.append(lambda: ts("c1" + n, "vf" + n, 4.0, OP.mult, 1024.0, OP.add))
-        later.append(lambda: tt("q1" + n, "cloc", "a1" + n, OP.subtract))
+        later.append(lambda: tt("q1" + n, "cloc", "a1" + n, OP.add))
         later.append(lambda: ts("i0" + n, "mask", ap("c1" + n), OP.mult, -1024.0, OP.add, r=("c1" + n,)))
         later.append(lambda: tt("dp" + n, "q1" + n, "vi" + n, OP.subtract))
         later.append(lambda: ts("oh" + n, "ja", ap("a1" + n), OP.is_equal, r=("a1" + n,), co=(0, 32), ci=(0, 32), a=("oh" + n,)))
@@ -438,20 +569,21 @@ def rank_program(g, core, T, topo):
             ts("ko" + n, "lf" + n, 4.0, OP.mult, T.t4[0:32, 0:1], OP.add, r=("t4",), po=b, pi=(0, 32), a=("ko" + n,))
         run("v", lambda: V.tensor_tensor(T[hb][:], T.kd[:, 0:2048].indirect(ap("ko" + n)), T[dq][:], OP.add), r=("kd", "ko" + n, dq), w=(hb,))
         quant(qn, 128, hb, 0, 512)
-        sem = "are%d" % t
-        send(sem, lambda s: (codes(h, A + CAP * beta(s), A + CAP * beta(s) + CAP), codes(qn, CAP * s, CAP * s + CAP)), (qn + "c",), CODES)
-        send(sem, lambda s: (plane(h, A + CAP * beta(s), A + CAP * beta(s) + CAP), plane(qn, CAP * s, CAP * s + CAP)), (qn + "s",), SCALES)
+        leave("b%d" % t, qn)
         both(h, A + 112, HOME, qn, CAP * me, CAP * me + CAP)
-        arrive(sem, per(CODES) + per(SCALES), (h + "c", h + "s"))
+        arrive("are%d" % t, coming("b%d" % t), (h + "c", h + "s"))
         cp(nl, sn, po=mine, co=(OWN, OWN + 1), ci=(15 + 16 * half, 16 + 16 * half), a=(nl,))
 
     q = quad[0]
-    send("aco0", lambda d: (codes("la", A * me, A * me + A), codes("hq0", 0, A)), ("hq0c",), CODES)
+    hand("x", "c", "hq0")
+    hand("x", "s", "hq0")
+    direct("x", "c", "hq0")
     ts("u_0", "stt", 256.0, OP.mult, T.af[q[0]:q[1], 0:1], OP.add, r=("af",), po=q, ci=(1, 2))
     route(0, q)
-    send("aco0", lambda d: (plane("la", A * me, A * me + A), plane("hq0", 0, A)), ("hq0s",), SCALES)
     both("la", A * me, A * me + A, "hq0", 0, A)
     expect(0, "la")
+    while len(later) > tiles:
+        gap()
     unpack(0)
     quant("kn", 512, "kb", 0, 2048)
     unpack_keys((0,))
@@ -467,8 +599,7 @@ def rank_program(g, core, T, topo):
     fill("rst", (0, 32, 4), 0)
     fill("rst", (32, 64, 16), 0)
     steps(1)
-    fill("one", None, 1)
-    ts("rowb", "ja", 32768.0, OP.mult)
+    ts("rowb", "ja", float(TURN), OP.mult)
     slots(0)
     hop(0)
     cp("nl1", "u_0", po=mine, pi=q, co=(KEPT, KEPT + 1), a=("nl1",))

from concourse.bass import DstId, RemoteDMATransfer
from concourse.mybir import dt, AluOpType, AxisListType, ActivationFunctionType

R, A, P, CAP, N = 3, 32, 512, 16, 8
HOME = A + N * CAP
FIRST, REST = (1, 2), (3,)
OWN, KEPT, STEP = 12, 13, 14
RANK = 32768
TURN, GATE = 2 ** 18, 2 ** 24
FLOOR = 2.0 ** -17 - 0.5
HELPERS = 2
XKEEP = 4
KEEP = 1
HALF = N * CAP // HELPERS
HAND = 4
LEGS = ["x", "b0", "f1", "b1", "f2", "b2"]

SCRATCH = {}


def _sb(name, cols, ty):
    SCRATCH[name] = ("sbuf", [128, cols], ty)


_F, _I, _U, _B, _Q, _S = "float32", "int32", "uint16", "bfloat16", "float8_e4m3fn_x4", "uint8"
for _n, _c, _t in [
    ("eF", 516, _B), ("iw", 128, _B), ("ia", 32, _I), ("ia2", 32, _I), ("ic", 32, _I), ("ic2", 32, _I), ("mask", 64, _F),
    ("ip", 1, _I), ("ip15", 1, _I), ("ip5", 1, _I), ("ip31", 1, _I), ("ip3", 1, _I), ("ipf", 1, _F),
    ("r1", 1, _F), ("k0", 1, _F), ("tb", 1, _F), ("af", 1, _F), ("t4", 1, _F), ("cl1", 1, _F), ("r4", 1, _F),
    ("cloc", 1, _F), ("i8", 8, _I), ("i82", 8, _I), ("mask8", 8, _F), ("ja", 64, _F), ("rowb", 64, _F), ("rowx", 64, _F), ("ct", 64, _F),
    ("rst", 64, _F), ("one", 73, _F), ("c1s", 4, _F), ("ik", 32, _I),
    ("ku", 32, _U), ("stt", 3, _I), ("nxa", 32, _I), ("nxf", 32, _F), ("nxt", 32, _F),
    ("nrow", 512, _F), ("tab", 512, _F), ("xb", 512, _B), ("kb", 2048, _B), ("wb", 512, _B), ("yb", 32, _F), ("m0", 128, _B), ("m1", 128, _B),
    ("kd", 2048, _F),
]:
    _sb(_n, _c, _t)
for _n, _c in [("kn", 512), ("kj", 512), ("wq", 128), ("e0", 128), ("e1", 128), ("e2", 128), ("e3", 128), ("hq0", 128), ("fin", 128), ("la", N * A)]:
    _sb(_n + "c", _c, _Q)
    _sb(_n + "s", _c, _S)
for _t in range(R):
    for _n, _c in [("sd", 128), ("ld", 128), ("qn", 128)]:
        if _n != "sd" or _t > 0:
            _sb("%s%dc" % (_n, _t), _c, _Q)
            _sb("%s%ds" % (_n, _t), _c, _S)
    _sb("hq%dc" % (_t + 1), HOME, _Q)
    _sb("hq%ds" % (_t + 1), HOME, _S)
    _sb("pk%d" % _t, 8, _I)
    _sb("vl%d" % _t, 12, _I)
    _sb("sn%d" % _t, 32, _F)
    _sb("nl%d" % (_t + 1), 80, _F)
    _sb("dq%d" % _t, 512, _F)
    _sb("hb%d" % _t, 512, _B)
_sb("hxc", A, _Q)
for _l in LEGS:
    _sb("h%ss" % _l, A if _l == "x" else HALF, _S)
SMALL, WIDE = {}, {"f": ["smf", 0], "i": ["smi", 0], "u": ["smu", 0]}


def _small(ty, name, cols):
    w = WIDE[ty]
    SMALL[name] = (w[0], w[1], w[1] + cols)
    w[1] += cols + cols % 2


for _t in range(R + 1):
    for _n, _c in [("u", 1), ("bc", 73), ("bt", 64), ("pkq", 64), ("ind", 64), ("cum", 64), ("pkr", 64), ("sp", 64),
                   ("q0", 8), ("n", 1), ("lm", 32), ("lsc", 32), ("vp", 8), ("pkf", 1), ("vf", 1), ("a1", 1),
                   ("c1", 1), ("i0", 64), ("oh", 64), ("oht", 64), ("q1", 1), ("dp", 1), ("p0", 128), ("p1", 128), ("p2", 128), ("p3", 128),
                   ("s4", 4), ("mx", 1), ("ne", 4), ("js", 4), ("d0", 64), ("dt", 64), ("ds", 64), ("lf", 32),
                   ("n1", 32), ("j0", 128), ("j1", 128), ("j2", 128)]:
        _small("f", "%s_%d" % (_n, _t), _c)
    for _n, _c in [("li", 32), ("be", 64), ("sr", 8), ("ui", 1), ("ni", 1), ("lr", 32), ("pki", 1), ("vi", 1), ("ai", 1)]:
        _small("i", "%s_%d" % (_n, _t), _c)
    for _n, _c in [("su", 8), ("lu", 2), ("ko", 32), ("l2u", 2)]:
        _small("u", "%s_%d" % (_n, _t), _c)
_sb("smf", WIDE["f"][1], _F)
_sb("smi", WIDE["i"][1], _I)
_sb("smu", WIDE["u"][1], _U)
for _b in range(4):
    SCRATCH["z%d" % _b] = ("psum", [128, 512], "float32")
    SCRATCH["d%d" % _b] = ("psum", [128, 512], "float32")

SEMAPHORES = ["qv", "qs", "qt", "qg", "ls"] + ["m%d" % _k for _k in range(40)] + ["h" + _l for _l in LEGS]
for _t in range(R):
    SEMAPHORES += ["apk%d" % _t, "aco%d" % _t, "adl%d" % _t, "are%d" % _t]


def helpers_of(core, T, topo):
    can = [c for c in topo.cores_of(core) if T.rank_of(c) is None and all(topo.may_write(c, r) for r in T.cores)]
    return sorted(can, key=lambda c: topo.die(c) == topo.die(core))[:HELPERS]


def lanes(n, width=8):
    calls = []
    while n:
        k = 1
        while 2 * k <= min(n, width):
            k *= 2
        w = width // k
        calls.append([tuple(range(w * i, w * i + w)) for i in range(k)])
        n -= k
    return calls


def parts(leg, s):
    out = {"c": [], "s": []}
    if leg == "x":
        to = [((s + 1 + b) % N, 0) for b in range(N - 1)]
        cut = XKEEP + (N - XKEEP) // 2
        out["c"] = [(None, to[:XKEEP], lanes(XKEEP)), (0, to[XKEEP:cut], lanes(cut - XKEEP)), (1, to[cut:], lanes(N - 1 - cut))]
        m = (N - 1) // 2
        out["s"] = [(0, to[:m], lanes(m)), (1, to[m:], lanes(N - 1 - m))]
        return out
    to = [((s + i) % N, (s + i) % N) for i in range(1, N)]
    out["c"].append((None, to, [[(i,) for i in range(6)] + [(6, 7)]]))
    by = [[e for e in to if e[1] * HELPERS // N == h] for h in range(HELPERS)]
    own = max(by, key=len)[-KEEP:]
    out["s"].append((None, own, [[(6, 7)]]))
    for h in range(HELPERS):
        l = [e for e in by[h] if e not in own]
        out["s"].append((h, l, lanes(len(l))))
    return out


def landing(leg, s, d):
    if leg == "x":
        return "la", A * s, A
    if leg[0] == "f":
        return "ld" + leg[1], CAP * s, CAP
    return "hq%d" % (int(leg[1]) + 1), A + CAP * ((s - d - 1) % N), CAP


def sem_of(leg):
    return "aco0" if leg == "x" else {"f": "aco", "b": "are"}[leg[0]] + leg[1]


def issue(g, core, T, topo, leg, s, what, src, first, entries, calls, total):
    todo = list(entries)
    for call in calls:
        tr = []
        for at in call:
            d, b = todo.pop(0)
            dst = T.cores[d]
            rid, pid, _ = topo.addr(dst)
            es = topo.engines(core, dst)
            name, lo, n = landing(leg, s, d)
            c = CAP * (b - first)
            o, i = T[name + what][:, lo:lo + n], T[src][:, c:c + n]
            if what == "c":
                o, i = o.bitcast(dt.uint8), i.bitcast(dt.uint8)
            tr.append(RemoteDMATransfer(dst_ids=[DstId(rid=rid, pnc=pid)], dma_engine_mask=sum(1 << es[k] for k in at), remote_sem=T.sem[sem_of(leg)], src=i, dst=o))
            total["ls"] = total.get("ls", 0) + len(at)
        g.remote_dma_fused(tr, local_sem=T.sem["ls"])


def helper_program(g, core, T, topo):
    rank = [c for c in topo.cores_of(core) if T.rank_of(c) is not None]
    if not rank or core not in helpers_of(rank[0], T, topo):
        return
    me, s, total = helpers_of(rank[0], T, topo).index(core), T.rank_of(rank[0]), {}
    for leg in LEGS:
        g.wait_ge(T.sem["h" + leg], HAND * (2 if leg == "x" else 1))
        for what, l in parts(leg, s).items():
            for h, entries, calls in l:
                if h == me:
                    issue(g, core, T, topo, leg, s, what, "h" + leg + what, 0 if leg == "x" else N // HELPERS * me, entries, calls, total)
    g.wait_ge(T.sem["ls"], total["ls"])


def rank_program(g, core, T, topo):
    me = T.rank_of(core)
    if me is None:
        helper_program(g, core, T, topo)
        return
    OP, X, CP = AluOpType, AxisListType.X, ActivationFunctionType.Copy
    V, S, TE, Y = g.vector, g.scalar, g.tensor, g.sync
    eng = {"v": V, "s": S, "t": TE, "g": g, "y": Y}
    known = {q: {} for q in eng}
    total, waited = {}, {}
    wr, rd = {}, {}
    nm = [0]

    def need(q, evs):
        for sem, n, clk in sorted(evs, key=lambda e: -sum(e[2].values())):
            k = known[q]
            if k.get(sem, 0) < n:
                eng[q].wait_ge(T.sem[sem], n)
                k[sem] = n
                waited[sem] = max(waited.get(sem, 0), n)
                for x in clk:
                    k[x] = max(k.get(x, 0), clk[x])

    def before(q, r, w):
        evs = []
        for k in r:
            evs += wr.get(k, [])
        for k in w:
            evs += wr.get(k, []) + rd.get(k, [])
        need(q, evs)

    def done(q, sem, n, r, w, a=()):
        ev = (sem, n, dict(known[q]))
        for k in r:
            rd.setdefault(k, []).append(ev)
        for k in w:
            wr[k] = [ev]
            rd[k] = []
        for k in a:
            wr.setdefault(k, []).append(ev)

    def run(q, fn, r=(), w=(), a=()):
        before(q, r, w)
        sem = "q" + q
        fn().then_inc(T.sem[sem], 1)
        total[sem] = total.get(sem, 0) + 1
        done(q, sem, total[sem], r, w, a)

    def dma(q, pairs, r=(), w=(), a=()):
        before(q, r, w)
        sem = "m%d" % nm[0]
        nm[0] += 1
        for o, i in pairs:
            eng[q].dma_start(o, i).then_inc(T.sem[sem], 16)
        total[sem] = 16 * len(pairs)
        done(q, sem, total[sem], r, w, a)

    others = [(me + i) % N for i in range(1, N)]
    helpers = helpers_of(core, T, topo)
    NUMBERS = [[(i,) for i in range(6)] + [(6, 7)]]
    per = lambda plan: sum(len(l) for c in plan for l in c)

    def send(sem, part, r, plan):
        before("g", r, ())
        todo = list(others)
        for call in plan:
            tr = []
            for at in call:
                d = todo.pop(0)
                dst = T.cores[d]
                rid, pid, _ = topo.addr(dst)
                es = topo.engines(core, dst)
                o, s = part(d)
                tr.append(RemoteDMATransfer(dst_ids=[DstId(rid=rid, pnc=pid)], dma_engine_mask=sum(1 << es[k] for k in at), remote_sem=T.sem[sem], src=s, dst=o))
                total["ls"] = total.get("ls", 0) + len(at)
            g.remote_dma_fused(tr, local_sem=T.sem["ls"])

    def hand(leg, what, src):
        before("g", (src + what,), ())
        free = [k for k in topo.engines(core, helpers[0]) if k not in topo.engines(core, T.cores[others[0]])]
        tr = []
        for h, c in enumerate(helpers):
            rid, pid, _ = topo.addr(c)
            n, lo = (A, 0) if leg == "x" else (HALF, HALF * h)
            o, i = T["h" + leg + what][:, 0:n], T[src + what][:, lo:lo + n]
            if what == "c":
                o, i = o.bitcast(dt.uint8), i.bitcast(dt.uint8)
            tr.append(RemoteDMATransfer(dst_ids=[DstId(rid=rid, pnc=pid)], dma_engine_mask=sum(1 << k for k in free[HAND * h:HAND * h + HAND]), remote_sem=T.sem["h" + leg], src=i, dst=o))
            total["ls"] = total.get("ls", 0) + HAND
        g.remote_dma_fused(tr, local_sem=T.sem["ls"])

    def direct(leg, what, src):
        before("g", (src + what,), ())
        for h, entries, calls in parts(leg, me)[what]:
            if h is None:
                issue(g, core, T, topo, leg, me, what, src + what, 0, entries, calls, total)

    def coming(leg):
        n = 0
        for s in others:
            for l in parts(leg, s).values():
                for h, entries, calls in l:
                    n += sum(len(at) for (d, b), at in zip(entries, [at for call in calls for at in call]) if d == me)
        return n

    def leave(leg, src):
        hand(leg, "s", src)
        direct(leg, "c", src)
        direct(leg, "s", src)

    def arrive(sem, n, keys):
        total[sem] = n
        for k in keys:
            wr.setdefault(k, []).append((sem, n, {}))

    def ap(name, p=None, c=None):
        if name in SMALL:
            buf, lo, hi = SMALL[name]
            c0, c1, st = (0, hi - lo, 1) if c is None else (c if len(c) == 3 else c + (1,))
            cols = slice(lo + c0, lo + c1, st)
        else:
            buf = name
            cols = slice(None) if c is None else (slice(*c))
        rows = slice(None) if p is None else slice(*p)
        return T[buf][rows, cols]

    def codes(name, lo, hi):
        return T[name + "c"][:, lo:hi].bitcast(dt.uint8)

    def words(name, lo, hi):
        return T[name + "c"][:, lo:hi].bitcast(dt.uint32)

    def plane(name, lo, hi):
        return T[name + "s"][:, lo:hi]

    def ts(o, i, s1, op0, s2=None, op1=None, r=(), po=None, pi=None, co=None, ci=None, a=()):
        def fn():
            out, in0 = ap(o, po, co), ap(i, pi if pi else po, ci)
            if op1 is None:
                return V.tensor_scalar(out, in0, s1, None, op0)
            return V.tensor_scalar(out, in0, s1, s2, op0, op1)
        run("v", fn, r=tuple(r) + (i,), w=() if a else (o,), a=a)

    def tt(o, x, y, op, po=None, co=None, cx=None, cy=None, a=()):
        run("v", lambda: V.tensor_tensor(ap(o, po, co), ap(x, po, cx), ap(y, po, cy), op), r=(x, y), w=() if a else (o,), a=a)

    def cp(o, i, po=None, pi=None, co=None, ci=None, a=()):
        run("v", lambda: V.tensor_copy(ap(o, po, co), ap(i, pi if pi else po, ci)), r=(i,), w=() if a else (o,), a=a)

    def scan(o, d0, d1, c0=None, c1=None, po=None):
        run("v", lambda: V.tensor_tensor_scan(ap(o, po), ap(d0, po, c0), ap(d1, po, c1), 0.0, OP.mult, OP.add), r=(d0, d1), w=(o,))

    def total_of(o, i, po=None, ci=None):
        run("v", lambda: V.tensor_reduce(ap(o, po), ap(i, po, ci), X, OP.add), r=(i,), w=(o,))

    def trans(o, i, po=None, ci=None):
        run("v", lambda: V.transpose(ap(o, po), ap(i, po, ci)), r=(i,), w=(o,))

    def fill(o, c, value, a=()):
        run("v", lambda: V.memset(ap(o, None, c), float(value)), w=() if a else (o,), a=a)

    def pick(o, olo, ohi, i, ilo, ihi, lst):
        off = ap(lst)
        run("v", lambda: V.tensor_copy(words(o, olo, ohi), words(i, ilo, ihi).indirect(off)), r=(i + "c", lst), a=(o + "c",))
        run("s", lambda: S.activation(plane(o, olo, ohi), plane(i, ilo, ihi).indirect(off), CP), r=(i + "s", lst), a=(o + "s",))

    def quant(o, hi, src, slo, shi):
        run("v", lambda: V.quantize_mx(T[o + "c"][:, 0:hi], T[o + "s"][:, 0:hi], T[src][:, slo:shi]), r=(src,), a=(o + "c", o + "s"))

    def mm(o, x, y, ylo, yhi):
        run("t", lambda: TE.matmul_mx(T[o][:, 0:yhi - ylo], T[x + "c"][:, 0:128], T[x + "s"][:, 0:128], T[y + "c"][:, ylo:yhi], T[y + "s"][:, ylo:yhi], True, True),
            r=(x + "c", x + "s", y + "c", y + "s"), w=(o,))

    def both(o, olo, ohi, i, ilo, ihi):
        dma("y", [(codes(o, olo, ohi), codes(i, ilo, ihi)), (plane(o, olo, ohi), plane(i, ilo, ihi))], r=(i + "c", i + "s"), a=(o + "c", o + "s"))

    def iota(name, pattern, base, cm):
        if SCRATCH[name][2] == "int32":
            run("g", lambda: g.iota(T[name][:], pattern, base, cm), w=(name,))
        else:
            run("g", lambda: g.iota(T[name][:], pattern, base, cm, allow_small_or_imprecise_dtypes=True), w=(name,))

    quad = [(32 * b, 32 * b + 32) for b in range(4)]
    mine = quad[me // 2]
    half = me % 2
    later = []

    def gap():
        if later:
            later.pop(0)()

    dma("y", [(T.stt[0:16, 1:3], T.st[:, :]), (T.stt[16:32, 0:2], T.st[:, :])], w=("stt",))
    dma("s", [(T.xb[:, 0:4 * A], T.x[:, :])], a=("xb",))
    dma("y", [(T.nxa[0:16, :], T.nx[:, :]), (T.nxa[16:32, :], T.nx[:, :])], w=("nxa",))
    dma("y", [(T.kb[:], T.ky[:, :])], w=("kb",))
    dma("y", [(T.wb[:], T.w[:, :])], w=("wb",))

    run("v", lambda: V.memset(T.xb[:, 4 * A:512], 0.0), a=("xb",))
    iota("ip", [[1, 1]], 0, 1)
    iota("ja", [[0, 2], [-1, A]], A, 0)
    iota("iw", [[1, 128]], 0, 0)
    iota("i8", [[-16, 8]], 256 - 16 * me, 1)
    iota("ik", [[1, 4], [64, 8]], 0, 0)
    iota("ia", [[1, 8], [0, 4]], 256, -1)
    iota("ic", [[1, 32]], 256, -1)
    fill("ct", (0, 32), 0)
    fill("ct", (32, 64), -RANK, a=("ct",))
    ts("ip31", "ip", 31, OP.bitwise_and)
    ts("ip15", "ip", 15, OP.bitwise_and)
    ts("ip5", "ip", 5, OP.logical_shift_right)
    cp("af", "ip31")
    ts("k0", "ip15", float(-GATE), OP.mult)
    ts("tb", "ip5", 2.0, OP.mult)
    ts("rowx", "ja", float(TURN), OP.mult, float(A * me), OP.add)
    fill("one", None, 1)
    quant("hq0", 128, "xb", 0, 512)

    later.append(lambda: fill("eF", None, 0))
    later.append(lambda: cp("ipf", "ip"))
    later.append(lambda: ts("ip3", "ip", 3, OP.bitwise_and))
    later.append(lambda: run("v", lambda: V.tensor_scalar(T.eF[:, 3:515:4], T.iw[:], T.ipf[:, 0:1], 0.5, OP.is_equal, OP.mult), r=("iw", "ipf"), w=("eF",)))
    tiles = len(later)
    later.append(lambda: ts("t4", "ip3", 1.0, OP.mult))
    later.append(lambda: ts("ia2", "ia", 3, OP.bitwise_and))
    later.append(lambda: ts("ic2", "ic", 15, OP.bitwise_and))
    later.append(lambda: ts("nxf", "nxa", 256.0, OP.mult, po=(0, 32)))
    later.append(lambda: ts("mask", "ia2", 0.0, OP.is_equal, co=(0, 32), a=("mask",)))
    later.append(lambda: trans("nxt", "nxf", (0, 32)))
    later.append(lambda: ts("mask", "ic2", 0.0, OP.is_equal, co=(32, 64), a=("mask",)))
    later.append(lambda: ts("r4", "ip15", 4.0, OP.mult))
    later.append(lambda: ts("i82", "i8", 112, OP.bitwise_and))
    later.append(lambda: ts("ku", "ik", T.r4[:, 0:1], OP.add, r=("r4",)))
    later.append(lambda: ts("mask8", "i82", 0.0, OP.is_equal))
    later.append(lambda: ts("cl1", "i82", -1.0, OP.mult, float(A + (N - 1) * CAP - RANK * me - A - 1), OP.add, ci=(0, 1)))
    later.append(lambda: ts("r1", "ip15", 1.0, OP.add))
    later.append(lambda: tt("cloc", "cl1", "r1", OP.add))
    tiles = len(later) - tiles

    def table():
        dma("y", [(T.nrow[0:1, :], T.nxt[0:32, 0:16])], r=("nxt",), w=("nrow",))
        run("g", lambda: g.partition_broadcast(T.tab[:], T.nrow[0:1, :], 128), r=("nrow",), w=("tab",))

    def unpack(b):
        quant("e%d" % b, 128, "eF", 3 - b, 3 - b + 512)

    def unpack_keys(parts):
        for b in parts:
            mm("d%d" % b, "e%d" % b, "kn", 0, 512)
            run("s", lambda: S.activation(T.kd[:, b:2048:4], T["d%d" % b][:, 0:512], CP), r=("d%d" % b,), a=("kd",))

    def steps(t):
        nl = "nl%d" % t
        for c, v in [((STEP, STEP + 64), 0), ((STEP + 32, STEP + 33), -RANK)]:
            run("v", lambda: V.memset(ap(nl, None, c), float(v)), r=(nl + "k",), a=(nl + "k",))

    def rows(t, q):
        n = "_%d" % t
        if t == 0:
            ts("bc" + n, "ct", ap("u" + n, q), OP.add, r=("u" + n,), po=q, co=(9, 73))
        else:
            nl = "nl%d" % t
            run("v", lambda: V.tensor_tensor_scan(ap("bc" + n, q), ap("one", q), ap(nl, q, (5, STEP + 64)), 0.0, OP.mult, OP.add), r=("one", nl, nl + "k"), w=("bc" + n,))
        gap()
        trans("bt" + n, "bc" + n, q, ci=(9, 73))
        gap()

    def route(t, q):
        n = "_%d" % t
        rows(t, q)
        for b in quad:
            ts("be" + n, "bt" + n, 1.0 / RANK, OP.mult, FLOOR, OP.add, po=b, pi=q, a=("be" + n,))
        tt("pkq" + n, "bt" + n, "rowb" if t else "rowx", OP.add, po=q)
        gap()
        ts("ind" + n, "be" + n, T.tb[:, 0:1], OP.is_equal, float(GATE), OP.mult, r=("tb",))
        for b in quad:
            cp("pkr" + n, "pkq" + n, po=b, pi=q, a=("pkr" + n,))
        two = [(0, A), (A, 2 * A)]
        for c in two:
            run("v", lambda: V.tensor_tensor_scan(ap("cum" + n, None, c), ap("one", None, (0, A)), ap("ind" + n, None, c), T.k0[:, 0:1], OP.mult, OP.add),
                r=("one", "ind" + n, "k0"), a=("cum" + n,))
        gap()
        for c in two:
            run("v", lambda: V.tensor_tensor_scan(ap("sp" + n, None, c), ap("pkr" + n, None, c), ap("cum" + n, None, c), 0.0, OP.max, OP.min),
                r=("pkr" + n, "cum" + n), a=("sp" + n,))
        gap()
        for b in range(4):
            ts("q0" + n, "sp" + n, 0.0, OP.max, po=(0, 32), pi=quad[b], co=(2 * b, 2 * b + 2), ci=(31, 64, 32), a=("q0" + n,))
        gap()
        for b in quad:
            cp("pk%d" % t, "q0" + n, po=b, pi=(0, 32), a=("pk%d" % t,))
        vl, pk = T["vl%d" % t], T["pk%d" % t]
        send("apk%d" % t, lambda d: (vl[:, 3 + (me - d) % N:4 + (me - d) % N], pk[:, d:d + 1]), ("pk%d" % t,), NUMBERS)
        if t > 0:
            ts("sr" + n, "pk%d" % t, 255, OP.bitwise_and)
            cp("su" + n, "sr" + n)

    def expect(t, land):
        cp("vl%d" % t, "pk%d" % t, co=(3, 4), ci=(me, me + 1), a=("vl%d" % t,))
        arrive("apk%d" % t, per(NUMBERS), ("vl%d" % t,))
        arrive("aco%d" % t, coming("f%d" % t if t else "x"), (land + "c", land + "s"))

    def depart(t):
        ld, sd = "ld%d" % t, "sd%d" % t
        pick(sd, 0, 128, "hq%d" % t, 0, HOME, "su_%d" % t)
        leave("f%d" % t, sd)
        both(ld, CAP * me, CAP * me + CAP, sd, CAP * me, CAP * me + CAP)
        expect(t, ld)

    def stand(t):
        n, q = "_%d" % t, mine
        cp("ui" + n, "bc" + n, po=q, ci=(8, 9))
        ts("ni" + n, "ui" + n, 8, OP.logical_shift_right, po=q)
        cp("n" + n, "ni" + n, po=q)
        if t < R:
            ts("nl%d" % (t + 1), "ni" + n, 256.0, OP.mult, T.af[q[0]:q[1], 0:1], OP.add, r=("af",), po=q, co=(KEPT, KEPT + 1), a=("nl%d" % (t + 1),))
        dma("y", [(T.nd[t:t + 1, 0:A], ap("n" + n, q))], r=("n" + n,))

    def places(t):
        n = "_%d" % t
        for b in quad:
            cp("li" + n, "bt" + n, po=b, pi=mine, ci=(0, A), a=("li" + n,))
        ts("lr" + n, "li" + n, 255, OP.bitwise_and)
        tt("lm" + n, "lr" + n, "mask", OP.mult, cy=(32, 64))
        scan("lsc" + n, "rst", "lm" + n, c0=(32, 64))
        cp("lu" + n, "lsc" + n, ci=(15, 32, 16))

    def slots(t):
        n = "_%d" % t
        if t == 0:
            ts("sr_0", "vl0", 255, OP.bitwise_and, ci=(3, 11))
        tt("vp" + n, "vl%d" % t, "mask8", OP.mult, cx=(3, 11))
        if t == 0:
            cp("su_0", "sr_0", co=(me, N), ci=(0, N - me), a=("su_0",))
        total_of("pkf" + n, "vp" + n)
        if t == 0 and me:
            cp("su_0", "sr_0", co=(0, me), ci=(N - me, N), a=("su_0",))
        cp("pki" + n, "pkf" + n)
        if t == 0:
            pick("ld0", 0, 128, "la", 0, N * A, "su_0")
        ts("vi" + n, "pki" + n, 32512, OP.bitwise_and)
        ts("ai" + n, "pki" + n, 18, OP.logical_shift_right)
        ts("vf" + n, "vi" + n, 1.0 / 256, OP.mult)
        cp("a1" + n, "ai" + n)
        ts("m%d" % (t % 2), "iw", ap("vf" + n), OP.is_equal, r=("vf" + n,))
        later.append(lambda: ts("c1" + n, "vf" + n, 4.0, OP.mult, 1024.0, OP.add))
        later.append(lambda: tt("q1" + n, "cloc", "a1" + n, OP.add))
        later.append(lambda: ts("i0" + n, "mask", ap("c1" + n), OP.mult, -1024.0, OP.add, r=("c1" + n,)))
        later.append(lambda: tt("dp" + n, "q1" + n, "vi" + n, OP.subtract))
        later.append(lambda: ts("oh" + n, "ja", ap("a1" + n), OP.is_equal, r=("a1" + n,), co=(0, 32), ci=(0, 32), a=("oh" + n,)))
        later.append(lambda: ts("oh" + n, "ja", ap("a1" + n), OP.is_equal, ap("dp" + n), OP.mult, r=("a1" + n, "dp" + n), co=(32, 64), ci=(0, 32), a=("oh" + n,)))
        later.append(lambda: trans("oht" + n, "oh" + n))
        while t and later:
            gap()

    def hop(t):
        n, ld, qn, sn, dq, hb = "_%d" % t, "ld%d" % t, "qn%d" % t, "sn%d" % t, "dq%d" % t, "hb%d" % t
        nl, h = "nl%d" % (t + 1), "hq%d" % (t + 1)
        for j in range(4):
            mm("z%d" % j, ld, "kj", 128 * j, 128 * j + 128)
        for j in range(4):
            tt("p%d" % j + n, "z%d" % j, "m%d" % (t % 2), OP.mult, cx=(0, 128))
            if j < 3:
                run("s", lambda: S.activation(ap("j%d" % j + n), ap("p%d" % j + n), CP, accum_out=ap("s4" + n, None, (3 - j, 4 - j))), r=("p%d" % j + n,), w=("j%d" % j + n,), a=("s4" + n,))
        if t == 0:
            unpack_keys(REST)
        for b in range(4):
            mm("d%d" % b, "e%d" % b, ld, 0, 128)
        for b in range(4):
            run("s", lambda: S.activation(T[dq][:, b:512:4], T["d%d" % b][:, 0:128], CP), r=("d%d" % b,), a=(dq,))
        run("v", lambda: V.tensor_reduce(ap("s4" + n, None, (0, 1)), ap("p3" + n), X, OP.add), r=("p3" + n,), a=("s4" + n,))
        gap()
        run("v", lambda: V.tensor_reduce(ap("mx" + n), ap("s4" + n), X, OP.max), r=("s4" + n,), w=("mx" + n,))
        gap()
        ts("ne" + n, "s4" + n, ap("mx" + n), OP.not_equal, 1000000.0, OP.mult, r=("mx" + n,))
        gap()
        run("v", lambda: V.tensor_tensor_scan(ap("js" + n), T.c1s[:], ap("ne" + n), 0.0, OP.add, OP.min), r=("c1s", "ne" + n), w=("js" + n,))
        gap()
        ts("d0" + n, "i0" + n, ap("js" + n, None, (3, 4)), OP.add, 0.0, OP.max, r=("js" + n,))
        gap()
        trans("dt" + n, "d0" + n)
        gap()
        scan("ds" + n, "rst", "dt" + n)
        gap()

        def join(b):
            cp("lf" + n, "ds" + n, po=(0, 32), pi=quad[b], co=(8 * b, 8 * b + 8), ci=(3, 32, 4), a=("lf" + n,))
        cp("l2u" + n, "ds" + n, ci=(47, 64, 16))
        join(0)
        run("v", lambda: V.tensor_tensor(ap("n1" + n), T.tab[:, 0:512].indirect(ap("l2u" + n)), ap("oht" + n, None, (0, 32)), OP.mult), r=("tab", "l2u" + n, "oht" + n), w=("n1" + n,))
        join(1)
        for i in range(2):
            lo, hi = CAP * i, CAP * i + CAP
            run("v", lambda: V.tensor_tensor_scan(T[sn][:, lo:hi], ap("oht" + n, None, (32 + lo, 32 + hi)), ap("n1" + n, None, (lo, hi)), 0.0, OP.add, OP.add), r=("n1" + n, "oht" + n), a=(sn,))
        beta = lambda s: (me - s - 1) % N
        send("adl%d" % t, lambda s: (T[nl][:, 5 + beta(s):6 + beta(s)], T[sn][:, 15 + 16 * (s % 2):16 + 16 * (s % 2)]), (sn,), NUMBERS)
        arrive("adl%d" % t, per(NUMBERS), (nl,))
        join(2)
        join(3)
        for b in quad:
            ts("ko" + n, "lf" + n, 4.0, OP.mult, T.t4[0:32, 0:1], OP.add, r=("t4",), po=b, pi=(0, 32), a=("ko" + n,))
        run("v", lambda: V.tensor_tensor(T[hb][:], T.kd[:, 0:2048].indirect(ap("ko" + n)), T[dq][:], OP.add), r=("kd", "ko" + n, dq), w=(hb,))
        quant(qn, 128, hb, 0, 512)
        leave("b%d" % t, qn)
        both(h, A + 112, HOME, qn, CAP * me, CAP * me + CAP)
        arrive("are%d" % t, coming("b%d" % t), (h + "c", h + "s"))
        cp(nl, sn, po=mine, co=(OWN, OWN + 1), ci=(15 + 16 * half, 16 + 16 * half), a=(nl,))

    q = quad[0]
    hand("x", "c", "hq0")
    hand("x", "s", "hq0")
    direct("x", "c", "hq0")
    ts("u_0", "stt", 256.0, OP.mult, T.af[q[0]:q[1], 0:1], OP.add, r=("af",), po=q, ci=(1, 2))
    route(0, q)
    both("la", A * me, A * me + A, "hq0", 0, A)
    expect(0, "la")
    while len(later) > tiles:
        gap()
    unpack(0)
    quant("kn", 512, "kb", 0, 2048)
    unpack_keys((0,))
    while later:
        gap()
    pick("kj", 0, 512, "kn", 0, 512, "ku")
    table()
    for b in range(1, 4):
        unpack(b)
    unpack_keys(FIRST)
    fill("c1s", None, 1)
    fill("rst", None, 1)
    fill("rst", (0, 32, 4), 0)
    fill("rst", (32, 64, 16), 0)
    steps(1)
    ts("rowb", "ja", float(TURN), OP.mult)
    slots(0)
    hop(0)
    cp("nl1", "u_0", po=mine, pi=q, co=(KEPT, KEPT + 1), a=("nl1",))
    both("fin", A, 128, "hq0", A, 128)
    both("hq1", 0, A, "hq0", 0, A)
    for t in range(1, R + 1):
        if t < R:
            route(t, mine)
            depart(t)
            stand(t)
            places(t)
            pick("hq%d" % (t + 1), 0, A, "hq%d" % t, 0, HOME, "lu_%d" % t)
            steps(t + 1)
            if t == 1:
                cp("n_0", "stt", po=q, ci=(1, 2))
                dma("y", [(T.nd[0:1, 0:A], ap("n_0", q))], r=("n_0",))
                quant("wq", 128, "wb", 0, 512)
            slots(t)
            hop(t)
        else:
            rows(t, mine)
            places(t)
            stand(t)
            pick("fin", 0, A, "hq%d" % t, 0, HOME, "lu_%d" % t)
            mm("z0", "wq", "fin", 0, 128)
            dma("y", [(T.oc[:, 0:4 * A], codes("fin", 0, A))], r=("finc",))
            dma("s", [(T.osc[4 * k:4 * k + 4, 0:A], T.fins[32 * k:32 * k + 4, 0:A]) for k in range(4)], r=("fins",))
            run("v", lambda: V.tensor_copy(T.yb[:], T.z0[:, 0:A]), r=("z0",), w=("yb",))
            dma("y", [(T.y[:, :], T.yb[:])], r=("yb",))
    for sem in total:
        if waited.get(sem, 0) < total[sem]:
            g.wait_ge(T.sem[sem], total[sem])
